import numpy as np
import ml_dtypes


def mxq(x, axis, fmt="e4m3"):
    dtype, down = {"e4m3": (ml_dtypes.float8_e4m3fn, 7), "e5m2": (ml_dtypes.float8_e5m2, 14)}[fmt]
    v = np.moveaxis(np.asarray(x, np.float32).astype(ml_dtypes.bfloat16).astype(np.float64), axis, -1)
    blocks = v.reshape(v.shape[:-1] + (-1, 32))
    amax = np.abs(blocks).max(-1, keepdims=True)
    byte = np.maximum(np.where(amax > 0, np.frexp(amax)[1] - 1 + 127, 0) - down, 1)
    scale = np.exp2(byte - 127.0)
    codes = (blocks / scale).astype(np.float32).astype(dtype).astype(np.float64)
    return np.moveaxis((codes * scale).reshape(v.shape), -1, axis)


WIDE = False


def mx_kscale(k):
    if not WIDE:
        return np.ones(k)
    levels = np.array([10, -10, 5, -5, 0])
    if k % 512:
        return np.exp2(np.random.permutation(np.resize(levels, k // 32))).repeat(32)
    a = np.empty((k // 512, 16))
    for p in range(k // 512):
        a[p, :8] = np.random.permutation(np.resize(levels, 8))
        for g in range(8):
            far = levels[np.abs(levels - a[p, g]) >= 10]
            a[p, g + 8] = far[np.random.randint(len(far))]
    return np.exp2(a.ravel()).repeat(32)


def f64(x):
    return np.asarray(x).astype(np.float64)


def striped(idx):
    return np.tile(idx.reshape(-1, 16).T, (8, 1)).astype(np.uint16)


def unstriped(offs):
    return offs[:16].T.reshape(-1).astype(np.int64)


E2M1 = np.array([0.0, 0.5, 1.0, 1.5, 2.0, 3.0, 4.0, 6.0, -0.0, -0.5, -1.0, -1.5, -2.0, -3.0, -4.0, -6.0])


def pack_weight(w, fmt):
    k, n = w.shape
    w = f64(np.asarray(w, np.float32).astype(ml_dtypes.bfloat16)).reshape(k // 32, 32, n)
    amax = np.abs(w).max(1)
    if fmt == "e4m3":
        byte = np.frexp(amax)[1] - 1 + 127 - 7
    else:
        mant, ex = np.frexp(amax / 6.0)
        byte = np.where(mant > 0.5, ex, ex - 1) + 127
    byte = np.clip(np.where(amax > 0, byte, 1), 1, 254)
    scaled = (w * np.exp2(127.0 - byte)[:, None, :]).reshape(k, n).astype(np.float32)
    by_word = np.ascontiguousarray(scaled.reshape(k // 512, 128, 4, n).transpose(0, 1, 3, 2))
    if fmt == "e4m3":
        words = by_word.astype(ml_dtypes.float8_e4m3fn).view(np.uint8)
    else:
        c = by_word.astype(ml_dtypes.float4_e2m1fn).view(np.uint8) & 0xF
        words = (c[..., 0::2] | (c[..., 1::2] << 4)).reshape(k // 512, 128, 2 * n)
    return np.ascontiguousarray(words), np.ascontiguousarray(byte.astype(np.uint8).reshape(k // 512, 16, n))


def unpack_weight(words, scales, fmt):
    g, _, n = scales.shape
    words = np.ascontiguousarray(words).reshape(g, 128, n, -1)
    if fmt == "e4m3":
        vals = words.view(ml_dtypes.float8_e4m3fn).astype(np.float64)
    else:
        nib = np.empty((g, 128, n, 4), np.uint8)
        nib[..., 0::2] = words & 0xF
        nib[..., 1::2] = words >> 4
        vals = E2M1[nib]
    vals = vals * np.repeat(np.exp2(scales.astype(np.float64) - 127.0), 8, axis=1)[..., None]
    return vals.transpose(0, 1, 3, 2).reshape(g * 512, n)


def gelu(v):
    return 0.5 * v * (1.0 + np.tanh(np.sqrt(2.0 / np.pi) * (v + 0.044715 * v**3)))


def striped8(idx):
    return np.concatenate([v.reshape(-1, 16).T for v in idx]).astype(np.uint16)


def unstriped8(offs):
    return np.stack([offs[16 * g:16 * g + 16].T.reshape(-1) for g in range(8)]).astype(np.int64)


def heads(xT, wgt, idx8):
    k = np.arange(xT.shape[0])
    return wgt[k // 4 % 128] * xT[k[:, None], idx8[k % 512 // 64]]


K, M, T, S, H, N = 1024, 1024, 2048, 1024, 512, 512

def setup_inputs():
    n = np.random.standard_normal
    sx = mx_kscale(K)[:, None]
    sv = mx_kscale(M)[:, None]
    u = mx_kscale(H)[:, None]
    tab_words, tab_scales = pack_weight(n((M, T)) * sv, "e4m3")
    wk_words, wk_scales = pack_weight(0.6 * n((M, H)) / np.sqrt(M) / sv, "e2m1")
    wo_words, wo_scales = pack_weight(n((H, N)) / np.sqrt(H) / u, "e4m3")
    return {
        "xT": (n((K, T)) * sx).astype(np.float32),
        "wgt": np.repeat(np.random.uniform(0.5, 2.0, (8, S)), 16, axis=0).astype(np.float32),
        "offs2": striped8(np.stack([np.random.permutation(T)[:S] for _ in range(8)])),
        "tab_words": tab_words, "tab_scales": tab_scales,
        "offs": striped(np.random.permutation(T)[:S]),
        "wq": (0.4 * n((K, H)) / np.sqrt(K) / sx).astype(np.float32),
        "wk_words": wk_words, "wk_scales": wk_scales,
        "wv": (n((M, H)) / np.sqrt(M) / sv * u.T).astype(np.float32),
        "wo_words": wo_words, "wo_scales": wo_scales,
        "bo": (0.5 * n(N)).astype(np.float32),
    }

def reference(xT, wgt, offs2, tab_words, tab_scales, offs, wq, wk_words, wk_scales, wv, wo_words, wo_scales, bo):
    xg = heads(f64(xT), f64(wgt), unstriped8(offs2))
    v = unpack_weight(tab_words, tab_scales, "e4m3")[:, unstriped(offs)]
    wk = unpack_weight(wk_words, wk_scales, "e2m1")
    wo = unpack_weight(wo_words, wo_scales, "e4m3")
    q = mxq(f64(wq), 0, "e4m3").T @ mxq(xg, 0, "e4m3")
    key = wk.T @ v
    val = mxq(f64(wv), 0, "e4m3").T @ v
    h = np.exp(q * key) * val
    return (wo.T @ mxq(h, 0, "e4m3")) + f64(bo)[:, None]

@@ -1,0 +1,254 @@
+from contextlib import ExitStack
+
+import concourse.mybir as mybir
+
+K, M, T, S, H, N = 1024, 1024, 2048, 1024, 512, 512
+FLOPS = 2 * S * (K * H + 2 * M * H + H * N)
+
+F32 = mybir.dt.float32
+BF16 = mybir.dt.bfloat16
+I32 = mybir.dt.int32
+U32 = mybir.dt.uint32
+U16 = mybir.dt.uint16
+U8 = mybir.dt.uint8
+FP8X4 = mybir.dt.float8_e4m3fn_x4
+FP4X4 = mybir.dt.float4_e2m1fn_x4
+MULT = mybir.AluOpType.mult
+ADD = mybir.AluOpType.add
+EXP = mybir.ActivationFunctionType.Exp
+IDENTITY = mybir.ActivationFunctionType.Identity
+
+P = 128
+PACK = 4
+PASSES = 2
+CH = 128
+PAIR = 256
+LANES = 16
+
+
+def tile_list_picked_exp_scores_kernel(
+    tc, xT, wgt, offs2, tab_words, tab_scales, offs, wq, wk_words, wk_scales, wv, wo_words, wo_scales, bo, out
+):
+    nc = tc.nc
+    with ExitStack() as ctx:
+        keep = ctx.enter_context(tc.tile_pool(name="keep", bufs=1))
+        stream = ctx.enter_context(tc.tile_pool(name="stream", bufs=1))
+        ring = ctx.enter_context(tc.tile_pool(name="ring", bufs=3))
+        psum = ctx.enter_context(tc.psum_pool(name="psum", bufs=1))
+
+        def load_scale_rows(plane, rows, packed):
+            for quad in range(4):
+                src = rows[:, 4 * quad : 4 * quad + 4, :]
+                if packed:
+                    dst = plane[32 * quad : 32 * quad + 4 * rows.shape[0], :]
+                else:
+                    dst = plane[32 * quad : 32 * quad + 4, :, :]
+                    src = src.rearrange("a r n -> r a n")
+                nc.gpsimd.dma_start(out=dst.bitcast(I32), in_=src.bitcast(I32))
+
+        warm = keep.tile([P, 2], F32, name="warm")
+        nc.vector.memset(warm[:, 0:1], 0.0)
+        nc.scalar.activation(warm[:, 1:2], warm[:, 0:1], EXP)
+
+        tab_sc = keep.tile([P, T], U8, name="tab_sc", align_bytes=64)
+        wk_sc_raw = keep.tile([P, PASSES, H], U8, name="wk_sc_raw", align_bytes=64)
+        wo_sc = keep.tile([P, 1, N], U8, name="wo_sc", align_bytes=64)
+        v_sc1 = keep.tile([P, S], U8, name="v_sc1", align_bytes=64)
+        nc.gpsimd.memset(tab_sc[:].bitcast(I32), 0)
+        load_scale_rows(tab_sc, tab_scales, True)
+        nc.gpsimd.memset(wk_sc_raw[:].bitcast(I32), 0)
+        load_scale_rows(wk_sc_raw, wk_scales, False)
+        nc.gpsimd.memset(v_sc1[:].bitcast(I32), 0)
+        nc.gpsimd.memset(wo_sc[:].bitcast(I32), 0)
+
+        tab_list = keep.tile([P, S // LANES], U16, name="tab_list")
+        nc.sync.dma_start(tab_list[:], offs)
+        wk_raw = keep.tile([P, PASSES, 2 * H], U8, name="wk_raw", align_bytes=64)
+        nc.sync.dma_start(out=wk_raw[:].bitcast(I32), in_=wk_words.rearrange("a p n -> p a n").bitcast(I32))
+        tab = []
+        for a in range(PASSES):
+            words = stream.tile([P, T], I32, name="slot%d" % a, align_bytes=64)
+            nc.sync.dma_start(out=words[:], in_=tab_words[a].rearrange("p t i -> p (t i)").bitcast(I32))
+            tab.append(words)
+        head_lists = keep.tile([P, S // LANES], U16, name="head_lists")
+        nc.sync.dma_start(head_lists[:], offs2)
+        weights = keep.tile([P, S], F32, name="weights")
+        nc.sync.dma_start(out=weights[:], in_=wgt)
+
+        x_rows = xT.rearrange("(a p i) t -> a i p t", a=PASSES, i=PACK)
+
+        def load_plane(a, i):
+            plane = stream.tile([P, T], F32, name="slot%d" % [2, 3, 4, 5, 7, 0, 2, 3][4 * a + i], align_bytes=64)
+            nc.sync.dma_start(out=plane[:], in_=x_rows[a, i])
+            return plane
+
+        def load_weight(w, a, slot):
+            raw = stream.tile([P, PACK, H], F32, name="slot%d" % slot, align_bytes=64)
+            nc.sync.dma_start(out=raw[:], in_=w.rearrange("(a p j) r -> a p j r", a=PASSES, j=PACK)[a])
+            return raw
+
+        wk_codes = keep.tile([P, PASSES, PACK, 2 * P], U8, name="wk_codes", align_bytes=64)
+        nc.vector.tensor_copy(
+            out=wk_codes[:].bitcast(U16),
+            in_=wk_raw[:].bitcast(U16).rearrange("p a (m t) -> p a t m", t=PACK),
+        )
+        wk_sc = keep.tile([P, PASSES, PACK, P], U8, name="wk_sc", align_bytes=64)
+        nc.vector.tensor_copy(out=wk_sc[:], in_=wk_sc_raw[:].rearrange("p a (m t) -> p a t m", t=PACK))
+
+        v_codes = []
+        for a in range(PASSES):
+            picked = keep.tile([P, S], U32, name="v_codes%d" % a, align_bytes=64)
+            nc.vector.tensor_copy(picked[:], tab[a][:].bitcast(U32).indirect(tab_list[:]))
+            v_codes.append(picked)
+        v_sc0 = keep.tile([P, S], U8, name="v_sc0", align_bytes=64)
+        nc.vector.tensor_copy(v_sc0[:], tab_sc[:].indirect(tab_list[:]))
+        nc.gpsimd.dma_start(out=v_sc1[0 : P - 4, :].bitcast(I32), in_=v_sc0[4:P, :].bitcast(I32))
+        v_sc = [v_sc0, v_sc1]
+        load_scale_rows(wo_sc, wo_scales, False)
+
+        def project(tag, bufs, c, w_codes, w_sc, w_dtype, a_codes, a_sc):
+            bank = psum.tile([P, PACK, CH], F32, name=tag, bufs=bufs)
+            cols = slice(c * CH, (c + 1) * CH)
+            for t in range(PACK):
+                for a in range(PASSES):
+                    nc.tensor.matmul_mx(
+                        out=bank[:, t, :],
+                        lhsT=w_codes(a, t).bitcast(w_dtype),
+                        lhsT_scale=w_sc(a, t),
+                        rhs=a_codes[a][:, cols].bitcast(FP8X4),
+                        rhs_scale=a_sc[a][:, cols],
+                        start=(a == 0),
+                        stop=(a == PASSES - 1),
+                    )
+            return bank[:].rearrange("p t n -> p n t")
+
+        keys = []
+        for c in range(S // CH):
+            bank = project(*[("kv", 3), ("q", 3), ("o", 2)][c % 3], c, lambda a, t: wk_codes[:, a, t, :], lambda a, t: wk_sc[:, a, t, :], FP4X4, v_codes, v_sc)
+            if c % 2 == 0:
+                keys.append(keep.tile([P, PAIR, PACK], F32, name="key%d" % c))
+            nc.scalar.copy(out=keys[c // 2][:, (c % 2) * CH : (c % 2 + 1) * CH, :], in_=bank)
+
+        def gather(dst, plane, lo, hi):
+            nc.vector.tensor_tensor(
+                dst[:, lo:hi], plane[:].indirect(head_lists[:, lo // LANES : hi // LANES]), weights[:, lo:hi], MULT
+            )
+
+        def weave(picked, woven, lo, hi):
+            nc.scalar.copy(
+                out=woven[:, lo:hi, :].rearrange("p (c n) i -> p c i n", n=4),
+                in_=picked[:, :, lo:hi].rearrange("p i (c n) -> p c i n", n=4),
+            )
+
+        def cast_weight_scalar(raw, name):
+            dealt = keep.tile([P, PACK, P, PACK], BF16, name=name, align_bytes=64)
+            nc.scalar.copy(
+                out=dealt[:].rearrange("p t m j -> p m j t"), in_=raw[:].rearrange("p j (m t) -> p m j t", t=PACK)
+            )
+            return dealt
+
+        def cast_weight_gpsimd(raw, name):
+            dealt = keep.tile([P, PACK, P, PACK], BF16, name=name, align_bytes=64)
+            src = raw[:].rearrange("p j (m t) -> p m t j", t=PACK)
+            dst = dealt[:].rearrange("p t m j -> p m t j")
+            for m0 in range(0, P, 32):
+                nc.gpsimd.tensor_scalar(dst[:, m0 : m0 + 32], src[:, m0 : m0 + 32], 1.0, 0.0, MULT, ADD)
+            return dealt
+
+        def quantize_weight(dealt, name, codes):
+            sc = keep.tile([P, H], U8, name=name + "_sc", align_bytes=64)
+            nc.vector.quantize_mx(
+                out=codes.bitcast(FP8X4), scales=sc[:], in_=dealt[:].rearrange("p t m j -> p (t m j)")
+            )
+            return codes, sc
+
+        picked = [keep.tile([P, PACK, S], F32, name="picked%d" % a) for a in range(PASSES)]
+        woven = [keep.tile([P, S, PACK], BF16, name="woven%d" % a, align_bytes=64) for a in range(PASSES)]
+        x_codes = [None, keep.tile([P, S], U32, name="x_codes1", align_bytes=64)]
+        x_sc = [keep.tile([P, S], U8, name="x_sc%d" % a, align_bytes=64) for a in range(PASSES)]
+
+        def quantize_x(a, lo, hi):
+            nc.vector.quantize_mx(
+                out=x_codes[a][:, lo:hi].bitcast(FP8X4),
+                scales=x_sc[a][:, lo:hi],
+                in_=woven[a][:, lo:hi, :].rearrange("p n i -> p (n i)"),
+            )
+
+        for i in range(PACK):
+            gather(picked[0][:, i, :], load_plane(0, i), 0, S)
+        wq_raw = load_weight(wq, 0, 6)
+        for lo in range(0, S, 512):
+            weave(picked[0], woven[0], lo, lo + 512)
+        wq_dealt = [cast_weight_scalar(wq_raw, "wq0")]
+        for i in range(2):
+            gather(picked[1][:, i, :], load_plane(1, i), 0, S)
+        x_codes[0] = stream.tile([P, S], U32, name="slot0", align_bytes=64)
+        for lo in range(0, S, 512):
+            quantize_x(0, lo, lo + 512)
+        wq_dealt.append(cast_weight_scalar(load_weight(wq, 1, 1), "wq1"))
+        gather(picked[1][:, 2, :], load_plane(1, 2), 0, S)
+        wq_codes = stream.tile([P, PASSES, H], U32, name="slot2", align_bytes=64)
+        wq_mx = [quantize_weight(wq_dealt[a], "wq%d" % a, wq_codes[:, a, :]) for a in range(PASSES)]
+        last = load_plane(1, 3)
+        wv_raw = [load_weight(wv, a, 4 + a) for a in range(PASSES)]
+        wo_codes = keep.tile([P, N], I32, name="wo_codes", align_bytes=64)
+        nc.sync.dma_start(out=wo_codes[:], in_=wo_words[0].rearrange("p c i -> p (c i)").bitcast(I32))
+        bias = keep.tile([P, N // P], F32, name="bias")
+        with nc.allow_non_contiguous_dma(reason="one bias value a partition"):
+            nc.sync.dma_start(out=bias[:], in_=bo.rearrange("(u p) -> p u", p=P))
+
+        for lo in range(0, S, PAIR):
+            gather(picked[1][:, 3, :], last, lo, lo + PAIR)
+        scores = []
+        for g in range(S // PAIR):
+            weave(picked[1], woven[1], g * PAIR, (g + 1) * PAIR)
+            quantize_x(1, g * PAIR, (g + 1) * PAIR)
+            prod = ring.tile([P, PAIR, PACK], F32, name="prod")
+            for u in range(2):
+                c = 2 * g + u
+                bank = project(
+                    "q", 3, c,
+                    lambda a, t: wq_mx[a][0][:, t * P : (t + 1) * P],
+                    lambda a, t: wq_mx[a][1][:, t * P : (t + 1) * P],
+                    FP8X4, x_codes, x_sc,
+                )
+                nc.vector.tensor_tensor(prod[:, u * CH : (u + 1) * CH, :], bank, keys[g][:, u * CH : (u + 1) * CH, :], MULT)
+            nc.scalar.activation(keys[g][:], prod[:], EXP)
+            scores.append(keys[g])
+
+        wv_mx = [quantize_weight(cast_weight_gpsimd(wv_raw[a], "wv%d" % a), "wv%d" % a, x_codes[0][:, a * H : (a + 1) * H]) for a in range(PASSES)]
+
+        out_rows = out.rearrange("(u p) j -> p u j", p=P)
+        for g in range(S // PAIR):
+            h = ring.tile([P, PAIR, PACK], BF16, name="h", align_bytes=64)
+            for u in range(2):
+                bank = project(
+                    "kv", 3, 2 * g + u,
+                    lambda a, t: wv_mx[a][0][:, t * P : (t + 1) * P],
+                    lambda a, t: wv_mx[a][1][:, t * P : (t + 1) * P],
+                    FP8X4, v_codes, v_sc,
+                )
+                nc.vector.tensor_tensor(h[:, u * CH : (u + 1) * CH, :], bank, scores[g][:, u * CH : (u + 1) * CH, :], MULT)
+            h_codes = ring.tile([P, PAIR], U32, name="h_codes", align_bytes=64)
+            h_sc = ring.tile([P, PAIR], U8, name="h_sc", align_bytes=64)
+            nc.vector.quantize_mx(
+                out=h_codes[:].bitcast(FP8X4), scales=h_sc[:], in_=h[:].rearrange("p n t -> p (n t)")
+            )
+            result = ring.tile([P, N // P, PAIR], F32, name="result")
+            for half in range(2):
+                bank = psum.tile([P, 2, PAIR], F32, name="o", bufs=2)
+                for s in range(2):
+                    u = 2 * half + s
+                    nc.tensor.matmul_mx(
+                        out=bank[:, s, :],
+                        lhsT=wo_codes[:, u * P : (u + 1) * P].bitcast(FP8X4),
+                        lhsT_scale=wo_sc[:, 0, u * P : (u + 1) * P],
+                        rhs=h_codes[:].bitcast(FP8X4),
+                        rhs_scale=h_sc[:],
+                        start=True,
+                        stop=True,
+                    )
+                for s in range(2):
+                    u = 2 * half + s
+                    nc.scalar.activation(result[:, u, :], bank[:, s, :], IDENTITY, bias=bias[:, u : u + 1])
+            nc.sync.dma_start(out=out_rows[:, :, g * PAIR : (g + 1) * PAIR], in_=result[:])

@@ -32,9 +32,12 @@ def tile_list_picked_exp_scores_kernel(
     nc = tc.nc
     with ExitStack() as ctx:
         keep = ctx.enter_context(tc.tile_pool(name="keep", bufs=1))
-        stream = ctx.enter_context(tc.tile_pool(name="stream", bufs=1))
+        shared = ctx.enter_context(tc.tile_pool(name="shared", bufs=1))
         ring = ctx.enter_context(tc.tile_pool(name="ring", bufs=3))
         psum = ctx.enter_context(tc.psum_pool(name="psum", bufs=1))
+
+        def slot(tag, shape, dtype):
+            return shared.tile(shape, dtype, name=tag, align_bytes=64)
 
         def load_scale_rows(plane, rows, packed):
             for quad in range(4):
@@ -44,90 +47,98 @@ def tile_list_picked_exp_scores_kernel(
                 else:
                     dst = plane[32 * quad : 32 * quad + 4, :, :]
                     src = src.rearrange("a r n -> r a n")
-                nc.gpsimd.dma_start(out=dst.bitcast(I32), in_=src.bitcast(I32))
+                nc.sync.dma_start(out=dst.bitcast(I32), in_=src.bitcast(I32))
 
         warm = keep.tile([P, 2], F32, name="warm")
         nc.vector.memset(warm[:, 0:1], 0.0)
         nc.scalar.activation(warm[:, 1:2], warm[:, 0:1], EXP)
 
-        tab_sc = keep.tile([P, T], U8, name="tab_sc", align_bytes=64)
-        wk_sc_raw = keep.tile([P, PASSES, H], U8, name="wk_sc_raw", align_bytes=64)
-        wo_sc = keep.tile([P, 1, N], U8, name="wo_sc", align_bytes=64)
+        tab_sc = slot("D", [P, T], U8)
+        wk_sc_raw = slot("E", [P, PASSES, H], U8)
         v_sc1 = keep.tile([P, S], U8, name="v_sc1", align_bytes=64)
         nc.gpsimd.memset(tab_sc[:].bitcast(I32), 0)
-        load_scale_rows(tab_sc, tab_scales, True)
         nc.gpsimd.memset(wk_sc_raw[:].bitcast(I32), 0)
-        load_scale_rows(wk_sc_raw, wk_scales, False)
         nc.gpsimd.memset(v_sc1[:].bitcast(I32), 0)
-        nc.gpsimd.memset(wo_sc[:].bitcast(I32), 0)
 
         tab_list = keep.tile([P, S // LANES], U16, name="tab_list")
         nc.sync.dma_start(tab_list[:], offs)
-        wk_raw = keep.tile([P, PASSES, 2 * H], U8, name="wk_raw", align_bytes=64)
-        nc.sync.dma_start(out=wk_raw[:].bitcast(I32), in_=wk_words.rearrange("a p n -> p a n").bitcast(I32))
-        tab = []
-        for a in range(PASSES):
-            words = stream.tile([P, T], I32, name="slot%d" % a, align_bytes=64)
-            nc.sync.dma_start(out=words[:], in_=tab_words[a].rearrange("p t i -> p (t i)").bitcast(I32))
-            tab.append(words)
         head_lists = keep.tile([P, S // LANES], U16, name="head_lists")
         nc.sync.dma_start(head_lists[:], offs2)
-        weights = keep.tile([P, S], F32, name="weights")
+        wk_raw = slot("A", [P, PASSES, 2 * H], U8)
+        nc.sync.dma_start(out=wk_raw[:].bitcast(I32), in_=wk_words.rearrange("a p n -> p a n").bitcast(I32))
+        tab = [slot("B", [P, T], I32), slot("C", [P, T], I32)]
+        for a in range(PASSES):
+            nc.sync.dma_start(out=tab[a][:], in_=tab_words[a].rearrange("p t i -> p (t i)").bitcast(I32))
+        weights = slot("W", [P, S], F32)
         nc.sync.dma_start(out=weights[:], in_=wgt)
+        load_scale_rows(tab_sc, tab_scales, True)
 
         x_rows = xT.rearrange("(a p i) t -> a i p t", a=PASSES, i=PACK)
 
-        def load_plane(a, i):
-            plane = stream.tile([P, T], F32, name="slot%d" % [2, 3, 4, 5, 7, 0, 2, 3][4 * a + i], align_bytes=64)
+        def load_plane(a, i, tag):
+            plane = slot(tag, [P, T], F32)
             nc.sync.dma_start(out=plane[:], in_=x_rows[a, i])
             return plane
 
-        def load_weight(w, a, slot):
-            raw = stream.tile([P, PACK, H], F32, name="slot%d" % slot, align_bytes=64)
+        def load_weight(w, a, tag):
+            raw = slot(tag, [P, PACK, H], F32)
             nc.sync.dma_start(out=raw[:], in_=w.rearrange("(a p j) r -> a p j r", a=PASSES, j=PACK)[a])
             return raw
 
-        wk_codes = keep.tile([P, PASSES, PACK, 2 * P], U8, name="wk_codes", align_bytes=64)
+        wk_codes = slot("F", [P, PASSES, PACK, 2 * P], U8)
         nc.vector.tensor_copy(
             out=wk_codes[:].bitcast(U16),
             in_=wk_raw[:].bitcast(U16).rearrange("p a (m t) -> p a t m", t=PACK),
         )
+        planes = [load_plane(0, 0, "A")]
+        load_scale_rows(wk_sc_raw, wk_scales, False)
+        v_codes = [keep.tile([P, S], U32, name="v_codes%d" % a, align_bytes=64) for a in range(PASSES)]
+        nc.vector.tensor_copy(v_codes[0][:], tab[0][:].bitcast(U32).indirect(tab_list[:]))
+        planes.append(load_plane(0, 1, "B"))
+        nc.vector.tensor_copy(v_codes[1][:], tab[1][:].bitcast(U32).indirect(tab_list[:]))
+        planes.append(load_plane(0, 2, "C"))
+        v_sc0 = keep.tile([P, S], U8, name="v_sc0", align_bytes=64)
+        nc.vector.tensor_copy(v_sc0[:], tab_sc[:].indirect(tab_list[:]))
+        nc.sync.dma_start(out=v_sc1[0 : P - 4, :].bitcast(I32), in_=v_sc0[4:P, :].bitcast(I32))
+        v_sc = [v_sc0, v_sc1]
+        planes.append(load_plane(0, 3, "D"))
         wk_sc = keep.tile([P, PASSES, PACK, P], U8, name="wk_sc", align_bytes=64)
         nc.vector.tensor_copy(out=wk_sc[:], in_=wk_sc_raw[:].rearrange("p a (m t) -> p a t m", t=PACK))
 
-        v_codes = []
-        for a in range(PASSES):
-            picked = keep.tile([P, S], U32, name="v_codes%d" % a, align_bytes=64)
-            nc.vector.tensor_copy(picked[:], tab[a][:].bitcast(U32).indirect(tab_list[:]))
-            v_codes.append(picked)
-        v_sc0 = keep.tile([P, S], U8, name="v_sc0", align_bytes=64)
-        nc.vector.tensor_copy(v_sc0[:], tab_sc[:].indirect(tab_list[:]))
-        nc.gpsimd.dma_start(out=v_sc1[0 : P - 4, :].bitcast(I32), in_=v_sc0[4:P, :].bitcast(I32))
-        v_sc = [v_sc0, v_sc1]
-        load_scale_rows(wo_sc, wo_scales, False)
+        def new_bank(c, shape):
+            return psum.tile(shape, F32, name="bank%d" % c)
 
-        def project(tag, bufs, c, w_codes, w_sc, w_dtype, a_codes, a_sc):
-            bank = psum.tile([P, PACK, CH], F32, name=tag, bufs=bufs)
+        def project(bank, c, a, w_codes, w_sc, w_dtype, a_codes, a_sc):
             cols = slice(c * CH, (c + 1) * CH)
             for t in range(PACK):
-                for a in range(PASSES):
-                    nc.tensor.matmul_mx(
-                        out=bank[:, t, :],
-                        lhsT=w_codes(a, t).bitcast(w_dtype),
-                        lhsT_scale=w_sc(a, t),
-                        rhs=a_codes[a][:, cols].bitcast(FP8X4),
-                        rhs_scale=a_sc[a][:, cols],
-                        start=(a == 0),
-                        stop=(a == PASSES - 1),
-                    )
+                nc.tensor.matmul_mx(
+                    out=bank[:, t, :],
+                    lhsT=w_codes(t).bitcast(w_dtype),
+                    lhsT_scale=w_sc(t),
+                    rhs=a_codes[:, cols].bitcast(FP8X4),
+                    rhs_scale=a_sc[:, cols],
+                    start=(a == 0 and t == 0),
+                    stop=(a == PASSES - 1 and t == PACK - 1),
+                )
+
+        def project_fp8(bank, c, a, w_mx, a_codes, a_sc):
+            project(
+                bank, c, a,
+                lambda t: w_mx[0][:, t * P : (t + 1) * P], lambda t: w_mx[1][:, t * P : (t + 1) * P],
+                FP8X4, a_codes, a_sc,
+            )
+
+        def by_token(bank):
             return bank[:].rearrange("p t n -> p n t")
 
         keys = []
         for c in range(S // CH):
-            bank = project(*[("kv", 3), ("q", 3), ("o", 2)][c % 3], c, lambda a, t: wk_codes[:, a, t, :], lambda a, t: wk_sc[:, a, t, :], FP4X4, v_codes, v_sc)
+            bank = new_bank(c, [P, PACK, CH])
+            for a in range(PASSES):
+                project(bank, c, a, lambda t: wk_codes[:, a, t, :], lambda t: wk_sc[:, a, t, :], FP4X4, v_codes[a], v_sc[a])
             if c % 2 == 0:
                 keys.append(keep.tile([P, PAIR, PACK], F32, name="key%d" % c))
-            nc.scalar.copy(out=keys[c // 2][:, (c % 2) * CH : (c % 2 + 1) * CH, :], in_=bank)
+            nc.scalar.copy(out=keys[c // 2][:, (c % 2) * CH : (c % 2 + 1) * CH, :], in_=by_token(bank))
 
         def gather(dst, plane, lo, hi):
             nc.vector.tensor_tensor(
@@ -140,19 +151,19 @@ def tile_list_picked_exp_scores_kernel(
                 in_=picked[:, :, lo:hi].rearrange("p i (c n) -> p c i n", n=4),
             )
 
-        def cast_weight_scalar(raw, name):
-            dealt = keep.tile([P, PACK, P, PACK], BF16, name=name, align_bytes=64)
+        def cast_weight_scalar(raw, dealt):
             nc.scalar.copy(
                 out=dealt[:].rearrange("p t m j -> p m j t"), in_=raw[:].rearrange("p j (m t) -> p m j t", t=PACK)
             )
             return dealt
 
-        def cast_weight_gpsimd(raw, name):
-            dealt = keep.tile([P, PACK, P, PACK], BF16, name=name, align_bytes=64)
+        def cast_weight_gpsimd(raw, dealt, vector_from):
             src = raw[:].rearrange("p j (m t) -> p m t j", t=PACK)
             dst = dealt[:].rearrange("p t m j -> p m t j")
-            for m0 in range(0, P, 32):
+            for m0 in range(0, vector_from, 32):
                 nc.gpsimd.tensor_scalar(dst[:, m0 : m0 + 32], src[:, m0 : m0 + 32], 1.0, 0.0, MULT, ADD)
+            if vector_from < P:
+                nc.vector.tensor_copy(dst[:, vector_from:], src[:, vector_from:])
             return dealt
 
         def quantize_weight(dealt, name, codes):
@@ -162,8 +173,8 @@ def tile_list_picked_exp_scores_kernel(
             )
             return codes, sc
 
-        picked = [keep.tile([P, PACK, S], F32, name="picked%d" % a) for a in range(PASSES)]
-        woven = [keep.tile([P, S, PACK], BF16, name="woven%d" % a, align_bytes=64) for a in range(PASSES)]
+        picked = [slot("I", [P, PACK, S], F32), keep.tile([P, PACK, S], F32, name="picked1")]
+        woven = [slot("F", [P, S, PACK], BF16), keep.tile([P, S, PACK], BF16, name="woven1", align_bytes=64)]
         x_codes = [None, keep.tile([P, S], U32, name="x_codes1", align_bytes=64)]
         x_sc = [keep.tile([P, S], U8, name="x_sc%d" % a, align_bytes=64) for a in range(PASSES)]
 
@@ -174,69 +185,91 @@ def tile_list_picked_exp_scores_kernel(
                 in_=woven[a][:, lo:hi, :].rearrange("p n i -> p (n i)"),
             )
 
-        for i in range(PACK):
-            gather(picked[0][:, i, :], load_plane(0, i), 0, S)
-        wq_raw = load_weight(wq, 0, 6)
+        gather(picked[0][:, 0, :], planes[0], 0, S)
+        wq_raw = [load_weight(wq, 0, "A")]
+        gather(picked[0][:, 1, :], planes[1], 0, S)
+        later = [load_plane(1, 0, "E"), load_plane(1, 1, "B")]
+        gather(picked[0][:, 2, :], planes[2], 0, S)
+        later.append(load_plane(1, 2, "C"))
+        gather(picked[0][:, 3, :], planes[3], 0, S)
+        wq_raw.append(load_weight(wq, 1, "D"))
         for lo in range(0, S, 512):
             weave(picked[0], woven[0], lo, lo + 512)
-        wq_dealt = [cast_weight_scalar(wq_raw, "wq0")]
-        for i in range(2):
-            gather(picked[1][:, i, :], load_plane(1, i), 0, S)
-        x_codes[0] = stream.tile([P, S], U32, name="slot0", align_bytes=64)
+        wq_dealt = [cast_weight_scalar(wq_raw[0], slot("G", [P, PACK, P, PACK], BF16))]
+        gather(picked[1][:, 0, :], later[0], 0, S)
+        last = load_plane(1, 3, "E")
+        for i in range(1, 3):
+            gather(picked[1][:, i, :], later[i], 0, S)
+        wv_raw = [load_weight(wv, 0, "B")]
+        after_x6 = slot("C", [P, S + H], U32)
+        x_codes[0] = after_x6[:, 0:S]
         for lo in range(0, S, 512):
             quantize_x(0, lo, lo + 512)
-        wq_dealt.append(cast_weight_scalar(load_weight(wq, 1, 1), "wq1"))
-        gather(picked[1][:, 2, :], load_plane(1, 2), 0, S)
-        wq_codes = stream.tile([P, PASSES, H], U32, name="slot2", align_bytes=64)
-        wq_mx = [quantize_weight(wq_dealt[a], "wq%d" % a, wq_codes[:, a, :]) for a in range(PASSES)]
-        last = load_plane(1, 3)
-        wv_raw = [load_weight(wv, a, 4 + a) for a in range(PASSES)]
-        wo_codes = keep.tile([P, N], I32, name="wo_codes", align_bytes=64)
+        wq_mx = [quantize_weight(wq_dealt[0], "wq0", after_x6[:, S : S + H])]
+        wv_raw.append(load_weight(wv, 1, "G"))
+        q_banks = [new_bank(c, [P, PACK, CH]) for c in range(S // CH)]
+        for c in range(S // CH):
+            project_fp8(q_banks[c], c, 0, wq_mx[0], x_codes[0], x_sc[0])
+        wq_dealt.append(cast_weight_scalar(wq_raw[1], slot("H", [P, PACK, P, PACK], BF16)))
+        wq1_codes = keep.tile([P, H], U32, name="wq1_codes", align_bytes=64)
+        wq_mx.append(quantize_weight(wq_dealt[1], "wq1", wq1_codes[:]))
+        wo_codes = slot("D", [P, N], I32)
         nc.sync.dma_start(out=wo_codes[:], in_=wo_words[0].rearrange("p c i -> p (c i)").bitcast(I32))
-        bias = keep.tile([P, N // P], F32, name="bias")
+        bias = slot("H", [P, N // P], F32)
         with nc.allow_non_contiguous_dma(reason="one bias value a partition"):
             nc.sync.dma_start(out=bias[:], in_=bo.rearrange("(u p) -> p u", p=P))
 
         for lo in range(0, S, PAIR):
             gather(picked[1][:, 3, :], last, lo, lo + PAIR)
+        wo_sc = slot("W", [P, 1, N], U8)
+        nc.gpsimd.memset(wo_sc[:].bitcast(I32), 0)
+        load_scale_rows(wo_sc, wo_scales, False)
+        wv_mx = []
+
+        def prepare_wv(a):
+            dealt = slot("V%d" % a, [P, PACK, P, PACK], BF16)
+            cast_weight_gpsimd(wv_raw[a], dealt, P)
+            codes = keep.tile([P, H], U32, name="wv%d_codes" % a, align_bytes=64)
+            wv_mx.append(quantize_weight(dealt, "wv%d" % a, codes[:]))
+
         scores = []
         for g in range(S // PAIR):
             weave(picked[1], woven[1], g * PAIR, (g + 1) * PAIR)
             quantize_x(1, g * PAIR, (g + 1) * PAIR)
-            prod = ring.tile([P, PAIR, PACK], F32, name="prod")
+            if g >= 2:
+                prepare_wv(g - 2)
+            prod = slot(["P0", "P1", "V0", "V1"][g], [P, PAIR, PACK], F32)
             for u in range(2):
                 c = 2 * g + u
-                bank = project(
-                    "q", 3, c,
-                    lambda a, t: wq_mx[a][0][:, t * P : (t + 1) * P],
-                    lambda a, t: wq_mx[a][1][:, t * P : (t + 1) * P],
-                    FP8X4, x_codes, x_sc,
-                )
-                nc.vector.tensor_tensor(prod[:, u * CH : (u + 1) * CH, :], bank, keys[g][:, u * CH : (u + 1) * CH, :], MULT)
+                project_fp8(q_banks[c], c, 1, wq_mx[1], x_codes[1], x_sc[1])
+                nc.vector.tensor_tensor(prod[:, u * CH : (u + 1) * CH, :], by_token(q_banks[c]), keys[g][:, u * CH : (u + 1) * CH, :], MULT)
             nc.scalar.activation(keys[g][:], prod[:], EXP)
             scores.append(keys[g])
 
-        wv_mx = [quantize_weight(cast_weight_gpsimd(wv_raw[a], "wv%d" % a), "wv%d" % a, x_codes[0][:, a * H : (a + 1) * H]) for a in range(PASSES)]
+        v_banks = [new_bank(c, [P, PACK, CH]) for c in range(S // CH)]
+        for c in range(4):
+            project_fp8(v_banks[c], c, 0, wv_mx[0], v_codes[0], v_sc[0])
 
         out_rows = out.rearrange("(u p) j -> p u j", p=P)
-        for g in range(S // PAIR):
-            h = ring.tile([P, PAIR, PACK], BF16, name="h", align_bytes=64)
-            for u in range(2):
-                bank = project(
-                    "kv", 3, 2 * g + u,
-                    lambda a, t: wv_mx[a][0][:, t * P : (t + 1) * P],
-                    lambda a, t: wv_mx[a][1][:, t * P : (t + 1) * P],
-                    FP8X4, v_codes, v_sc,
+        for first, count in ((0, 2), (2, 2), (4, 2), (6, 1), (7, 1)):
+            width = count * CH
+            h = ring.tile([P, width, PACK], BF16, name="h", align_bytes=64)
+            for u in range(count):
+                c = first + u
+                if c >= 4:
+                    project_fp8(v_banks[c], c, 0, wv_mx[0], v_codes[0], v_sc[0])
+                project_fp8(v_banks[c], c, 1, wv_mx[1], v_codes[1], v_sc[1])
+                nc.vector.tensor_tensor(
+                    h[:, u * CH : (u + 1) * CH, :], by_token(v_banks[c]),
+                    scores[c // 2][:, (c % 2) * CH : (c % 2 + 1) * CH, :], MULT,
                 )
-                nc.vector.tensor_tensor(h[:, u * CH : (u + 1) * CH, :], bank, scores[g][:, u * CH : (u + 1) * CH, :], MULT)
-            h_codes = ring.tile([P, PAIR], U32, name="h_codes", align_bytes=64)
-            h_sc = ring.tile([P, PAIR], U8, name="h_sc", align_bytes=64)
+            h_codes = ring.tile([P, width], U32, name="h_codes", align_bytes=64)
+            h_sc = ring.tile([P, width], U8, name="h_sc", align_bytes=64)
             nc.vector.quantize_mx(
                 out=h_codes[:].bitcast(FP8X4), scales=h_sc[:], in_=h[:].rearrange("p n t -> p (n t)")
             )
-            result = ring.tile([P, N // P, PAIR], F32, name="result")
             for half in range(2):
-                bank = psum.tile([P, 2, PAIR], F32, name="o", bufs=2)
+                bank = new_bank({0: 0, 2: 2, 4: 4, 6: 0, 7: 2}[first] + half, [P, 2, width])
                 for s in range(2):
                     u = 2 * half + s
                     nc.tensor.matmul_mx(
@@ -248,7 +281,13 @@ def tile_list_picked_exp_scores_kernel(
                         start=True,
                         stop=True,
                     )
+                result = ring.tile([P, 2, width], F32, name="result", bufs=4)
                 for s in range(2):
                     u = 2 * half + s
-                    nc.scalar.activation(result[:, u, :], bank[:, s, :], IDENTITY, bias=bias[:, u : u + 1])
-            nc.sync.dma_start(out=out_rows[:, :, g * PAIR : (g + 1) * PAIR], in_=result[:])
+                    if first == 7 and half == 1:
+                        nc.vector.tensor_scalar_add(result[:, s, :], bank[:, s, :], bias[:, u : u + 1])
+                    else:
+                        nc.scalar.activation(result[:, s, :], bank[:, s, :], IDENTITY, bias=bias[:, u : u + 1])
+                nc.sync.dma_start(
+                    out=out_rows[:, 2 * half : 2 * half + 2, first * CH : first * CH + width], in_=result[:]
+                )

@@ -21,9 +21,18 @@ IDENTITY = mybir.ActivationFunctionType.Identity
 P = 128
 PACK = 4
 PASSES = 2
-CH = 128
-PAIR = 256
-LANES = 16
+LIST_ROWS = 16
+QUADRANT = 32
+CHUNK = 128
+PAIR = 2 * CHUNK
+HALF = S // 2
+CHUNKS = S // CHUNK
+EARLY_Q = 2
+EARLY_VAL = 4
+GPSIMD_STEP = 32
+WV_SPLIT = (P, 96)
+MOVED_ROWS = 112
+OUT_GROUPS = ((0, 2, 0), (2, 2, 2), (4, 2, 4), (6, 1, 0), (7, 1, 2))
 
 
 def tile_list_picked_exp_scores_kernel(
@@ -36,258 +45,283 @@ def tile_list_picked_exp_scores_kernel(
         ring = ctx.enter_context(tc.tile_pool(name="ring", bufs=3))
         psum = ctx.enter_context(tc.psum_pool(name="psum", bufs=1))
 
-        def slot(tag, shape, dtype):
-            return shared.tile(shape, dtype, name=tag, align_bytes=64)
+        def shared_tile(name, shape, dtype):
+            return shared.tile(shape, dtype, name=name, align_bytes=64)
 
-        def load_scale_rows(plane, rows, packed):
-            for quad in range(4):
-                src = rows[:, 4 * quad : 4 * quad + 4, :]
-                if packed:
-                    dst = plane[32 * quad : 32 * quad + 4 * rows.shape[0], :]
-                else:
-                    dst = plane[32 * quad : 32 * quad + 4, :, :]
-                    src = src.rearrange("a r n -> r a n")
-                nc.sync.dma_start(out=dst.bitcast(I32), in_=src.bitcast(I32))
+        def psum_bank(index, shape):
+            return psum.tile(shape, F32, name="bank%d" % index)
 
-        warm = keep.tile([P, 2], F32, name="warm")
-        nc.vector.memset(warm[:, 0:1], 0.0)
-        nc.scalar.activation(warm[:, 1:2], warm[:, 0:1], EXP)
+        def load_scales_side_by_side(tile, rows):
+            for quad in range(P // QUADRANT):
+                nc.sync.dma_start(
+                    out=tile[QUADRANT * quad : QUADRANT * quad + 4, :, :].bitcast(I32),
+                    in_=rows[:, 4 * quad : 4 * quad + 4, :].rearrange("a r n -> r a n").bitcast(I32),
+                )
 
-        tab_sc = slot("D", [P, T], U8)
-        wk_sc_raw = slot("E", [P, PASSES, H], U8)
+        def load_plane(a, i, name):
+            plane = shared_tile(name, [P, T], F32)
+            nc.sync.dma_start(out=plane[:], in_=xT.rearrange("(a p i) t -> a i p t", a=PASSES, i=PACK)[a, i])
+            return plane
+
+        def load_weight(w, a, name):
+            raw = shared_tile(name, [P, PACK, H], F32)
+            nc.sync.dma_start(out=raw[:], in_=w.rearrange("(a p j) r -> a p j r", a=PASSES, j=PACK)[a])
+            return raw
+
+        def project(bank, c, nth, w_codes, w_scales, w_dtype, a_codes, a_scales):
+            entries = slice(c * CHUNK, (c + 1) * CHUNK)
+            for t in range(PACK):
+                nc.tensor.matmul_mx(
+                    out=bank[:, t, :],
+                    lhsT=w_codes(t).bitcast(w_dtype),
+                    lhsT_scale=w_scales(t),
+                    rhs=a_codes[:, entries].bitcast(FP8X4),
+                    rhs_scale=a_scales[:, entries],
+                    start=(nth == 0 and t == 0),
+                    stop=(nth == PASSES - 1 and t == PACK - 1),
+                )
+
+        def project_e4m3(bank, c, nth, weight, a_codes, a_scales):
+            codes, scales = weight
+            project(
+                bank, c, nth,
+                lambda t: codes[:, t * P : (t + 1) * P], lambda t: scales[:, t * P : (t + 1) * P], FP8X4,
+                a_codes, a_scales,
+            )
+
+        def by_entry(bank):
+            return bank[:].rearrange("p t n -> p n t")
+
+        def chunk_of(pairs, c):
+            return pairs[c // 2][:, (c % 2) * CHUNK : (c % 2 + 1) * CHUNK, :]
+
+        tab_sc = shared_tile("load3", [P, T], U8)
+        wk_sc_raw = shared_tile("load4", [P, PASSES, H], U8)
         v_sc1 = keep.tile([P, S], U8, name="v_sc1", align_bytes=64)
         nc.gpsimd.memset(tab_sc[:].bitcast(I32), 0)
         nc.gpsimd.memset(wk_sc_raw[:].bitcast(I32), 0)
         nc.gpsimd.memset(v_sc1[:].bitcast(I32), 0)
 
-        tab_list = keep.tile([P, S // LANES], U16, name="tab_list")
+        tab_list = keep.tile([P, S // LIST_ROWS], U16, name="tab_list")
         nc.sync.dma_start(tab_list[:], offs)
-        head_lists = keep.tile([P, S // LANES], U16, name="head_lists")
+        head_lists = keep.tile([P, S // LIST_ROWS], U16, name="head_lists")
         nc.sync.dma_start(head_lists[:], offs2)
-        wk_raw = slot("A", [P, PASSES, 2 * H], U8)
+        wk_raw = shared_tile("load0", [P, PASSES, 2 * H], U8)
         nc.sync.dma_start(out=wk_raw[:].bitcast(I32), in_=wk_words.rearrange("a p n -> p a n").bitcast(I32))
-        tab = [slot("B", [P, T], I32), slot("C", [P, T], I32)]
+        tab = [shared_tile("load1", [P, T], I32), shared_tile("load2", [P, T], I32)]
         for a in range(PASSES):
             nc.sync.dma_start(out=tab[a][:], in_=tab_words[a].rearrange("p t i -> p (t i)").bitcast(I32))
-        weights = slot("W", [P, S], F32)
+        weights = shared_tile("weights", [P, S], F32)
         nc.sync.dma_start(out=weights[:], in_=wgt)
-        load_scale_rows(tab_sc, tab_scales, True)
+        for quad in range(P // QUADRANT):
+            nc.sync.dma_start(
+                out=tab_sc[QUADRANT * quad : QUADRANT * quad + 4 * PASSES, :].bitcast(I32),
+                in_=tab_scales[:, 4 * quad : 4 * quad + 4, :].bitcast(I32),
+            )
 
-        x_rows = xT.rearrange("(a p i) t -> a i p t", a=PASSES, i=PACK)
-
-        def load_plane(a, i, tag):
-            plane = slot(tag, [P, T], F32)
-            nc.sync.dma_start(out=plane[:], in_=x_rows[a, i])
-            return plane
-
-        def load_weight(w, a, tag):
-            raw = slot(tag, [P, PACK, H], F32)
-            nc.sync.dma_start(out=raw[:], in_=w.rearrange("(a p j) r -> a p j r", a=PASSES, j=PACK)[a])
-            return raw
-
-        wk_codes = slot("F", [P, PASSES, PACK, 2 * P], U8)
+        wk_codes = shared_tile("wk_then_xg", [P, PASSES, PACK, 2 * P], U8)
         nc.vector.tensor_copy(
             out=wk_codes[:].bitcast(U16),
             in_=wk_raw[:].bitcast(U16).rearrange("p a (m t) -> p a t m", t=PACK),
         )
-        planes = [load_plane(0, 0, "A")]
-        load_scale_rows(wk_sc_raw, wk_scales, False)
+        planes0 = [load_plane(0, 0, "load0")]
+        load_scales_side_by_side(wk_sc_raw, wk_scales)
         v_codes = [keep.tile([P, S], U32, name="v_codes%d" % a, align_bytes=64) for a in range(PASSES)]
-        nc.vector.tensor_copy(v_codes[0][:], tab[0][:].bitcast(U32).indirect(tab_list[:]))
-        planes.append(load_plane(0, 1, "B"))
-        nc.vector.tensor_copy(v_codes[1][:], tab[1][:].bitcast(U32).indirect(tab_list[:]))
-        planes.append(load_plane(0, 2, "C"))
+        for a in range(PASSES):
+            nc.vector.tensor_copy(v_codes[a][:], tab[a][:].bitcast(U32).indirect(tab_list[:]))
+            planes0.append(load_plane(0, 1 + a, "load%d" % (1 + a)))
         v_sc0 = keep.tile([P, S], U8, name="v_sc0", align_bytes=64)
         nc.vector.tensor_copy(v_sc0[:], tab_sc[:].indirect(tab_list[:]))
-        nc.sync.dma_start(out=v_sc1[0 : P - 4, :].bitcast(I32), in_=v_sc0[4:P, :].bitcast(I32))
+        nc.scalar.dma_start(out=v_sc1[0:MOVED_ROWS, :].bitcast(I32), in_=v_sc0[4 : 4 + MOVED_ROWS, :].bitcast(I32))
         v_sc = [v_sc0, v_sc1]
-        planes.append(load_plane(0, 3, "D"))
+        planes0.append(load_plane(0, 3, "load3"))
         wk_sc = keep.tile([P, PASSES, PACK, P], U8, name="wk_sc", align_bytes=64)
         nc.vector.tensor_copy(out=wk_sc[:], in_=wk_sc_raw[:].rearrange("p a (m t) -> p a t m", t=PACK))
 
-        def new_bank(c, shape):
-            return psum.tile(shape, F32, name="bank%d" % c)
-
-        def project(bank, c, a, w_codes, w_sc, w_dtype, a_codes, a_sc):
-            cols = slice(c * CH, (c + 1) * CH)
-            for t in range(PACK):
-                nc.tensor.matmul_mx(
-                    out=bank[:, t, :],
-                    lhsT=w_codes(t).bitcast(w_dtype),
-                    lhsT_scale=w_sc(t),
-                    rhs=a_codes[:, cols].bitcast(FP8X4),
-                    rhs_scale=a_sc[:, cols],
-                    start=(a == 0 and t == 0),
-                    stop=(a == PASSES - 1 and t == PACK - 1),
+        keys = [keep.tile([P, PAIR, PACK], F32, name="keys%d" % g) for g in range(S // PAIR)]
+        for c in range(CHUNKS):
+            bank = psum_bank(c, [P, PACK, CHUNK])
+            for nth, a in enumerate((1, 0)):
+                project(
+                    bank, c, nth, lambda t: wk_codes[:, a, t, :], lambda t: wk_sc[:, a, t, :], FP4X4, v_codes[a], v_sc[a]
                 )
-
-        def project_fp8(bank, c, a, w_mx, a_codes, a_sc):
-            project(
-                bank, c, a,
-                lambda t: w_mx[0][:, t * P : (t + 1) * P], lambda t: w_mx[1][:, t * P : (t + 1) * P],
-                FP8X4, a_codes, a_sc,
-            )
-
-        def by_token(bank):
-            return bank[:].rearrange("p t n -> p n t")
-
-        keys = []
-        for c in range(S // CH):
-            bank = new_bank(c, [P, PACK, CH])
-            for a in range(PASSES):
-                project(bank, c, a, lambda t: wk_codes[:, a, t, :], lambda t: wk_sc[:, a, t, :], FP4X4, v_codes[a], v_sc[a])
-            if c % 2 == 0:
-                keys.append(keep.tile([P, PAIR, PACK], F32, name="key%d" % c))
-            nc.scalar.copy(out=keys[c // 2][:, (c % 2) * CH : (c % 2 + 1) * CH, :], in_=by_token(bank))
+            nc.scalar.copy(out=chunk_of(keys, c), in_=by_entry(bank))
 
         def gather(dst, plane, lo, hi):
-            nc.vector.tensor_tensor(
-                dst[:, lo:hi], plane[:].indirect(head_lists[:, lo // LANES : hi // LANES]), weights[:, lo:hi], MULT
-            )
+            lists = head_lists[:, lo // LIST_ROWS : hi // LIST_ROWS]
+            nc.vector.tensor_tensor(dst[:, lo:hi], plane[:].indirect(lists), weights[:, lo:hi], MULT)
 
-        def weave(picked, woven, lo, hi):
+        def interleave(picked_pass, woven, lo, hi):
             nc.scalar.copy(
-                out=woven[:, lo:hi, :].rearrange("p (c n) i -> p c i n", n=4),
-                in_=picked[:, :, lo:hi].rearrange("p i (c n) -> p c i n", n=4),
+                out=woven.rearrange("p (c n) i -> p c i n", n=4),
+                in_=picked_pass[:, :, lo:hi].rearrange("p i (c n) -> p c i n", n=4),
             )
 
-        def cast_weight_scalar(raw, dealt):
+        def deal_wq(raw, name):
+            dealt = shared_tile(name, [P, PACK, P, PACK], BF16)
             nc.scalar.copy(
                 out=dealt[:].rearrange("p t m j -> p m j t"), in_=raw[:].rearrange("p j (m t) -> p m j t", t=PACK)
             )
             return dealt
 
-        def cast_weight_gpsimd(raw, dealt, vector_from):
+        def deal_wv(raw, name, split):
+            dealt = shared_tile(name, [P, PACK, P, PACK], BF16)
             src = raw[:].rearrange("p j (m t) -> p m t j", t=PACK)
             dst = dealt[:].rearrange("p t m j -> p m t j")
-            for m0 in range(0, vector_from, 32):
-                nc.gpsimd.tensor_scalar(dst[:, m0 : m0 + 32], src[:, m0 : m0 + 32], 1.0, 0.0, MULT, ADD)
-            if vector_from < P:
-                nc.vector.tensor_copy(dst[:, vector_from:], src[:, vector_from:])
+            for m0 in range(0, split, GPSIMD_STEP):
+                ms = slice(m0, m0 + GPSIMD_STEP)
+                nc.gpsimd.tensor_scalar(dst[:, ms], src[:, ms], 1.0, 0.0, MULT, ADD)
+            if split < P:
+                nc.vector.tensor_copy(dst[:, split:], src[:, split:])
             return dealt
 
-        def quantize_weight(dealt, name, codes):
-            sc = keep.tile([P, H], U8, name=name + "_sc", align_bytes=64)
+        def quantize_weight(dealt, codes, name):
+            scales = keep.tile([P, H], U8, name=name, align_bytes=64)
             nc.vector.quantize_mx(
-                out=codes.bitcast(FP8X4), scales=sc[:], in_=dealt[:].rearrange("p t m j -> p (t m j)")
+                out=codes.bitcast(FP8X4), scales=scales[:], in_=dealt[:].rearrange("p t m j -> p (t m j)")
             )
-            return codes, sc
+            return codes, scales
 
-        picked = [slot("I", [P, PACK, S], F32), keep.tile([P, PACK, S], F32, name="picked1")]
-        woven = [slot("F", [P, S, PACK], BF16), keep.tile([P, S, PACK], BF16, name="woven1", align_bytes=64)]
-        x_codes = [None, keep.tile([P, S], U32, name="x_codes1", align_bytes=64)]
-        x_sc = [keep.tile([P, S], U8, name="x_sc%d" % a, align_bytes=64) for a in range(PASSES)]
-
-        def quantize_x(a, lo, hi):
+        def quantize_xg(codes, scales, woven, lo, hi):
             nc.vector.quantize_mx(
-                out=x_codes[a][:, lo:hi].bitcast(FP8X4),
-                scales=x_sc[a][:, lo:hi],
-                in_=woven[a][:, lo:hi, :].rearrange("p n i -> p (n i)"),
+                out=codes[:, lo:hi].bitcast(FP8X4), scales=scales[:, lo:hi], in_=woven.rearrange("p n i -> p (n i)")
             )
 
-        gather(picked[0][:, 0, :], planes[0], 0, S)
-        wq_raw = [load_weight(wq, 0, "A")]
-        gather(picked[0][:, 1, :], planes[1], 0, S)
-        later = [load_plane(1, 0, "E"), load_plane(1, 1, "B")]
-        gather(picked[0][:, 2, :], planes[2], 0, S)
-        later.append(load_plane(1, 2, "C"))
-        gather(picked[0][:, 3, :], planes[3], 0, S)
-        wq_raw.append(load_weight(wq, 1, "D"))
-        for lo in range(0, S, 512):
-            weave(picked[0], woven[0], lo, lo + 512)
-        wq_dealt = [cast_weight_scalar(wq_raw[0], slot("G", [P, PACK, P, PACK], BF16))]
-        gather(picked[1][:, 0, :], later[0], 0, S)
-        last = load_plane(1, 3, "E")
-        for i in range(1, 3):
-            gather(picked[1][:, i, :], later[i], 0, S)
-        wv_raw = [load_weight(wv, 0, "B")]
-        after_x6 = slot("C", [P, S + H], U32)
-        x_codes[0] = after_x6[:, 0:S]
-        for lo in range(0, S, 512):
-            quantize_x(0, lo, lo + 512)
-        wq_mx = [quantize_weight(wq_dealt[0], "wq0", after_x6[:, S : S + H])]
-        wv_raw.append(load_weight(wv, 1, "G"))
-        q_banks = [new_bank(c, [P, PACK, CH]) for c in range(S // CH)]
-        for c in range(S // CH):
-            project_fp8(q_banks[c], c, 0, wq_mx[0], x_codes[0], x_sc[0])
-        wq_dealt.append(cast_weight_scalar(wq_raw[1], slot("H", [P, PACK, P, PACK], BF16)))
-        wq1_codes = keep.tile([P, H], U32, name="wq1_codes", align_bytes=64)
-        wq_mx.append(quantize_weight(wq_dealt[1], "wq1", wq1_codes[:]))
-        wo_codes = slot("D", [P, N], I32)
-        nc.sync.dma_start(out=wo_codes[:], in_=wo_words[0].rearrange("p c i -> p (c i)").bitcast(I32))
-        bias = slot("H", [P, N // P], F32)
-        with nc.allow_non_contiguous_dma(reason="one bias value a partition"):
-            nc.sync.dma_start(out=bias[:], in_=bo.rearrange("(u p) -> p u", p=P))
-
+        picked = [keep.tile([P, PACK, S], F32, name="picked%d" % a) for a in range(PASSES)]
+        woven0 = shared_tile("wk_then_xg", [P, S, PACK], BF16)
+        gather(picked[0][:, 0, :], planes0[0], 0, S)
+        wq_raw = [load_weight(wq, 0, "load0")]
+        gather(picked[0][:, 1, :], planes0[1], 0, S)
+        planes1 = [load_plane(1, 0, "load4"), load_plane(1, 1, "load1")]
+        gather(picked[0][:, 2, :], planes0[2], 0, S)
+        planes1.append(load_plane(1, 2, "load2"))
+        gather(picked[0][:, 3, :], planes0[3], 0, S)
+        planes1.append(load_plane(1, 3, "load3"))
+        wq_dealt = [deal_wq(wq_raw[0], "wq0_then_bias")]
+        for lo in range(0, S, HALF):
+            interleave(picked[0], woven0[:, lo : lo + HALF, :], lo, lo + HALF)
+        gather(picked[1][:, 0, :], planes1[0], 0, S)
+        wq_raw.append(load_weight(wq, 1, "load4"))
+        gather(picked[1][:, 1, :], planes1[1], 0, S)
+        wv_raw = [load_weight(wv, 0, "load1")]
+        gather(picked[1][:, 2, :], planes1[2], 0, S)
+        wv_raw.append(load_weight(wv, 1, "load2"))
         for lo in range(0, S, PAIR):
-            gather(picked[1][:, 3, :], last, lo, lo + PAIR)
-        wo_sc = slot("W", [P, 1, N], U8)
+            gather(picked[1][:, 3, :], planes1[3], lo, lo + PAIR)
+        wo_sc = shared_tile("weights", [P, 1, N], U8)
         nc.gpsimd.memset(wo_sc[:].bitcast(I32), 0)
-        load_scale_rows(wo_sc, wo_scales, False)
-        wv_mx = []
 
-        def prepare_wv(a):
-            dealt = slot("V%d" % a, [P, PACK, P, PACK], BF16)
-            cast_weight_gpsimd(wv_raw[a], dealt, P)
-            codes = keep.tile([P, H], U32, name="wv%d_codes" % a, align_bytes=64)
-            wv_mx.append(quantize_weight(dealt, "wv%d" % a, codes[:]))
+        first_codes = shared_tile("load3", [P, S + H], U32)
+        xg_codes = [first_codes[:, 0:S], keep.tile([P, S], U32, name="xg_codes1", align_bytes=64)]
+        xg_sc = [keep.tile([P, S], U8, name="xg_sc%d" % a, align_bytes=64) for a in range(PASSES)]
+        quantize_xg(xg_codes[0], xg_sc[0], woven0[:, 0:HALF, :], 0, HALF)
+        wq_mx = [quantize_weight(wq_dealt[0], first_codes[:, S : S + H], "wq_sc0")]
+        quantize_xg(xg_codes[0], xg_sc[0], woven0[:, HALF:S, :], HALF, S)
+        q_banks = [psum_bank(c, [P, PACK, CHUNK]) for c in range(CHUNKS)]
+        for c in range(EARLY_Q):
+            project_e4m3(q_banks[c], c, 0, wq_mx[0], xg_codes[0], xg_sc[0])
 
-        scores = []
-        for g in range(S // PAIR):
-            weave(picked[1], woven[1], g * PAIR, (g + 1) * PAIR)
-            quantize_x(1, g * PAIR, (g + 1) * PAIR)
-            if g >= 2:
-                prepare_wv(g - 2)
-            prod = slot(["P0", "P1", "V0", "V1"][g], [P, PAIR, PACK], F32)
+        woven1 = [shared_tile("xg_then_wo", [P, PAIR, PACK], BF16)]
+        interleave(picked[1], woven1[0][:], 0, PAIR)
+        wq_dealt.append(deal_wq(wq_raw[1], "wq1_wv0_product"))
+        woven_rest = shared_tile("load4", [P, S - PAIR, PACK], BF16)
+        woven1.extend(woven_rest[:, lo : lo + PAIR, :] for lo in range(0, S - PAIR, PAIR))
+        wq1_codes = keep.tile([P, H], U32, name="wq1_codes", align_bytes=64)
+        wq_mx.append(quantize_weight(wq_dealt[1], wq1_codes[:], "wq_sc1"))
+
+        bias = shared_tile("wq0_then_bias", [P, N // P], F32)
+        with nc.allow_non_contiguous_dma(reason="one bias value a partition and tile of 128 outputs"):
+            nc.sync.dma_start(out=bias[:], in_=bo.rearrange("(u p) -> p u", p=P))
+        load_scales_side_by_side(wo_sc, wo_scales)
+        quantize_xg(xg_codes[1], xg_sc[1], woven1[0][:], 0, PAIR)
+        wo_codes = shared_tile("xg_then_wo", [P, N], I32)
+        nc.sync.dma_start(out=wo_codes[:], in_=wo_words[0].rearrange("p c i -> p (c i)").bitcast(I32))
+        for g in range(1, S // PAIR):
+            interleave(picked[1], woven1[g], g * PAIR, (g + 1) * PAIR)
+            quantize_xg(xg_codes[1], xg_sc[1], woven1[g], g * PAIR, (g + 1) * PAIR)
+
+        def prepare_wv(a, name):
+            dealt = deal_wv(wv_raw[a], name, WV_SPLIT[a])
+            codes = keep.tile([P, H], U32, name="wv_codes%d" % a, align_bytes=64)
+            return quantize_weight(dealt, codes[:], "wv_sc%d" % a)
+
+        def score_pair(g, name):
+            product = shared_tile(name, [P, PAIR, PACK], F32)
             for u in range(2):
                 c = 2 * g + u
-                project_fp8(q_banks[c], c, 1, wq_mx[1], x_codes[1], x_sc[1])
-                nc.vector.tensor_tensor(prod[:, u * CH : (u + 1) * CH, :], by_token(q_banks[c]), keys[g][:, u * CH : (u + 1) * CH, :], MULT)
-            nc.scalar.activation(keys[g][:], prod[:], EXP)
-            scores.append(keys[g])
-
-        v_banks = [new_bank(c, [P, PACK, CH]) for c in range(S // CH)]
-        for c in range(4):
-            project_fp8(v_banks[c], c, 0, wv_mx[0], v_codes[0], v_sc[0])
-
-        out_rows = out.rearrange("(u p) j -> p u j", p=P)
-        for first, count in ((0, 2), (2, 2), (4, 2), (6, 1), (7, 1)):
-            width = count * CH
-            h = ring.tile([P, width, PACK], BF16, name="h", align_bytes=64)
-            for u in range(count):
-                c = first + u
-                if c >= 4:
-                    project_fp8(v_banks[c], c, 0, wv_mx[0], v_codes[0], v_sc[0])
-                project_fp8(v_banks[c], c, 1, wv_mx[1], v_codes[1], v_sc[1])
+                if c < EARLY_Q:
+                    project_e4m3(q_banks[c], c, 1, wq_mx[1], xg_codes[1], xg_sc[1])
+                else:
+                    project_e4m3(q_banks[c], c, 0, wq_mx[1], xg_codes[1], xg_sc[1])
+                    project_e4m3(q_banks[c], c, 1, wq_mx[0], xg_codes[0], xg_sc[0])
                 nc.vector.tensor_tensor(
-                    h[:, u * CH : (u + 1) * CH, :], by_token(v_banks[c]),
-                    scores[c // 2][:, (c % 2) * CH : (c % 2 + 1) * CH, :], MULT,
+                    product[:, u * CHUNK : (u + 1) * CHUNK, :], by_entry(q_banks[c]), chunk_of(keys, c), MULT
                 )
+            nc.scalar.activation(keys[g][:], product[:], EXP)
+
+        score_pair(0, "product0")
+        score_pair(1, "product1")
+        wv_mx = [prepare_wv(0, "wq1_wv0_product")]
+        score_pair(2, "wq1_wv0_product")
+        score_pair(3, "product3")
+        wv_mx.append(prepare_wv(1, "wv1"))
+        scores = keys
+
+        val_banks = [psum_bank(c, [P, PACK, CHUNK]) for c in range(CHUNKS)]
+        for c in range(EARLY_VAL):
+            project_e4m3(val_banks[c], c, 0, wv_mx[0], v_codes[0], v_sc[0])
+        h_tiles = [
+            keep.tile([P, count * CHUNK, PACK], BF16, name="h%d" % first, align_bytes=64)
+            for first, count, first_bank in OUT_GROUPS
+        ]
+        out_rows = out.rearrange("(u p) j -> p u j", p=P)
+
+        def weigh_values(group, u):
+            c = OUT_GROUPS[group][0] + u
+            if c >= EARLY_VAL:
+                project_e4m3(val_banks[c], c, 0, wv_mx[0], v_codes[0], v_sc[0])
+            project_e4m3(val_banks[c], c, 1, wv_mx[1], v_codes[1], v_sc[1])
+            nc.vector.tensor_tensor(
+                h_tiles[group][:, u * CHUNK : (u + 1) * CHUNK, :], by_entry(val_banks[c]), chunk_of(scores, c), MULT
+            )
+
+        def finish(group):
+            first, count, first_bank = OUT_GROUPS[group]
+            width = count * CHUNK
             h_codes = ring.tile([P, width], U32, name="h_codes", align_bytes=64)
             h_sc = ring.tile([P, width], U8, name="h_sc", align_bytes=64)
             nc.vector.quantize_mx(
-                out=h_codes[:].bitcast(FP8X4), scales=h_sc[:], in_=h[:].rearrange("p n t -> p (n t)")
+                out=h_codes[:].bitcast(FP8X4), scales=h_sc[:], in_=h_tiles[group][:].rearrange("p n t -> p (n t)")
             )
             for half in range(2):
-                bank = new_bank({0: 0, 2: 2, 4: 4, 6: 0, 7: 2}[first] + half, [P, 2, width])
+                bank = psum_bank(first_bank + half, [P, 2, width])
                 for s in range(2):
-                    u = 2 * half + s
+                    outputs = slice((2 * half + s) * P, (2 * half + s + 1) * P)
                     nc.tensor.matmul_mx(
                         out=bank[:, s, :],
-                        lhsT=wo_codes[:, u * P : (u + 1) * P].bitcast(FP8X4),
-                        lhsT_scale=wo_sc[:, 0, u * P : (u + 1) * P],
+                        lhsT=wo_codes[:, outputs].bitcast(FP8X4),
+                        lhsT_scale=wo_sc[:, 0, outputs],
                         rhs=h_codes[:].bitcast(FP8X4),
                         rhs_scale=h_sc[:],
                         start=True,
                         stop=True,
                     )
-                result = ring.tile([P, 2, width], F32, name="result", bufs=4)
+                result = keep.tile([P, 2, width], F32, name="result%d_%d" % (first, half))
+                on_vector = group == len(OUT_GROUPS) - 1 and half == 1
                 for s in range(2):
-                    u = 2 * half + s
-                    if first == 7 and half == 1:
-                        nc.vector.tensor_scalar_add(result[:, s, :], bank[:, s, :], bias[:, u : u + 1])
+                    column = bias[:, 2 * half + s : 2 * half + s + 1]
+                    if on_vector:
+                        nc.vector.tensor_scalar_add(result[:, s, :], bank[:, s, :], column)
                     else:
-                        nc.scalar.activation(result[:, s, :], bank[:, s, :], IDENTITY, bias=bias[:, u : u + 1])
+                        nc.scalar.activation(result[:, s, :], bank[:, s, :], IDENTITY, bias=column)
                 nc.sync.dma_start(
-                    out=out_rows[:, 2 * half : 2 * half + 2, first * CH : first * CH + width], in_=result[:]
+                    out=out_rows[:, 2 * half : 2 * half + 2, first * CHUNK : first * CHUNK + width], in_=result[:]
                 )
+
+        for group, (first, count, first_bank) in enumerate(OUT_GROUPS):
+            weigh_values(group, 0)
+            if group > 0:
+                finish(group - 1)
+            for u in range(1, count):
+                weigh_values(group, u)
+        finish(len(OUT_GROUPS) - 1)

@@ -27,10 +27,7 @@ CHUNK = 128
 PAIR = 2 * CHUNK
 HALF = S // 2
 CHUNKS = S // CHUNK
-EARLY_Q = 2
-EARLY_VAL = 4
-GPSIMD_STEP = 32
-WV_SPLIT = (P, 96)
+WV1_SPLIT = 64
 MOVED_ROWS = 112
 OUT_GROUPS = ((0, 2, 0), (2, 2, 2), (4, 2, 4), (6, 1, 0), (7, 1, 2))
 
@@ -95,8 +92,8 @@ def tile_list_picked_exp_scores_kernel(
         def chunk_of(pairs, c):
             return pairs[c // 2][:, (c % 2) * CHUNK : (c % 2 + 1) * CHUNK, :]
 
-        tab_sc = shared_tile("load3", [P, T], U8)
-        wk_sc_raw = shared_tile("load4", [P, PASSES, H], U8)
+        tab_sc = keep.tile([P, T], U8, name="tab_sc", align_bytes=64)
+        wk_sc_raw = keep.tile([P, PASSES, H], U8, name="wk_sc_raw", align_bytes=64)
         v_sc1 = keep.tile([P, S], U8, name="v_sc1", align_bytes=64)
         nc.gpsimd.memset(tab_sc[:].bitcast(I32), 0)
         nc.gpsimd.memset(wk_sc_raw[:].bitcast(I32), 0)
@@ -104,39 +101,42 @@ def tile_list_picked_exp_scores_kernel(
 
         tab_list = keep.tile([P, S // LIST_ROWS], U16, name="tab_list")
         nc.sync.dma_start(tab_list[:], offs)
-        head_lists = keep.tile([P, S // LIST_ROWS], U16, name="head_lists")
-        nc.sync.dma_start(head_lists[:], offs2)
-        wk_raw = shared_tile("load0", [P, PASSES, 2 * H], U8)
+        wk_raw = keep.tile([P, PASSES, 2 * H], U8, name="wk_raw", align_bytes=64)
         nc.sync.dma_start(out=wk_raw[:].bitcast(I32), in_=wk_words.rearrange("a p n -> p a n").bitcast(I32))
-        tab = [shared_tile("load1", [P, T], I32), shared_tile("load2", [P, T], I32)]
-        for a in range(PASSES):
-            nc.sync.dma_start(out=tab[a][:], in_=tab_words[a].rearrange("p t i -> p (t i)").bitcast(I32))
-        weights = shared_tile("weights", [P, S], F32)
-        nc.sync.dma_start(out=weights[:], in_=wgt)
         for quad in range(P // QUADRANT):
             nc.sync.dma_start(
                 out=tab_sc[QUADRANT * quad : QUADRANT * quad + 4 * PASSES, :].bitcast(I32),
                 in_=tab_scales[:, 4 * quad : 4 * quad + 4, :].bitcast(I32),
             )
+        tab = [shared_tile("big0", [P, T], I32), shared_tile("big1", [P, T], I32)]
+        nc.sync.dma_start(out=tab[0][:], in_=tab_words[0].rearrange("p t i -> p (t i)").bitcast(I32))
+        load_scales_side_by_side(wk_sc_raw, wk_scales)
+        nc.sync.dma_start(out=tab[1][:], in_=tab_words[1].rearrange("p t i -> p (t i)").bitcast(I32))
+        head_lists = keep.tile([P, S // LIST_ROWS], U16, name="head_lists")
+        nc.sync.dma_start(head_lists[:], offs2)
+        weights = shared_tile("weights", [P, S], F32)
+        nc.sync.dma_start(out=weights[:], in_=wgt)
+        planes0 = [load_plane(0, 0, "big2")]
+        planes0.extend(load_plane(0, i, "big%d" % (2 + i)) for i in range(1, PACK))
+        planes1 = [load_plane(1, 0, "big6"), load_plane(1, 1, "big7")]
+        wq_raw = [load_weight(wq, 0, "big8")]
 
+        v_codes = [keep.tile([P, S], U32, name="v_codes%d" % a, align_bytes=64) for a in range(PASSES)]
+        v_sc0 = keep.tile([P, S], U8, name="v_sc0", align_bytes=64)
         wk_codes = shared_tile("wk_then_xg", [P, PASSES, PACK, 2 * P], U8)
         nc.vector.tensor_copy(
             out=wk_codes[:].bitcast(U16),
             in_=wk_raw[:].bitcast(U16).rearrange("p a (m t) -> p a t m", t=PACK),
         )
-        planes0 = [load_plane(0, 0, "load0")]
-        load_scales_side_by_side(wk_sc_raw, wk_scales)
-        v_codes = [keep.tile([P, S], U32, name="v_codes%d" % a, align_bytes=64) for a in range(PASSES)]
-        for a in range(PASSES):
-            nc.vector.tensor_copy(v_codes[a][:], tab[a][:].bitcast(U32).indirect(tab_list[:]))
-            planes0.append(load_plane(0, 1 + a, "load%d" % (1 + a)))
-        v_sc0 = keep.tile([P, S], U8, name="v_sc0", align_bytes=64)
         nc.vector.tensor_copy(v_sc0[:], tab_sc[:].indirect(tab_list[:]))
         nc.scalar.dma_start(out=v_sc1[0:MOVED_ROWS, :].bitcast(I32), in_=v_sc0[4 : 4 + MOVED_ROWS, :].bitcast(I32))
         v_sc = [v_sc0, v_sc1]
-        planes0.append(load_plane(0, 3, "load3"))
+        nc.vector.tensor_copy(v_codes[0][:], tab[0][:].bitcast(U32).indirect(tab_list[:]))
+        planes1.append(load_plane(1, 2, "big0"))
         wk_sc = keep.tile([P, PASSES, PACK, P], U8, name="wk_sc", align_bytes=64)
         nc.vector.tensor_copy(out=wk_sc[:], in_=wk_sc_raw[:].rearrange("p a (m t) -> p a t m", t=PACK))
+        nc.vector.tensor_copy(v_codes[1][:], tab[1][:].bitcast(U32).indirect(tab_list[:]))
+        planes1.append(load_plane(1, 3, "big1"))
 
         keys = [keep.tile([P, PAIR, PACK], F32, name="keys%d" % g) for g in range(S // PAIR)]
         for c in range(CHUNKS):
@@ -157,28 +157,20 @@ def tile_list_picked_exp_scores_kernel(
                 in_=picked_pass[:, :, lo:hi].rearrange("p i (c n) -> p c i n", n=4),
             )
 
-        def deal_wq(raw, name):
-            dealt = shared_tile(name, [P, PACK, P, PACK], BF16)
-            nc.scalar.copy(
-                out=dealt[:].rearrange("p t m j -> p m j t"), in_=raw[:].rearrange("p j (m t) -> p m j t", t=PACK)
-            )
-            return dealt
-
-        def deal_wv(raw, name, split):
-            dealt = shared_tile(name, [P, PACK, P, PACK], BF16)
-            src = raw[:].rearrange("p j (m t) -> p m t j", t=PACK)
-            dst = dealt[:].rearrange("p t m j -> p m t j")
-            for m0 in range(0, split, GPSIMD_STEP):
-                ms = slice(m0, m0 + GPSIMD_STEP)
-                nc.gpsimd.tensor_scalar(dst[:, ms], src[:, ms], 1.0, 0.0, MULT, ADD)
+        def deal(raw, dealt, split):
+            src = raw[:].rearrange("p j (m t) -> p m j t", t=PACK)
+            dst = dealt.rearrange("p t m j -> p m j t")
+            if split > 0:
+                nc.scalar.copy(out=dst[:, :split], in_=src[:, :split])
             if split < P:
                 nc.vector.tensor_copy(dst[:, split:], src[:, split:])
             return dealt
 
-        def quantize_weight(dealt, codes, name):
-            scales = keep.tile([P, H], U8, name=name, align_bytes=64)
+        def quantize_weight(dealt, name, place):
+            codes = shared_tile(place, [P, H], U32)
+            scales = keep.tile([P, H], U8, name=name + "_sc", align_bytes=64)
             nc.vector.quantize_mx(
-                out=codes.bitcast(FP8X4), scales=scales[:], in_=dealt[:].rearrange("p t m j -> p (t m j)")
+                out=codes[:].bitcast(FP8X4), scales=scales[:], in_=dealt.rearrange("p t m j -> p (t m j)")
             )
             return codes, scales
 
@@ -187,99 +179,90 @@ def tile_list_picked_exp_scores_kernel(
                 out=codes[:, lo:hi].bitcast(FP8X4), scales=scales[:, lo:hi], in_=woven.rearrange("p n i -> p (n i)")
             )
 
-        picked = [keep.tile([P, PACK, S], F32, name="picked%d" % a) for a in range(PASSES)]
+        picked = [shared_tile("picked%d" % a, [P, PACK, S], F32) for a in range(PASSES)]
         woven0 = shared_tile("wk_then_xg", [P, S, PACK], BF16)
+        xg_codes = [keep.tile([P, S], U32, name="xg_codes%d" % a, align_bytes=64) for a in range(PASSES)]
+        xg_sc = [keep.tile([P, S], U8, name="xg_sc%d" % a, align_bytes=64) for a in range(PASSES)]
         gather(picked[0][:, 0, :], planes0[0], 0, S)
-        wq_raw = [load_weight(wq, 0, "load0")]
+        wq_raw.append(load_weight(wq, 1, "big2"))
         gather(picked[0][:, 1, :], planes0[1], 0, S)
-        planes1 = [load_plane(1, 0, "load4"), load_plane(1, 1, "load1")]
+        wv_raw = [load_weight(wv, 0, "big3")]
         gather(picked[0][:, 2, :], planes0[2], 0, S)
-        planes1.append(load_plane(1, 2, "load2"))
+        wv_raw.append(load_weight(wv, 1, "big4"))
         gather(picked[0][:, 3, :], planes0[3], 0, S)
-        planes1.append(load_plane(1, 3, "load3"))
-        wq_dealt = [deal_wq(wq_raw[0], "wq0_then_bias")]
+        wo_codes = shared_tile("big5", [P, N], I32)
+        nc.sync.dma_start(out=wo_codes[:], in_=wo_words[0].rearrange("p c i -> p (c i)").bitcast(I32))
         for lo in range(0, S, HALF):
             interleave(picked[0], woven0[:, lo : lo + HALF, :], lo, lo + HALF)
         gather(picked[1][:, 0, :], planes1[0], 0, S)
-        wq_raw.append(load_weight(wq, 1, "load4"))
+        bias = shared_tile("big6", [P, N // P], F32)
+        with nc.allow_non_contiguous_dma(reason="one bias value a partition and tile of 128 outputs"):
+            nc.sync.dma_start(out=bias[:], in_=bo.rearrange("(u p) -> p u", p=P))
         gather(picked[1][:, 1, :], planes1[1], 0, S)
-        wv_raw = [load_weight(wv, 0, "load1")]
+        for lo in range(0, S, HALF):
+            quantize_xg(xg_codes[0], xg_sc[0], woven0[:, lo : lo + HALF, :], lo, lo + HALF)
+        wq_dealt = [deal(wq_raw[0], shared_tile("picked0", [P, PACK, P, PACK], BF16)[:], P)]
         gather(picked[1][:, 2, :], planes1[2], 0, S)
-        wv_raw.append(load_weight(wv, 1, "load2"))
+        wq_mx = [quantize_weight(wq_dealt[0], "wq0", "big0")]
         for lo in range(0, S, PAIR):
             gather(picked[1][:, 3, :], planes1[3], lo, lo + PAIR)
         wo_sc = shared_tile("weights", [P, 1, N], U8)
         nc.gpsimd.memset(wo_sc[:].bitcast(I32), 0)
-
-        first_codes = shared_tile("load3", [P, S + H], U32)
-        xg_codes = [first_codes[:, 0:S], keep.tile([P, S], U32, name="xg_codes1", align_bytes=64)]
-        xg_sc = [keep.tile([P, S], U8, name="xg_sc%d" % a, align_bytes=64) for a in range(PASSES)]
-        quantize_xg(xg_codes[0], xg_sc[0], woven0[:, 0:HALF, :], 0, HALF)
-        wq_mx = [quantize_weight(wq_dealt[0], first_codes[:, S : S + H], "wq_sc0")]
-        quantize_xg(xg_codes[0], xg_sc[0], woven0[:, HALF:S, :], HALF, S)
+        load_scales_side_by_side(wo_sc, wo_scales)
         q_banks = [psum_bank(c, [P, PACK, CHUNK]) for c in range(CHUNKS)]
-        for c in range(EARLY_Q):
+        for c in range(CHUNKS):
             project_e4m3(q_banks[c], c, 0, wq_mx[0], xg_codes[0], xg_sc[0])
 
-        woven1 = [shared_tile("xg_then_wo", [P, PAIR, PACK], BF16)]
-        interleave(picked[1], woven1[0][:], 0, PAIR)
-        wq_dealt.append(deal_wq(wq_raw[1], "wq1_wv0_product"))
-        woven_rest = shared_tile("load4", [P, S - PAIR, PACK], BF16)
-        woven1.extend(woven_rest[:, lo : lo + PAIR, :] for lo in range(0, S - PAIR, PAIR))
-        wq1_codes = keep.tile([P, H], U32, name="wq1_codes", align_bytes=64)
-        wq_mx.append(quantize_weight(wq_dealt[1], wq1_codes[:], "wq_sc1"))
-
-        bias = shared_tile("wq0_then_bias", [P, N // P], F32)
-        with nc.allow_non_contiguous_dma(reason="one bias value a partition and tile of 128 outputs"):
-            nc.sync.dma_start(out=bias[:], in_=bo.rearrange("(u p) -> p u", p=P))
-        load_scales_side_by_side(wo_sc, wo_scales)
+        woven1 = [keep.tile([P, PAIR, PACK], BF16, name="woven1_%d" % g, align_bytes=64) for g in range(S // PAIR)]
+        for g in range(S // PAIR):
+            interleave(picked[1], woven1[g][:], g * PAIR, (g + 1) * PAIR)
+        wq1_dealt = keep.tile([P, PACK, P, PACK], BF16, name="wq1_dealt", align_bytes=64)
+        wq_dealt.append(deal(wq_raw[1], wq1_dealt[:], 0))
         quantize_xg(xg_codes[1], xg_sc[1], woven1[0][:], 0, PAIR)
-        wo_codes = shared_tile("xg_then_wo", [P, N], I32)
-        nc.sync.dma_start(out=wo_codes[:], in_=wo_words[0].rearrange("p c i -> p (c i)").bitcast(I32))
+        wq_mx.append(quantize_weight(wq_dealt[1], "wq1", "wq1_codes"))
         for g in range(1, S // PAIR):
-            interleave(picked[1], woven1[g], g * PAIR, (g + 1) * PAIR)
-            quantize_xg(xg_codes[1], xg_sc[1], woven1[g], g * PAIR, (g + 1) * PAIR)
+            quantize_xg(xg_codes[1], xg_sc[1], woven1[g][:], g * PAIR, (g + 1) * PAIR)
+        wv_both = shared_tile("picked1", [P, PASSES, PACK * P * PACK], BF16)
+        wv_views = [wv_both[:, a, :].rearrange("p (t m j) -> p t m j", t=PACK, j=PACK) for a in range(PASSES)]
+        wv_dealt = [deal(wv_raw[0], wv_views[0], P)]
 
-        def prepare_wv(a, name):
-            dealt = deal_wv(wv_raw[a], name, WV_SPLIT[a])
-            codes = keep.tile([P, H], U32, name="wv_codes%d" % a, align_bytes=64)
-            return quantize_weight(dealt, codes[:], "wv_sc%d" % a)
+        products = [shared_tile(("big7", "big1")[u], [P, 2 * PAIR * PACK], F32) for u in range(2)]
 
-        def score_pair(g, name):
-            product = shared_tile(name, [P, PAIR, PACK], F32)
+        def score_pair(g):
+            product = products[g // 2][:, (g % 2) * PAIR * PACK : (g % 2 + 1) * PAIR * PACK]
+            product = product.rearrange("p (n t) -> p n t", t=PACK)
             for u in range(2):
                 c = 2 * g + u
-                if c < EARLY_Q:
-                    project_e4m3(q_banks[c], c, 1, wq_mx[1], xg_codes[1], xg_sc[1])
-                else:
-                    project_e4m3(q_banks[c], c, 0, wq_mx[1], xg_codes[1], xg_sc[1])
-                    project_e4m3(q_banks[c], c, 1, wq_mx[0], xg_codes[0], xg_sc[0])
+                project_e4m3(q_banks[c], c, 1, wq_mx[1], xg_codes[1], xg_sc[1])
                 nc.vector.tensor_tensor(
                     product[:, u * CHUNK : (u + 1) * CHUNK, :], by_entry(q_banks[c]), chunk_of(keys, c), MULT
                 )
-            nc.scalar.activation(keys[g][:], product[:], EXP)
+            return product
 
-        score_pair(0, "product0")
-        score_pair(1, "product1")
-        wv_mx = [prepare_wv(0, "wq1_wv0_product")]
-        score_pair(2, "wq1_wv0_product")
-        score_pair(3, "product3")
-        wv_mx.append(prepare_wv(1, "wv1"))
+        def exponential(g, product):
+            nc.scalar.activation(keys[g][:], product, EXP)
+
+        made = [score_pair(0), score_pair(1), score_pair(2)]
+        wv_mx = [quantize_weight(wv_dealt[0], "wv0", "wv0_codes")]
+        made.append(score_pair(3))
+        wv_dealt.append(deal(wv_raw[1], wv_views[1], WV1_SPLIT))
+        for g in range(S // PAIR):
+            exponential(g, made[g])
+        wv_mx.append(quantize_weight(wv_dealt[1], "wv1", "wv1_codes"))
         scores = keys
 
         val_banks = [psum_bank(c, [P, PACK, CHUNK]) for c in range(CHUNKS)]
-        for c in range(EARLY_VAL):
+        for c in range(CHUNKS):
             project_e4m3(val_banks[c], c, 0, wv_mx[0], v_codes[0], v_sc[0])
         h_tiles = [
             keep.tile([P, count * CHUNK, PACK], BF16, name="h%d" % first, align_bytes=64)
             for first, count, first_bank in OUT_GROUPS
         ]
         out_rows = out.rearrange("(u p) j -> p u j", p=P)
+        results = [shared_tile("big8", [P, 2, S], F32), shared_tile("big2", [P, 2, S], F32)]
 
         def weigh_values(group, u):
             c = OUT_GROUPS[group][0] + u
-            if c >= EARLY_VAL:
-                project_e4m3(val_banks[c], c, 0, wv_mx[0], v_codes[0], v_sc[0])
             project_e4m3(val_banks[c], c, 1, wv_mx[1], v_codes[1], v_sc[1])
             nc.vector.tensor_tensor(
                 h_tiles[group][:, u * CHUNK : (u + 1) * CHUNK, :], by_entry(val_banks[c]), chunk_of(scores, c), MULT
@@ -288,6 +271,7 @@ def tile_list_picked_exp_scores_kernel(
         def finish(group):
             first, count, first_bank = OUT_GROUPS[group]
             width = count * CHUNK
+            entries = slice(first * CHUNK, first * CHUNK + width)
             h_codes = ring.tile([P, width], U32, name="h_codes", align_bytes=64)
             h_sc = ring.tile([P, width], U8, name="h_sc", align_bytes=64)
             nc.vector.quantize_mx(
@@ -306,17 +290,15 @@ def tile_list_picked_exp_scores_kernel(
                         start=True,
                         stop=True,
                     )
-                result = keep.tile([P, 2, width], F32, name="result%d_%d" % (first, half))
+                result = results[half]
                 on_vector = group == len(OUT_GROUPS) - 1 and half == 1
                 for s in range(2):
                     column = bias[:, 2 * half + s : 2 * half + s + 1]
                     if on_vector:
-                        nc.vector.tensor_scalar_add(result[:, s, :], bank[:, s, :], column)
+                        nc.vector.tensor_scalar_add(result[:, s, entries], bank[:, s, :], column)
                     else:
-                        nc.scalar.activation(result[:, s, :], bank[:, s, :], IDENTITY, bias=column)
-                nc.sync.dma_start(
-                    out=out_rows[:, 2 * half : 2 * half + 2, first * CHUNK : first * CHUNK + width], in_=result[:]
-                )
+                        nc.scalar.activation(result[:, s, entries], bank[:, s, :], IDENTITY, bias=column)
+                nc.sync.dma_start(out=out_rows[:, 2 * half : 2 * half + 2, entries], in_=result[:, :, entries])
 
         for group, (first, count, first_bank) in enumerate(OUT_GROUPS):
             weigh_values(group, 0)

@@ -86,11 +86,11 @@ def tile_list_picked_exp_scores_kernel(
                 a_codes, a_scales,
             )
 
-        def by_entry(bank):
-            return bank[:].rearrange("p t n -> p n t")
+        def by_two_entries(values):
+            return values.rearrange("p t (c n) -> p c t n", n=2)
 
         def chunk_of(pairs, c):
-            return pairs[c // 2][:, (c % 2) * CHUNK : (c % 2 + 1) * CHUNK, :]
+            return pairs[c // 2][:, c % 2, :, :]
 
         tab_sc = keep.tile([P, T], U8, name="tab_sc", align_bytes=64)
         wk_sc_raw = keep.tile([P, PASSES, H], U8, name="wk_sc_raw", align_bytes=64)
@@ -138,14 +138,14 @@ def tile_list_picked_exp_scores_kernel(
         nc.vector.tensor_copy(v_codes[1][:], tab[1][:].bitcast(U32).indirect(tab_list[:]))
         planes1.append(load_plane(1, 3, "big1"))
 
-        keys = [keep.tile([P, PAIR, PACK], F32, name="keys%d" % g) for g in range(S // PAIR)]
+        keys = [keep.tile([P, 2, PACK, CHUNK], F32, name="keys%d" % g) for g in range(S // PAIR)]
         for c in range(CHUNKS):
             bank = psum_bank(c, [P, PACK, CHUNK])
             for nth, a in enumerate((1, 0)):
                 project(
                     bank, c, nth, lambda t: wk_codes[:, a, t, :], lambda t: wk_sc[:, a, t, :], FP4X4, v_codes[a], v_sc[a]
                 )
-            nc.scalar.copy(out=chunk_of(keys, c), in_=by_entry(bank))
+            nc.scalar.copy(out=chunk_of(keys, c), in_=bank[:])
 
         def gather(dst, plane, lo, hi):
             lists = head_lists[:, lo // LIST_ROWS : hi // LIST_ROWS]
@@ -230,13 +230,11 @@ def tile_list_picked_exp_scores_kernel(
 
         def score_pair(g):
             product = products[g // 2][:, (g % 2) * PAIR * PACK : (g % 2 + 1) * PAIR * PACK]
-            product = product.rearrange("p (n t) -> p n t", t=PACK)
+            product = product.rearrange("p (u t n) -> p u t n", u=2, t=PACK)
             for u in range(2):
                 c = 2 * g + u
                 project_e4m3(q_banks[c], c, 1, wq_mx[1], xg_codes[1], xg_sc[1])
-                nc.vector.tensor_tensor(
-                    product[:, u * CHUNK : (u + 1) * CHUNK, :], by_entry(q_banks[c]), chunk_of(keys, c), MULT
-                )
+                nc.vector.tensor_tensor(product[:, u], q_banks[c][:], chunk_of(keys, c), MULT)
             return product
 
         def exponential(g, product):
@@ -264,9 +262,8 @@ def tile_list_picked_exp_scores_kernel(
         def weigh_values(group, u):
             c = OUT_GROUPS[group][0] + u
             project_e4m3(val_banks[c], c, 1, wv_mx[1], v_codes[1], v_sc[1])
-            nc.vector.tensor_tensor(
-                h_tiles[group][:, u * CHUNK : (u + 1) * CHUNK, :], by_entry(val_banks[c]), chunk_of(scores, c), MULT
-            )
+            woven = h_tiles[group][:, u * CHUNK : (u + 1) * CHUNK, :].rearrange("p (c n) t -> p c t n", n=2)
+            nc.vector.tensor_tensor(woven, by_two_entries(val_banks[c][:]), by_two_entries(chunk_of(scores, c)), MULT)
 
         def finish(group):
             first, count, first_bank = OUT_GROUPS[group]

@@ -1,6 +1,7 @@
 from contextlib import ExitStack
 
 import concourse.mybir as mybir
+from concourse.masks import make_identity
 
 K, M, T, S, H, N = 1024, 1024, 2048, 1024, 512, 512
 FLOPS = 2 * S * (K * H + 2 * M * H + H * N)
@@ -14,7 +15,6 @@ U8 = mybir.dt.uint8
 FP8X4 = mybir.dt.float8_e4m3fn_x4
 FP4X4 = mybir.dt.float4_e2m1fn_x4
 MULT = mybir.AluOpType.mult
-ADD = mybir.AluOpType.add
 EXP = mybir.ActivationFunctionType.Exp
 IDENTITY = mybir.ActivationFunctionType.Identity
 
@@ -27,7 +27,7 @@ CHUNK = 128
 PAIR = 2 * CHUNK
 HALF = S // 2
 CHUNKS = S // CHUNK
-WV1_SPLIT = 64
+EARLY_VAL = 6
 MOVED_ROWS = 112
 OUT_GROUPS = ((0, 2, 0), (2, 2, 2), (4, 2, 4), (6, 1, 0), (7, 1, 2))
 
@@ -48,11 +48,16 @@ def tile_list_picked_exp_scores_kernel(
         def psum_bank(index, shape):
             return psum.tile(shape, F32, name="bank%d" % index)
 
-        def load_scales_side_by_side(tile, rows):
-            for quad in range(P // QUADRANT):
+        def load_scale_quadrant(tile, rows, quad):
+            nc.sync.dma_start(
+                out=tile[QUADRANT * quad : QUADRANT * quad + 4, :, :].bitcast(I32),
+                in_=rows[:, 4 * quad : 4 * quad + 4, :].rearrange("a r n -> r a n").bitcast(I32),
+            )
+
+        def load_table_scales(r):
+            for a in range(PASSES):
                 nc.sync.dma_start(
-                    out=tile[QUADRANT * quad : QUADRANT * quad + 4, :, :].bitcast(I32),
-                    in_=rows[:, 4 * quad : 4 * quad + 4, :].rearrange("a r n -> r a n").bitcast(I32),
+                    out=tab_sc[4 * a + r : P : QUADRANT, :].bitcast(I32), in_=tab_scales[a, r:16:4, :].bitcast(I32)
                 )
 
         def load_plane(a, i, name):
@@ -89,67 +94,93 @@ def tile_list_picked_exp_scores_kernel(
         def by_two_entries(values):
             return values.rearrange("p t (c n) -> p c t n", n=2)
 
-        def chunk_of(pairs, c):
-            return pairs[c // 2][:, c % 2, :, :]
-
         tab_sc = keep.tile([P, T], U8, name="tab_sc", align_bytes=64)
         wk_sc_raw = keep.tile([P, PASSES, H], U8, name="wk_sc_raw", align_bytes=64)
         v_sc1 = keep.tile([P, S], U8, name="v_sc1", align_bytes=64)
         nc.gpsimd.memset(tab_sc[:].bitcast(I32), 0)
-        nc.gpsimd.memset(wk_sc_raw[:].bitcast(I32), 0)
-        nc.gpsimd.memset(v_sc1[:].bitcast(I32), 0)
+        nc.vector.memset(wk_sc_raw[:].bitcast(I32), 0)
+        nc.vector.memset(v_sc1[:].bitcast(I32), 0)
+        identity = keep.tile([P, P], F32, name="identity")
+        make_identity(nc, identity[:])
 
         tab_list = keep.tile([P, S // LIST_ROWS], U16, name="tab_list")
         nc.sync.dma_start(tab_list[:], offs)
-        wk_raw = keep.tile([P, PASSES, 2 * H], U8, name="wk_raw", align_bytes=64)
-        nc.sync.dma_start(out=wk_raw[:].bitcast(I32), in_=wk_words.rearrange("a p n -> p a n").bitcast(I32))
-        for quad in range(P // QUADRANT):
-            nc.sync.dma_start(
-                out=tab_sc[QUADRANT * quad : QUADRANT * quad + 4 * PASSES, :].bitcast(I32),
-                in_=tab_scales[:, 4 * quad : 4 * quad + 4, :].bitcast(I32),
-            )
+        wgt_parts = keep.tile([P, CHUNK], F32, name="wgt_parts")
+        nc.sync.dma_start(
+            out=wgt_parts[:],
+            in_=wgt.rearrange("(b u) (v x) -> b (u v) x", u=CHUNKS, v=CHUNKS)[:, 0 : CHUNKS * CHUNKS : CHUNKS + 1, :],
+        )
         tab = [shared_tile("big0", [P, T], I32), shared_tile("big1", [P, T], I32)]
-        nc.sync.dma_start(out=tab[0][:], in_=tab_words[0].rearrange("p t i -> p (t i)").bitcast(I32))
-        load_scales_side_by_side(wk_sc_raw, wk_scales)
-        nc.sync.dma_start(out=tab[1][:], in_=tab_words[1].rearrange("p t i -> p (t i)").bitcast(I32))
+        for a in range(PASSES):
+            nc.sync.dma_start(out=tab[a][:], in_=tab_words[a].rearrange("p t i -> p (t i)").bitcast(I32))
+            load_table_scales(a)
         head_lists = keep.tile([P, S // LIST_ROWS], U16, name="head_lists")
         nc.sync.dma_start(head_lists[:], offs2)
+        load_table_scales(2)
+        planes = {(0, 0): load_plane(0, 0, "big2")}
+        load_table_scales(3)
+        wk_raw = keep.tile([P, PASSES, 2 * H], U8, name="wk_raw", align_bytes=64)
+        nc.sync.dma_start(out=wk_raw[:].bitcast(I32), in_=wk_words.rearrange("a p n -> p a n").bitcast(I32))
+        for i in (1, 2):
+            for quad in (2 * i - 2, 2 * i - 1):
+                load_scale_quadrant(wk_sc_raw, wk_scales, quad)
+            planes[0, i] = load_plane(0, i, "big%d" % (2 + i))
+        planes[0, 3] = load_plane(0, 3, "big5")
+        planes[1, 0] = load_plane(1, 0, "big6")
+        planes[1, 1] = load_plane(1, 1, "big7")
+
+        turned = psum_bank(0, [P, P])
+        nc.tensor.transpose(turned[:], wgt_parts[:], identity[:])
+        spread = shared_tile("woven0", [P, CHUNKS, P], F32)
+        nc.scalar.copy(
+            out=spread[:].rearrange("x u (b c) -> x u b c", c=CHUNKS),
+            in_=turned[:].rearrange("x (b u) -> x u b", u=CHUNKS).unsqueeze(3).to_broadcast([P, CHUNKS, 16, CHUNKS]),
+        )
         weights = shared_tile("weights", [P, S], F32)
-        nc.sync.dma_start(out=weights[:], in_=wgt)
-        planes0 = [load_plane(0, 0, "big2")]
-        planes0.extend(load_plane(0, i, "big%d" % (2 + i)) for i in range(1, PACK))
-        planes1 = [load_plane(1, 0, "big6"), load_plane(1, 1, "big7")]
-        wq_raw = [load_weight(wq, 0, "big8")]
+        for half in range(2):
+            back = psum_bank(1 + half, [P, PACK, CHUNK])
+            for u in range(PACK):
+                nc.tensor.transpose(back[:, u, :], spread[:, PACK * half + u, :], identity[:])
+            nc.scalar.copy(out=weights[:, half * HALF : (half + 1) * HALF], in_=back[:].rearrange("p u x -> p (u x)"))
 
         v_codes = [keep.tile([P, S], U32, name="v_codes%d" % a, align_bytes=64) for a in range(PASSES)]
+        for a in range(PASSES):
+            nc.vector.tensor_copy(v_codes[a][:], tab[a][:].bitcast(U32).indirect(tab_list[:]))
+            planes[1, 2 + a] = load_plane(1, 2 + a, "big%d" % a)
+
+        def gather(dst, plane, lo, hi):
+            lists = head_lists[:, lo // LIST_ROWS : hi // LIST_ROWS]
+            nc.vector.tensor_tensor(dst[:, lo:hi], plane[:].indirect(lists), weights[:, lo:hi], MULT)
+
+        picked = [shared_tile("picked%d" % a, [P, PACK, S], F32) for a in range(PASSES)]
+        gather(picked[0][:, 0, :], planes[0, 0], 0, S)
+        wq_raw = [load_weight(wq, 0, "big2")]
         v_sc0 = keep.tile([P, S], U8, name="v_sc0", align_bytes=64)
-        wk_codes = shared_tile("wk_then_xg", [P, PASSES, PACK, 2 * P], U8)
+        nc.vector.tensor_copy(v_sc0[:], tab_sc[:].indirect(tab_list[:]))
+        nc.scalar.dma_start(out=v_sc1[0:MOVED_ROWS, :].bitcast(I32), in_=v_sc0[4 : 4 + MOVED_ROWS, :].bitcast(I32))
+        v_sc = [v_sc0, v_sc1]
+        wk_codes = keep.tile([P, PASSES, PACK, 2 * P], U8, name="wk_codes", align_bytes=64)
         nc.vector.tensor_copy(
             out=wk_codes[:].bitcast(U16),
             in_=wk_raw[:].bitcast(U16).rearrange("p a (m t) -> p a t m", t=PACK),
         )
-        nc.vector.tensor_copy(v_sc0[:], tab_sc[:].indirect(tab_list[:]))
-        nc.scalar.dma_start(out=v_sc1[0:MOVED_ROWS, :].bitcast(I32), in_=v_sc0[4 : 4 + MOVED_ROWS, :].bitcast(I32))
-        v_sc = [v_sc0, v_sc1]
-        nc.vector.tensor_copy(v_codes[0][:], tab[0][:].bitcast(U32).indirect(tab_list[:]))
-        planes1.append(load_plane(1, 2, "big0"))
+        gather(picked[0][:, 1, :], planes[0, 1], 0, S)
+        wq_raw.append(load_weight(wq, 1, "big3"))
         wk_sc = keep.tile([P, PASSES, PACK, P], U8, name="wk_sc", align_bytes=64)
         nc.vector.tensor_copy(out=wk_sc[:], in_=wk_sc_raw[:].rearrange("p a (m t) -> p a t m", t=PACK))
-        nc.vector.tensor_copy(v_codes[1][:], tab[1][:].bitcast(U32).indirect(tab_list[:]))
-        planes1.append(load_plane(1, 3, "big1"))
+        gather(picked[0][:, 2, :], planes[0, 2], 0, S)
+        wv_raw = [load_weight(wv, 0, "big4")]
+        gather(picked[0][:, 3, :], planes[0, 3], 0, S)
+        wv_raw.append(load_weight(wv, 1, "big5"))
 
-        keys = [keep.tile([P, 2, PACK, CHUNK], F32, name="keys%d" % g) for g in range(S // PAIR)]
+        keys = [shared_tile("keys%d" % c, [P, PACK, CHUNK], F32) for c in range(CHUNKS)]
         for c in range(CHUNKS):
             bank = psum_bank(c, [P, PACK, CHUNK])
             for nth, a in enumerate((1, 0)):
                 project(
                     bank, c, nth, lambda t: wk_codes[:, a, t, :], lambda t: wk_sc[:, a, t, :], FP4X4, v_codes[a], v_sc[a]
                 )
-            nc.scalar.copy(out=chunk_of(keys, c), in_=bank[:])
-
-        def gather(dst, plane, lo, hi):
-            lists = head_lists[:, lo // LIST_ROWS : hi // LIST_ROWS]
-            nc.vector.tensor_tensor(dst[:, lo:hi], plane[:].indirect(lists), weights[:, lo:hi], MULT)
+            nc.scalar.copy(out=keys[c][:], in_=bank[:])
 
         def interleave(picked_pass, woven, lo, hi):
             nc.scalar.copy(
@@ -157,113 +188,107 @@ def tile_list_picked_exp_scores_kernel(
                 in_=picked_pass[:, :, lo:hi].rearrange("p i (c n) -> p c i n", n=4),
             )
 
-        def deal(raw, dealt, split):
-            src = raw[:].rearrange("p j (m t) -> p m j t", t=PACK)
-            dst = dealt.rearrange("p t m j -> p m j t")
-            if split > 0:
-                nc.scalar.copy(out=dst[:, :split], in_=src[:, :split])
-            if split < P:
-                nc.vector.tensor_copy(dst[:, split:], src[:, split:])
-            return dealt
+        def deal(engine, raw, dealt, lo, hi):
+            src = raw[:].rearrange("p j (m t) -> p m j t", t=PACK)[:, lo:hi]
+            dst = dealt.rearrange("p (t m j) -> p m j t", t=PACK, j=PACK)[:, lo:hi]
+            if engine is nc.scalar:
+                nc.scalar.copy(out=dst, in_=src)
+            else:
+                nc.vector.tensor_copy(dst, src)
 
-        def quantize_weight(dealt, name, place):
-            codes = shared_tile(place, [P, H], U32)
-            scales = keep.tile([P, H], U8, name=name + "_sc", align_bytes=64)
-            nc.vector.quantize_mx(
-                out=codes[:].bitcast(FP8X4), scales=scales[:], in_=dealt.rearrange("p t m j -> p (t m j)")
-            )
+        def quantize(codes, name, values):
+            scales = keep.tile([P, codes.shape[1]], U8, name=name, align_bytes=64)
+            nc.vector.quantize_mx(out=codes.bitcast(FP8X4), scales=scales[:], in_=values)
             return codes, scales
 
-        def quantize_xg(codes, scales, woven, lo, hi):
-            nc.vector.quantize_mx(
-                out=codes[:, lo:hi].bitcast(FP8X4), scales=scales[:, lo:hi], in_=woven.rearrange("p n i -> p (n i)")
-            )
-
-        picked = [shared_tile("picked%d" % a, [P, PACK, S], F32) for a in range(PASSES)]
-        woven0 = shared_tile("wk_then_xg", [P, S, PACK], BF16)
-        xg_codes = [keep.tile([P, S], U32, name="xg_codes%d" % a, align_bytes=64) for a in range(PASSES)]
-        xg_sc = [keep.tile([P, S], U8, name="xg_sc%d" % a, align_bytes=64) for a in range(PASSES)]
-        gather(picked[0][:, 0, :], planes0[0], 0, S)
-        wq_raw.append(load_weight(wq, 1, "big2"))
-        gather(picked[0][:, 1, :], planes0[1], 0, S)
-        wv_raw = [load_weight(wv, 0, "big3")]
-        gather(picked[0][:, 2, :], planes0[2], 0, S)
-        wv_raw.append(load_weight(wv, 1, "big4"))
-        gather(picked[0][:, 3, :], planes0[3], 0, S)
-        wo_codes = shared_tile("big5", [P, N], I32)
-        nc.sync.dma_start(out=wo_codes[:], in_=wo_words[0].rearrange("p c i -> p (c i)").bitcast(I32))
+        woven0 = shared_tile("woven0", [P, S, PACK], BF16)
         for lo in range(0, S, HALF):
             interleave(picked[0], woven0[:, lo : lo + HALF, :], lo, lo + HALF)
-        gather(picked[1][:, 0, :], planes1[0], 0, S)
-        bias = shared_tile("big6", [P, N // P], F32)
+        gather(picked[1][:, 0, :], planes[1, 0], 0, S)
+        wo_codes = shared_tile("big6", [P, N], I32)
+        nc.sync.dma_start(out=wo_codes[:], in_=wo_words[0].rearrange("p c i -> p (c i)").bitcast(I32))
+        gather(picked[1][:, 1, :], planes[1, 1], 0, S)
+        bias = shared_tile("big7", [P, N // P], F32)
         with nc.allow_non_contiguous_dma(reason="one bias value a partition and tile of 128 outputs"):
             nc.sync.dma_start(out=bias[:], in_=bo.rearrange("(u p) -> p u", p=P))
-        gather(picked[1][:, 1, :], planes1[1], 0, S)
-        for lo in range(0, S, HALF):
-            quantize_xg(xg_codes[0], xg_sc[0], woven0[:, lo : lo + HALF, :], lo, lo + HALF)
-        wq_dealt = [deal(wq_raw[0], shared_tile("picked0", [P, PACK, P, PACK], BF16)[:], P)]
-        gather(picked[1][:, 2, :], planes1[2], 0, S)
-        wq_mx = [quantize_weight(wq_dealt[0], "wq0", "big0")]
+        gather(picked[1][:, 2, :], planes[1, 2], 0, S)
+        xg0_codes = shared_tile("big0", [P, S], U32)
+        xg0 = [
+            quantize(
+                xg0_codes[:, lo : lo + HALF], "xg0_sc%d" % lo, woven0[:, lo : lo + HALF, :].rearrange("p n i -> p (n i)")
+            )
+            for lo in range(0, S, HALF)
+        ]
         for lo in range(0, S, PAIR):
-            gather(picked[1][:, 3, :], planes1[3], lo, lo + PAIR)
+            gather(picked[1][:, 3, :], planes[1, 3], lo, lo + PAIR)
         wo_sc = shared_tile("weights", [P, 1, N], U8)
         nc.gpsimd.memset(wo_sc[:].bitcast(I32), 0)
-        load_scales_side_by_side(wo_sc, wo_scales)
-        q_banks = [psum_bank(c, [P, PACK, CHUNK]) for c in range(CHUNKS)]
-        for c in range(CHUNKS):
-            project_e4m3(q_banks[c], c, 0, wq_mx[0], xg_codes[0], xg_sc[0])
+        for quad in range(P // QUADRANT):
+            load_scale_quadrant(wo_sc, wo_scales, quad)
 
         woven1 = [keep.tile([P, PAIR, PACK], BF16, name="woven1_%d" % g, align_bytes=64) for g in range(S // PAIR)]
         for g in range(S // PAIR):
             interleave(picked[1], woven1[g][:], g * PAIR, (g + 1) * PAIR)
-        wq1_dealt = keep.tile([P, PACK, P, PACK], BF16, name="wq1_dealt", align_bytes=64)
-        wq_dealt.append(deal(wq_raw[1], wq1_dealt[:], 0))
-        quantize_xg(xg_codes[1], xg_sc[1], woven1[0][:], 0, PAIR)
-        wq_mx.append(quantize_weight(wq_dealt[1], "wq1", "wq1_codes"))
-        for g in range(1, S // PAIR):
-            quantize_xg(xg_codes[1], xg_sc[1], woven1[g][:], g * PAIR, (g + 1) * PAIR)
-        wv_both = shared_tile("picked1", [P, PASSES, PACK * P * PACK], BF16)
-        wv_views = [wv_both[:, a, :].rearrange("p (t m j) -> p t m j", t=PACK, j=PACK) for a in range(PASSES)]
-        wv_dealt = [deal(wv_raw[0], wv_views[0], P)]
+        wq0_dealt = shared_tile("big1", [P, H * PACK], BF16)
+        deal(nc.vector, wq_raw[0], wq0_dealt[:], 0, P)
+        xg1_codes = keep.tile([P, S], U32, name="xg1_codes", align_bytes=64)
 
-        products = [shared_tile(("big7", "big1")[u], [P, 2 * PAIR * PACK], F32) for u in range(2)]
+        def quantize_pair(g):
+            values = woven1[g][:].rearrange("p n i -> p (n i)")
+            return quantize(xg1_codes[:, g * PAIR : (g + 1) * PAIR], "xg1_sc%d" % g, values)
 
-        def score_pair(g):
-            product = products[g // 2][:, (g % 2) * PAIR * PACK : (g % 2 + 1) * PAIR * PACK]
-            product = product.rearrange("p (u t n) -> p u t n", u=2, t=PACK)
-            for u in range(2):
-                c = 2 * g + u
-                project_e4m3(q_banks[c], c, 1, wq_mx[1], xg_codes[1], xg_sc[1])
-                nc.vector.tensor_tensor(product[:, u], q_banks[c][:], chunk_of(keys, c), MULT)
-            return product
+        xg1 = [quantize_pair(0)]
+        w_codes = keep.tile([P, PASSES + 1, H], U32, name="w_codes", align_bytes=64)
+        wq_mx = [quantize(w_codes[:, 0, :], "wq0_sc", wq0_dealt[:])]
+        xg1.extend(quantize_pair(g) for g in range(1, S // PAIR))
+        q_banks = [psum_bank(c, [P, PACK, CHUNK]) for c in range(CHUNKS)]
+        for c in range(CHUNKS):
+            project_e4m3(q_banks[c], c % PACK, 0, wq_mx[0], *xg0[c // PACK])
 
-        def exponential(g, product):
-            nc.scalar.activation(keys[g][:], product, EXP)
+        late_dealt = shared_tile("picked1", [P, 2, H * PACK], BF16)
+        deal(nc.scalar, wq_raw[1], late_dealt[:, 0, :], 0, P // 2)
+        deal(nc.vector, wq_raw[1], late_dealt[:, 0, :], P // 2, P)
+        wq_mx.append(quantize(w_codes[:, 1, :], "wq1_sc", late_dealt[:, 0, :]))
+        deal(nc.scalar, wv_raw[0], late_dealt[:, 1, :], 0, P)
 
-        made = [score_pair(0), score_pair(1), score_pair(2)]
-        wv_mx = [quantize_weight(wv_dealt[0], "wv0", "wv0_codes")]
-        made.append(score_pair(3))
-        wv_dealt.append(deal(wv_raw[1], wv_views[1], WV1_SPLIT))
+        products = shared_tile("picked0", [P, CHUNKS, PACK, CHUNK], F32)
+
+        def score(c):
+            project_e4m3(q_banks[c], c % 2, 1, wq_mx[1], *xg1[c // 2])
+            nc.vector.tensor_tensor(products[:, c], q_banks[c][:], keys[c][:], MULT)
+
+        for c in range(CHUNKS - 2):
+            score(c)
+        wv_mx = [quantize(shared_tile("keys4", [P, H], U32)[:], "wv0_sc", late_dealt[:, 1, :])]
+        wv1_dealt = shared_tile("keys5", [P, H * PACK], BF16)
+        deal(nc.scalar, wv_raw[1], wv1_dealt[:], 0, P // 2)
+        deal(nc.vector, wv_raw[1], wv1_dealt[:], P // 2, P)
+        score(CHUNKS - 2)
+        wv_mx.append(quantize(w_codes[:, 2, :], "wv1_sc", wv1_dealt[:]))
+        score(CHUNKS - 1)
+        first_scores = shared_tile("big5", [P, PACK, PACK, CHUNK], F32)
+        scores = [first_scores[:, c] if c < PACK else products[:, c] for c in range(CHUNKS)]
         for g in range(S // PAIR):
-            exponential(g, made[g])
-        wv_mx.append(quantize_weight(wv_dealt[1], "wv1", "wv1_codes"))
-        scores = keys
+            target = first_scores if g < 2 else products
+            nc.scalar.activation(target[:, 2 * g : 2 * g + 2], products[:, 2 * g : 2 * g + 2], EXP)
 
         val_banks = [psum_bank(c, [P, PACK, CHUNK]) for c in range(CHUNKS)]
-        for c in range(CHUNKS):
+        for c in range(EARLY_VAL):
             project_e4m3(val_banks[c], c, 0, wv_mx[0], v_codes[0], v_sc[0])
         h_tiles = [
             keep.tile([P, count * CHUNK, PACK], BF16, name="h%d" % first, align_bytes=64)
             for first, count, first_bank in OUT_GROUPS
         ]
         out_rows = out.rearrange("(u p) j -> p u j", p=P)
-        results = [shared_tile("big8", [P, 2, S], F32), shared_tile("big2", [P, 2, S], F32)]
+        results = [shared_tile("big2", [P, 2, S], F32), shared_tile("big3", [P, 2, S], F32)]
 
         def weigh_values(group, u):
             c = OUT_GROUPS[group][0] + u
-            project_e4m3(val_banks[c], c, 1, wv_mx[1], v_codes[1], v_sc[1])
+            order = (1,) if c < EARLY_VAL else (1, 0)
+            for nth, a in enumerate(order):
+                project_e4m3(val_banks[c], c, PASSES - len(order) + nth, wv_mx[a], v_codes[a], v_sc[a])
             woven = h_tiles[group][:, u * CHUNK : (u + 1) * CHUNK, :].rearrange("p (c n) t -> p c t n", n=2)
-            nc.vector.tensor_tensor(woven, by_two_entries(val_banks[c][:]), by_two_entries(chunk_of(scores, c)), MULT)
+            nc.vector.tensor_tensor(woven, by_two_entries(val_banks[c][:]), by_two_entries(scores[c]), MULT)
 
         def finish(group):
             first, count, first_bank = OUT_GROUPS[group]

@@ -27,6 +27,7 @@ CHUNK = 128
 PAIR = 2 * CHUNK
 HALF = S // 2
 CHUNKS = S // CHUNK
+EARLY_Q = 4
 EARLY_VAL = 6
 MOVED_ROWS = 112
 OUT_GROUPS = ((0, 2, 0), (2, 2, 2), (4, 2, 4), (6, 1, 0), (7, 1, 2))
@@ -54,20 +55,14 @@ def tile_list_picked_exp_scores_kernel(
                 in_=rows[:, 4 * quad : 4 * quad + 4, :].rearrange("a r n -> r a n").bitcast(I32),
             )
 
-        def load_table_scales(r):
-            for a in range(PASSES):
-                nc.sync.dma_start(
-                    out=tab_sc[4 * a + r : P : QUADRANT, :].bitcast(I32), in_=tab_scales[a, r:16:4, :].bitcast(I32)
-                )
-
         def load_plane(a, i, name):
             plane = shared_tile(name, [P, T], F32)
             nc.sync.dma_start(out=plane[:], in_=xT.rearrange("(a p i) t -> a i p t", a=PASSES, i=PACK)[a, i])
             return plane
 
-        def load_weight(w, a, name):
-            raw = shared_tile(name, [P, PACK, H], F32)
-            nc.sync.dma_start(out=raw[:], in_=w.rearrange("(a p j) r -> a p j r", a=PASSES, j=PACK)[a])
+        def load_weight(w, a, name, lo=0, hi=H):
+            raw = shared_tile(name, [P, PACK, hi - lo], F32)
+            nc.sync.dma_start(out=raw[:], in_=w.rearrange("(a p j) r -> a p j r", a=PASSES, j=PACK)[a, :, :, lo:hi])
             return raw
 
         def project(bank, c, nth, w_codes, w_scales, w_dtype, a_codes, a_scales):
@@ -105,6 +100,15 @@ def tile_list_picked_exp_scores_kernel(
 
         tab_list = keep.tile([P, S // LIST_ROWS], U16, name="tab_list")
         nc.sync.dma_start(tab_list[:], offs)
+        wk_raw = keep.tile([P, PASSES, 2 * H], U8, name="wk_raw", align_bytes=64)
+        nc.sync.dma_start(out=wk_raw[:].bitcast(I32), in_=wk_words.rearrange("a p n -> p a n").bitcast(I32))
+        for quad in range(P // QUADRANT):
+            nc.sync.dma_start(
+                out=tab_sc[QUADRANT * quad : QUADRANT * quad + 4 * PASSES, :].bitcast(I32),
+                in_=tab_scales[:, 4 * quad : 4 * quad + 4, :].bitcast(I32),
+            )
+        for quad in range(P // QUADRANT):
+            load_scale_quadrant(wk_sc_raw, wk_scales, quad)
         wgt_parts = keep.tile([P, CHUNK], F32, name="wgt_parts")
         nc.sync.dma_start(
             out=wgt_parts[:],
@@ -113,19 +117,9 @@ def tile_list_picked_exp_scores_kernel(
         tab = [shared_tile("big0", [P, T], I32), shared_tile("big1", [P, T], I32)]
         for a in range(PASSES):
             nc.sync.dma_start(out=tab[a][:], in_=tab_words[a].rearrange("p t i -> p (t i)").bitcast(I32))
-            load_table_scales(a)
         head_lists = keep.tile([P, S // LIST_ROWS], U16, name="head_lists")
         nc.sync.dma_start(head_lists[:], offs2)
-        load_table_scales(2)
-        planes = {(0, 0): load_plane(0, 0, "big2")}
-        load_table_scales(3)
-        wk_raw = keep.tile([P, PASSES, 2 * H], U8, name="wk_raw", align_bytes=64)
-        nc.sync.dma_start(out=wk_raw[:].bitcast(I32), in_=wk_words.rearrange("a p n -> p a n").bitcast(I32))
-        for i in (1, 2):
-            for quad in (2 * i - 2, 2 * i - 1):
-                load_scale_quadrant(wk_sc_raw, wk_scales, quad)
-            planes[0, i] = load_plane(0, i, "big%d" % (2 + i))
-        planes[0, 3] = load_plane(0, 3, "big5")
+        planes = {(0, i): load_plane(0, i, "big%d" % (2 + i)) for i in range(PACK)}
         planes[1, 0] = load_plane(1, 0, "big6")
         planes[1, 1] = load_plane(1, 1, "big7")
 
@@ -143,10 +137,21 @@ def tile_list_picked_exp_scores_kernel(
                 nc.tensor.transpose(back[:, u, :], spread[:, PACK * half + u, :], identity[:])
             nc.scalar.copy(out=weights[:, half * HALF : (half + 1) * HALF], in_=back[:].rearrange("p u x -> p (u x)"))
 
+        wk_codes = keep.tile([P, PASSES, PACK, 2 * P], U8, name="wk_codes", align_bytes=64)
+        nc.vector.tensor_copy(
+            out=wk_codes[:].bitcast(U16),
+            in_=wk_raw[:].bitcast(U16).rearrange("p a (m t) -> p a t m", t=PACK),
+        )
+        v_sc0 = keep.tile([P, S], U8, name="v_sc0", align_bytes=64)
+        nc.vector.tensor_copy(v_sc0[:], tab_sc[:].indirect(tab_list[:]))
+        nc.scalar.dma_start(out=v_sc1[0:MOVED_ROWS, :].bitcast(I32), in_=v_sc0[4 : 4 + MOVED_ROWS, :].bitcast(I32))
+        v_sc = [v_sc0, v_sc1]
+        wk_sc = keep.tile([P, PASSES, PACK, P], U8, name="wk_sc", align_bytes=64)
+        nc.vector.tensor_copy(out=wk_sc[:], in_=wk_sc_raw[:].rearrange("p a (m t) -> p a t m", t=PACK))
         v_codes = [keep.tile([P, S], U32, name="v_codes%d" % a, align_bytes=64) for a in range(PASSES)]
         for a in range(PASSES):
             nc.vector.tensor_copy(v_codes[a][:], tab[a][:].bitcast(U32).indirect(tab_list[:]))
-            planes[1, 2 + a] = load_plane(1, 2 + a, "big%d" % a)
+        planes[1, 2] = load_plane(1, 2, "big0")
 
         def gather(dst, plane, lo, hi):
             lists = head_lists[:, lo // LIST_ROWS : hi // LIST_ROWS]
@@ -154,24 +159,14 @@ def tile_list_picked_exp_scores_kernel(
 
         picked = [shared_tile("picked%d" % a, [P, PACK, S], F32) for a in range(PASSES)]
         gather(picked[0][:, 0, :], planes[0, 0], 0, S)
-        wq_raw = [load_weight(wq, 0, "big2")]
-        v_sc0 = keep.tile([P, S], U8, name="v_sc0", align_bytes=64)
-        nc.vector.tensor_copy(v_sc0[:], tab_sc[:].indirect(tab_list[:]))
-        nc.scalar.dma_start(out=v_sc1[0:MOVED_ROWS, :].bitcast(I32), in_=v_sc0[4 : 4 + MOVED_ROWS, :].bitcast(I32))
-        v_sc = [v_sc0, v_sc1]
-        wk_codes = keep.tile([P, PASSES, PACK, 2 * P], U8, name="wk_codes", align_bytes=64)
-        nc.vector.tensor_copy(
-            out=wk_codes[:].bitcast(U16),
-            in_=wk_raw[:].bitcast(U16).rearrange("p a (m t) -> p a t m", t=PACK),
-        )
+        wq0_raw = [load_weight(wq, 0, "big2", 0, H // 2)]
+        planes[1, 3] = load_plane(1, 3, "big1")
         gather(picked[0][:, 1, :], planes[0, 1], 0, S)
-        wq_raw.append(load_weight(wq, 1, "big3"))
-        wk_sc = keep.tile([P, PASSES, PACK, P], U8, name="wk_sc", align_bytes=64)
-        nc.vector.tensor_copy(out=wk_sc[:], in_=wk_sc_raw[:].rearrange("p a (m t) -> p a t m", t=PACK))
+        wq0_raw.append(load_weight(wq, 0, "big3", H // 2, H))
         gather(picked[0][:, 2, :], planes[0, 2], 0, S)
-        wv_raw = [load_weight(wv, 0, "big4")]
+        wq1_raw = load_weight(wq, 1, "big4")
         gather(picked[0][:, 3, :], planes[0, 3], 0, S)
-        wv_raw.append(load_weight(wv, 1, "big5"))
+        wv_raw = [load_weight(wv, 0, "big5")]
 
         keys = [shared_tile("keys%d" % c, [P, PACK, CHUNK], F32) for c in range(CHUNKS)]
         for c in range(CHUNKS):
@@ -188,8 +183,8 @@ def tile_list_picked_exp_scores_kernel(
                 in_=picked_pass[:, :, lo:hi].rearrange("p i (c n) -> p c i n", n=4),
             )
 
-        def deal(engine, raw, dealt, lo, hi):
-            src = raw[:].rearrange("p j (m t) -> p m j t", t=PACK)[:, lo:hi]
+        def deal(engine, raw, dealt, lo, hi, first=0):
+            src = raw[:].rearrange("p j (m t) -> p m j t", t=PACK)[:, lo - first : hi - first]
             dst = dealt.rearrange("p (t m j) -> p m j t", t=PACK, j=PACK)[:, lo:hi]
             if engine is nc.scalar:
                 nc.scalar.copy(out=dst, in_=src)
@@ -205,13 +200,13 @@ def tile_list_picked_exp_scores_kernel(
         for lo in range(0, S, HALF):
             interleave(picked[0], woven0[:, lo : lo + HALF, :], lo, lo + HALF)
         gather(picked[1][:, 0, :], planes[1, 0], 0, S)
-        wo_codes = shared_tile("big6", [P, N], I32)
-        nc.sync.dma_start(out=wo_codes[:], in_=wo_words[0].rearrange("p c i -> p (c i)").bitcast(I32))
+        wv_raw.append(load_weight(wv, 1, "big6"))
         gather(picked[1][:, 1, :], planes[1, 1], 0, S)
-        bias = shared_tile("big7", [P, N // P], F32)
-        with nc.allow_non_contiguous_dma(reason="one bias value a partition and tile of 128 outputs"):
-            nc.sync.dma_start(out=bias[:], in_=bo.rearrange("(u p) -> p u", p=P))
+        wo_codes = shared_tile("big7", [P, N], I32)
+        nc.sync.dma_start(out=wo_codes[:], in_=wo_words[0].rearrange("p c i -> p (c i)").bitcast(I32))
         gather(picked[1][:, 2, :], planes[1, 2], 0, S)
+        wq0_dealt = keep.tile([P, H * PACK], BF16, name="wq0_dealt", align_bytes=64)
+        deal(nc.scalar, wq0_raw[0], wq0_dealt[:], 0, P // 2)
         xg0_codes = shared_tile("big0", [P, S], U32)
         xg0 = [
             quantize(
@@ -221,16 +216,21 @@ def tile_list_picked_exp_scores_kernel(
         ]
         for lo in range(0, S, PAIR):
             gather(picked[1][:, 3, :], planes[1, 3], lo, lo + PAIR)
+        bias = shared_tile("big1", [P, N // P], F32)
+        with nc.allow_non_contiguous_dma(reason="one bias value a partition and tile of 128 outputs"):
+            nc.sync.dma_start(out=bias[:], in_=bo.rearrange("(u p) -> p u", p=P))
         wo_sc = shared_tile("weights", [P, 1, N], U8)
         nc.gpsimd.memset(wo_sc[:].bitcast(I32), 0)
         for quad in range(P // QUADRANT):
             load_scale_quadrant(wo_sc, wo_scales, quad)
 
         woven1 = [keep.tile([P, PAIR, PACK], BF16, name="woven1_%d" % g, align_bytes=64) for g in range(S // PAIR)]
+        wq1_dealt = keep.tile([P, H * PACK], BF16, name="wq1_dealt", align_bytes=64)
         for g in range(S // PAIR):
+            if g == S // PAIR - 1:
+                deal(nc.scalar, wq1_raw, wq1_dealt[:], 0, P // 2)
             interleave(picked[1], woven1[g][:], g * PAIR, (g + 1) * PAIR)
-        wq0_dealt = shared_tile("big1", [P, H * PACK], BF16)
-        deal(nc.vector, wq_raw[0], wq0_dealt[:], 0, P)
+        deal(nc.vector, wq0_raw[1], wq0_dealt[:], P // 2, P, P // 2)
         xg1_codes = keep.tile([P, S], U32, name="xg1_codes", align_bytes=64)
 
         def quantize_pair(g):
@@ -238,35 +238,36 @@ def tile_list_picked_exp_scores_kernel(
             return quantize(xg1_codes[:, g * PAIR : (g + 1) * PAIR], "xg1_sc%d" % g, values)
 
         xg1 = [quantize_pair(0)]
-        w_codes = keep.tile([P, PASSES + 1, H], U32, name="w_codes", align_bytes=64)
+        w_codes = keep.tile([P, PASSES, H], U32, name="w_codes", align_bytes=64)
         wq_mx = [quantize(w_codes[:, 0, :], "wq0_sc", wq0_dealt[:])]
-        xg1.extend(quantize_pair(g) for g in range(1, S // PAIR))
+        deal(nc.vector, wq1_raw, wq1_dealt[:], P // 2, P)
+        xg1.extend(quantize_pair(g) for g in (1, 2))
+        wq_mx.append(quantize(w_codes[:, 1, :], "wq1_sc", wq1_dealt[:]))
+        xg1.append(quantize_pair(3))
         q_banks = [psum_bank(c, [P, PACK, CHUNK]) for c in range(CHUNKS)]
-        for c in range(CHUNKS):
+        for c in range(EARLY_Q):
             project_e4m3(q_banks[c], c % PACK, 0, wq_mx[0], *xg0[c // PACK])
-
-        late_dealt = shared_tile("picked1", [P, 2, H * PACK], BF16)
-        deal(nc.scalar, wq_raw[1], late_dealt[:, 0, :], 0, P // 2)
-        deal(nc.vector, wq_raw[1], late_dealt[:, 0, :], P // 2, P)
-        wq_mx.append(quantize(w_codes[:, 1, :], "wq1_sc", late_dealt[:, 0, :]))
-        deal(nc.scalar, wv_raw[0], late_dealt[:, 1, :], 0, P)
+        late_dealt = shared_tile("picked1", [P, PASSES, H * PACK], BF16)
+        for a in range(PASSES):
+            deal(nc.scalar, wv_raw[a], late_dealt[:, a, :], 0, P)
 
         products = shared_tile("picked0", [P, CHUNKS, PACK, CHUNK], F32)
 
         def score(c):
-            project_e4m3(q_banks[c], c % 2, 1, wq_mx[1], *xg1[c // 2])
+            if c < EARLY_Q:
+                project_e4m3(q_banks[c], c % 2, 1, wq_mx[1], *xg1[c // 2])
+            else:
+                project_e4m3(q_banks[c], c % 2, 0, wq_mx[1], *xg1[c // 2])
+                project_e4m3(q_banks[c], c % PACK, 1, wq_mx[0], *xg0[c // PACK])
             nc.vector.tensor_tensor(products[:, c], q_banks[c][:], keys[c][:], MULT)
 
         for c in range(CHUNKS - 2):
             score(c)
-        wv_mx = [quantize(shared_tile("keys4", [P, H], U32)[:], "wv0_sc", late_dealt[:, 1, :])]
-        wv1_dealt = shared_tile("keys5", [P, H * PACK], BF16)
-        deal(nc.scalar, wv_raw[1], wv1_dealt[:], 0, P // 2)
-        deal(nc.vector, wv_raw[1], wv1_dealt[:], P // 2, P)
+        wv_mx = [quantize(shared_tile("keys4", [P, H], U32)[:], "wv0_sc", late_dealt[:, 0, :])]
         score(CHUNKS - 2)
-        wv_mx.append(quantize(w_codes[:, 2, :], "wv1_sc", wv1_dealt[:]))
+        wv_mx.append(quantize(shared_tile("keys5", [P, H], U32)[:], "wv1_sc", late_dealt[:, 1, :]))
         score(CHUNKS - 1)
-        first_scores = shared_tile("big5", [P, PACK, PACK, CHUNK], F32)
+        first_scores = shared_tile("big6", [P, PACK, PACK, CHUNK], F32)
         scores = [first_scores[:, c] if c < PACK else products[:, c] for c in range(CHUNKS)]
         for g in range(S // PAIR):
             target = first_scores if g < 2 else products

@@ -27,7 +27,6 @@ CHUNK = 128
 PAIR = 2 * CHUNK
 HALF = S // 2
 CHUNKS = S // CHUNK
-EARLY_Q = 4
 EARLY_VAL = 6
 MOVED_ROWS = 112
 OUT_GROUPS = ((0, 2, 0), (2, 2, 2), (4, 2, 4), (6, 1, 0), (7, 1, 2))
@@ -90,36 +89,43 @@ def tile_list_picked_exp_scores_kernel(
             return values.rearrange("p t (c n) -> p c t n", n=2)
 
         tab_sc = keep.tile([P, T], U8, name="tab_sc", align_bytes=64)
-        wk_sc_raw = keep.tile([P, PASSES, H], U8, name="wk_sc_raw", align_bytes=64)
+        wk_sc = keep.tile([P, PASSES, H], U8, name="wk_sc", align_bytes=64)
         v_sc1 = keep.tile([P, S], U8, name="v_sc1", align_bytes=64)
         nc.gpsimd.memset(tab_sc[:].bitcast(I32), 0)
-        nc.vector.memset(wk_sc_raw[:].bitcast(I32), 0)
+        nc.vector.memset(wk_sc[:].bitcast(I32), 0)
         nc.vector.memset(v_sc1[:].bitcast(I32), 0)
         identity = keep.tile([P, P], F32, name="identity")
         make_identity(nc, identity[:])
 
         tab_list = keep.tile([P, S // LIST_ROWS], U16, name="tab_list")
         nc.sync.dma_start(tab_list[:], offs)
-        wk_raw = keep.tile([P, PASSES, 2 * H], U8, name="wk_raw", align_bytes=64)
-        nc.sync.dma_start(out=wk_raw[:].bitcast(I32), in_=wk_words.rearrange("a p n -> p a n").bitcast(I32))
-        for quad in range(P // QUADRANT):
-            nc.sync.dma_start(
-                out=tab_sc[QUADRANT * quad : QUADRANT * quad + 4 * PASSES, :].bitcast(I32),
-                in_=tab_scales[:, 4 * quad : 4 * quad + 4, :].bitcast(I32),
-            )
-        for quad in range(P // QUADRANT):
-            load_scale_quadrant(wk_sc_raw, wk_scales, quad)
         wgt_parts = keep.tile([P, CHUNK], F32, name="wgt_parts")
         nc.sync.dma_start(
             out=wgt_parts[:],
             in_=wgt.rearrange("(b u) (v x) -> b (u v) x", u=CHUNKS, v=CHUNKS)[:, 0 : CHUNKS * CHUNKS : CHUNKS + 1, :],
         )
+        for quad in range(P // QUADRANT):
+            nc.sync.dma_start(
+                out=tab_sc[QUADRANT * quad : QUADRANT * quad + 4 * PASSES, :].bitcast(I32),
+                in_=tab_scales[:, 4 * quad : 4 * quad + 4, :].bitcast(I32),
+            )
         tab = [shared_tile("big0", [P, T], I32), shared_tile("big1", [P, T], I32)]
         for a in range(PASSES):
             nc.sync.dma_start(out=tab[a][:], in_=tab_words[a].rearrange("p t i -> p (t i)").bitcast(I32))
         head_lists = keep.tile([P, S // LIST_ROWS], U16, name="head_lists")
         nc.sync.dma_start(head_lists[:], offs2)
-        planes = {(0, i): load_plane(0, i, "big%d" % (2 + i)) for i in range(PACK)}
+        planes = {(0, 0): load_plane(0, 0, "big2")}
+        v_sc0 = keep.tile([P, S], U8, name="v_sc0", align_bytes=64)
+        nc.vector.tensor_copy(v_sc0[:], tab_sc[:].indirect(tab_list[:]))
+        nc.sync.dma_start(out=v_sc1[0:MOVED_ROWS, :].bitcast(I32), in_=v_sc0[4 : 4 + MOVED_ROWS, :].bitcast(I32))
+        v_sc = [v_sc0, v_sc1]
+        for quad in range(P // QUADRANT):
+            load_scale_quadrant(wk_sc, wk_scales, quad)
+        wk_codes = keep.tile([P, PASSES, 2 * H], U8, name="wk_codes", align_bytes=64)
+        nc.sync.dma_start(out=wk_codes[:].bitcast(I32), in_=wk_words.rearrange("a p n -> p a n").bitcast(I32))
+        planes[0, 1] = load_plane(0, 1, "big3")
+        for i in (2, 3):
+            planes[0, i] = load_plane(0, i, "big%d" % (2 + i))
         planes[1, 0] = load_plane(1, 0, "big6")
         planes[1, 1] = load_plane(1, 1, "big7")
 
@@ -137,17 +143,6 @@ def tile_list_picked_exp_scores_kernel(
                 nc.tensor.transpose(back[:, u, :], spread[:, PACK * half + u, :], identity[:])
             nc.scalar.copy(out=weights[:, half * HALF : (half + 1) * HALF], in_=back[:].rearrange("p u x -> p (u x)"))
 
-        wk_codes = keep.tile([P, PASSES, PACK, 2 * P], U8, name="wk_codes", align_bytes=64)
-        nc.vector.tensor_copy(
-            out=wk_codes[:].bitcast(U16),
-            in_=wk_raw[:].bitcast(U16).rearrange("p a (m t) -> p a t m", t=PACK),
-        )
-        v_sc0 = keep.tile([P, S], U8, name="v_sc0", align_bytes=64)
-        nc.vector.tensor_copy(v_sc0[:], tab_sc[:].indirect(tab_list[:]))
-        nc.scalar.dma_start(out=v_sc1[0:MOVED_ROWS, :].bitcast(I32), in_=v_sc0[4 : 4 + MOVED_ROWS, :].bitcast(I32))
-        v_sc = [v_sc0, v_sc1]
-        wk_sc = keep.tile([P, PASSES, PACK, P], U8, name="wk_sc", align_bytes=64)
-        nc.vector.tensor_copy(out=wk_sc[:], in_=wk_sc_raw[:].rearrange("p a (m t) -> p a t m", t=PACK))
         v_codes = [keep.tile([P, S], U32, name="v_codes%d" % a, align_bytes=64) for a in range(PASSES)]
         for a in range(PASSES):
             nc.vector.tensor_copy(v_codes[a][:], tab[a][:].bitcast(U32).indirect(tab_list[:]))
@@ -159,23 +154,35 @@ def tile_list_picked_exp_scores_kernel(
 
         picked = [shared_tile("picked%d" % a, [P, PACK, S], F32) for a in range(PASSES)]
         gather(picked[0][:, 0, :], planes[0, 0], 0, S)
-        wq0_raw = [load_weight(wq, 0, "big2", 0, H // 2)]
-        planes[1, 3] = load_plane(1, 3, "big1")
+        wq0_raw = load_weight(wq, 0, "big2")
         gather(picked[0][:, 1, :], planes[0, 1], 0, S)
-        wq0_raw.append(load_weight(wq, 0, "big3", H // 2, H))
+        wq1_raw = [load_weight(wq, 1, "big3", 0, H // 2)]
+        planes[1, 3] = load_plane(1, 3, "big1")
         gather(picked[0][:, 2, :], planes[0, 2], 0, S)
-        wq1_raw = load_weight(wq, 1, "big4")
+        wq1_raw.append(load_weight(wq, 1, "big4", H // 2, H))
         gather(picked[0][:, 3, :], planes[0, 3], 0, S)
         wv_raw = [load_weight(wv, 0, "big5")]
 
         keys = [shared_tile("keys%d" % c, [P, PACK, CHUNK], F32) for c in range(CHUNKS)]
         for c in range(CHUNKS):
-            bank = psum_bank(c, [P, PACK, CHUNK])
+            entries = slice(c * CHUNK, (c + 1) * CHUNK)
+            by_entry = psum_bank(c % PACK, [P, H])
             for nth, a in enumerate((1, 0)):
-                project(
-                    bank, c, nth, lambda t: wk_codes[:, a, t, :], lambda t: wk_sc[:, a, t, :], FP4X4, v_codes[a], v_sc[a]
+                nc.tensor.matmul_mx(
+                    out=by_entry[:],
+                    lhsT=v_codes[a][:, entries].bitcast(FP8X4),
+                    lhsT_scale=v_sc[a][:, entries],
+                    rhs=wk_codes[:, a, :].bitcast(FP4X4),
+                    rhs_scale=wk_sc[:, a, :],
+                    start=(nth == 0),
+                    stop=(nth == PASSES - 1),
                 )
-            nc.scalar.copy(out=keys[c][:], in_=bank[:])
+            dealt = ring.tile([P, PACK, P], F32, name="keys_by_entry")
+            nc.scalar.copy(out=dealt[:], in_=by_entry[:].rearrange("j (m t) -> j t m", t=PACK))
+            by_channel = psum_bank(PACK + c % PACK, [P, PACK, CHUNK])
+            for t in range(PACK):
+                nc.tensor.transpose(by_channel[:, t, :], dealt[:, t, :], identity[:])
+            nc.scalar.copy(out=keys[c][:], in_=by_channel[:])
 
         def interleave(picked_pass, woven, lo, hi):
             nc.scalar.copy(
@@ -205,15 +212,18 @@ def tile_list_picked_exp_scores_kernel(
         wo_codes = shared_tile("big7", [P, N], I32)
         nc.sync.dma_start(out=wo_codes[:], in_=wo_words[0].rearrange("p c i -> p (c i)").bitcast(I32))
         gather(picked[1][:, 2, :], planes[1, 2], 0, S)
-        wq0_dealt = keep.tile([P, H * PACK], BF16, name="wq0_dealt", align_bytes=64)
-        deal(nc.scalar, wq0_raw[0], wq0_dealt[:], 0, P // 2)
-        xg0_codes = shared_tile("big0", [P, S], U32)
+        wq_dealt = shared_tile("picked0", [P, PASSES, H * PACK], BF16)
+        deal(nc.scalar, wq0_raw, wq_dealt[:, 0, :], 0, P)
+        deal(nc.scalar, wq1_raw[0], wq_dealt[:, 1, :], 0, P // 2)
+        first_codes = shared_tile("big0", [P, S + H], U32)
+        xg0_codes = first_codes[:, 0:S]
         xg0 = [
             quantize(
                 xg0_codes[:, lo : lo + HALF], "xg0_sc%d" % lo, woven0[:, lo : lo + HALF, :].rearrange("p n i -> p (n i)")
             )
             for lo in range(0, S, HALF)
         ]
+        wq_mx = [quantize(first_codes[:, S : S + H], "wq0_sc", wq_dealt[:, 0, :])]
         for lo in range(0, S, PAIR):
             gather(picked[1][:, 3, :], planes[1, 3], lo, lo + PAIR)
         bias = shared_tile("big1", [P, N // P], F32)
@@ -225,12 +235,9 @@ def tile_list_picked_exp_scores_kernel(
             load_scale_quadrant(wo_sc, wo_scales, quad)
 
         woven1 = [keep.tile([P, PAIR, PACK], BF16, name="woven1_%d" % g, align_bytes=64) for g in range(S // PAIR)]
-        wq1_dealt = keep.tile([P, H * PACK], BF16, name="wq1_dealt", align_bytes=64)
         for g in range(S // PAIR):
-            if g == S // PAIR - 1:
-                deal(nc.scalar, wq1_raw, wq1_dealt[:], 0, P // 2)
             interleave(picked[1], woven1[g][:], g * PAIR, (g + 1) * PAIR)
-        deal(nc.vector, wq0_raw[1], wq0_dealt[:], P // 2, P, P // 2)
+        deal(nc.vector, wq1_raw[1], wq_dealt[:, 1, :], P // 2, P, P // 2)
         xg1_codes = keep.tile([P, S], U32, name="xg1_codes", align_bytes=64)
 
         def quantize_pair(g):
@@ -238,27 +245,22 @@ def tile_list_picked_exp_scores_kernel(
             return quantize(xg1_codes[:, g * PAIR : (g + 1) * PAIR], "xg1_sc%d" % g, values)
 
         xg1 = [quantize_pair(0)]
-        w_codes = keep.tile([P, PASSES, H], U32, name="w_codes", align_bytes=64)
-        wq_mx = [quantize(w_codes[:, 0, :], "wq0_sc", wq0_dealt[:])]
-        deal(nc.vector, wq1_raw, wq1_dealt[:], P // 2, P)
-        xg1.extend(quantize_pair(g) for g in (1, 2))
-        wq_mx.append(quantize(w_codes[:, 1, :], "wq1_sc", wq1_dealt[:]))
-        xg1.append(quantize_pair(3))
+        wq1_codes = keep.tile([P, H], U32, name="wq1_codes", align_bytes=64)
+        wq_mx.append(quantize(wq1_codes[:], "wq1_sc", wq_dealt[:, 1, :]))
+        xg1.append(quantize_pair(1))
         q_banks = [psum_bank(c, [P, PACK, CHUNK]) for c in range(CHUNKS)]
-        for c in range(EARLY_Q):
+        for c in range(CHUNKS):
             project_e4m3(q_banks[c], c % PACK, 0, wq_mx[0], *xg0[c // PACK])
         late_dealt = shared_tile("picked1", [P, PASSES, H * PACK], BF16)
-        for a in range(PASSES):
-            deal(nc.scalar, wv_raw[a], late_dealt[:, a, :], 0, P)
+        deal(nc.scalar, wv_raw[0], late_dealt[:, 0, :], 0, P)
+        deal(nc.scalar, wv_raw[1], late_dealt[:, 1, :], 0, P)
 
         products = shared_tile("picked0", [P, CHUNKS, PACK, CHUNK], F32)
 
         def score(c):
-            if c < EARLY_Q:
-                project_e4m3(q_banks[c], c % 2, 1, wq_mx[1], *xg1[c // 2])
-            else:
-                project_e4m3(q_banks[c], c % 2, 0, wq_mx[1], *xg1[c // 2])
-                project_e4m3(q_banks[c], c % PACK, 1, wq_mx[0], *xg0[c // PACK])
+            if c in (2, 4):
+                xg1.append(quantize_pair(c // 2 + 1))
+            project_e4m3(q_banks[c], c % 2, 1, wq_mx[1], *xg1[c // 2])
             nc.vector.tensor_tensor(products[:, c], q_banks[c][:], keys[c][:], MULT)
 
         for c in range(CHUNKS - 2):

@@ -27,6 +27,7 @@ CHUNK = 128
 PAIR = 2 * CHUNK
 HALF = S // 2
 CHUNKS = S // CHUNK
+WV1_SPLIT = 96
 EARLY_VAL = 6
 MOVED_ROWS = 112
 OUT_GROUPS = ((0, 2, 0), (2, 2, 2), (4, 2, 4), (6, 1, 0), (7, 1, 2))
@@ -104,10 +105,10 @@ def tile_list_picked_exp_scores_kernel(
             out=wgt_parts[:],
             in_=wgt.rearrange("(b u) (v x) -> b (u v) x", u=CHUNKS, v=CHUNKS)[:, 0 : CHUNKS * CHUNKS : CHUNKS + 1, :],
         )
-        for quad in range(P // QUADRANT):
+        for r in range(4):
             nc.sync.dma_start(
-                out=tab_sc[QUADRANT * quad : QUADRANT * quad + 4 * PASSES, :].bitcast(I32),
-                in_=tab_scales[:, 4 * quad : 4 * quad + 4, :].bitcast(I32),
+                out=tab_sc[r : P : QUADRANT // PASSES, :].bitcast(I32),
+                in_=tab_scales[:, r:16:4, :].rearrange("a q t -> q a t").bitcast(I32),
             )
         tab = [shared_tile("big0", [P, T], I32), shared_tile("big1", [P, T], I32)]
         for a in range(PASSES):
@@ -117,7 +118,7 @@ def tile_list_picked_exp_scores_kernel(
         planes = {(0, 0): load_plane(0, 0, "big2")}
         v_sc0 = keep.tile([P, S], U8, name="v_sc0", align_bytes=64)
         nc.vector.tensor_copy(v_sc0[:], tab_sc[:].indirect(tab_list[:]))
-        nc.sync.dma_start(out=v_sc1[0:MOVED_ROWS, :].bitcast(I32), in_=v_sc0[4 : 4 + MOVED_ROWS, :].bitcast(I32))
+        nc.sync.dma_start(out=v_sc1[0:MOVED_ROWS, :].bitcast(I32), in_=v_sc0[P - MOVED_ROWS : P, :].bitcast(I32))
         v_sc = [v_sc0, v_sc1]
         for quad in range(P // QUADRANT):
             load_scale_quadrant(wk_sc, wk_scales, quad)
@@ -253,7 +254,7 @@ def tile_list_picked_exp_scores_kernel(
             project_e4m3(q_banks[c], c % PACK, 0, wq_mx[0], *xg0[c // PACK])
         late_dealt = shared_tile("picked1", [P, PASSES, H * PACK], BF16)
         deal(nc.scalar, wv_raw[0], late_dealt[:, 0, :], 0, P)
-        deal(nc.scalar, wv_raw[1], late_dealt[:, 1, :], 0, P)
+        deal(nc.scalar, wv_raw[1], late_dealt[:, 1, :], 0, WV1_SPLIT)
 
         products = shared_tile("picked0", [P, CHUNKS, PACK, CHUNK], F32)
 
@@ -265,6 +266,7 @@ def tile_list_picked_exp_scores_kernel(
 
         for c in range(CHUNKS - 2):
             score(c)
+        deal(nc.vector, wv_raw[1], late_dealt[:, 1, :], WV1_SPLIT, P)
         wv_mx = [quantize(shared_tile("keys4", [P, H], U32)[:], "wv0_sc", late_dealt[:, 0, :])]
         score(CHUNKS - 2)
         wv_mx.append(quantize(shared_tile("keys5", [P, H], U32)[:], "wv1_sc", late_dealt[:, 1, :]))

@@ -15,6 +15,7 @@ U8 = mybir.dt.uint8
 FP8X4 = mybir.dt.float8_e4m3fn_x4
 FP4X4 = mybir.dt.float4_e2m1fn_x4
 MULT = mybir.AluOpType.mult
+ADD = mybir.AluOpType.add
 EXP = mybir.ActivationFunctionType.Exp
 IDENTITY = mybir.ActivationFunctionType.Identity
 
@@ -27,8 +28,8 @@ CHUNK = 128
 PAIR = 2 * CHUNK
 HALF = S // 2
 CHUNKS = S // CHUNK
-WV1_SPLIT = 96
-EARLY_VAL = 6
+GPSIMD_STEP = 32
+EARLY_VAL = 4
 MOVED_ROWS = 112
 OUT_GROUPS = ((0, 2, 0), (2, 2, 2), (4, 2, 4), (6, 1, 0), (7, 1, 2))
 
@@ -235,7 +236,7 @@ def tile_list_picked_exp_scores_kernel(
         for quad in range(P // QUADRANT):
             load_scale_quadrant(wo_sc, wo_scales, quad)
 
-        woven1 = [keep.tile([P, PAIR, PACK], BF16, name="woven1_%d" % g, align_bytes=64) for g in range(S // PAIR)]
+        woven1 = [shared_tile("woven1_%d" % g, [P, PAIR, PACK], BF16) for g in range(S // PAIR)]
         for g in range(S // PAIR):
             interleave(picked[1], woven1[g][:], g * PAIR, (g + 1) * PAIR)
         deal(nc.vector, wq1_raw[1], wq_dealt[:, 1, :], P // 2, P, P // 2)
@@ -252,9 +253,8 @@ def tile_list_picked_exp_scores_kernel(
         q_banks = [psum_bank(c, [P, PACK, CHUNK]) for c in range(CHUNKS)]
         for c in range(CHUNKS):
             project_e4m3(q_banks[c], c % PACK, 0, wq_mx[0], *xg0[c // PACK])
-        late_dealt = shared_tile("picked1", [P, PASSES, H * PACK], BF16)
-        deal(nc.scalar, wv_raw[0], late_dealt[:, 0, :], 0, P)
-        deal(nc.scalar, wv_raw[1], late_dealt[:, 1, :], 0, WV1_SPLIT)
+        wv0_dealt = shared_tile("picked1", [P, H * PACK], BF16)
+        deal(nc.scalar, wv_raw[0], wv0_dealt[:], 0, P)
 
         products = shared_tile("picked0", [P, CHUNKS, PACK, CHUNK], F32)
 
@@ -264,14 +264,20 @@ def tile_list_picked_exp_scores_kernel(
             project_e4m3(q_banks[c], c % 2, 1, wq_mx[1], *xg1[c // 2])
             nc.vector.tensor_tensor(products[:, c], q_banks[c][:], keys[c][:], MULT)
 
-        for c in range(CHUNKS - 2):
+        for c in range(3):
             score(c)
-        deal(nc.vector, wv_raw[1], late_dealt[:, 1, :], WV1_SPLIT, P)
-        wv_mx = [quantize(shared_tile("keys4", [P, H], U32)[:], "wv0_sc", late_dealt[:, 0, :])]
+        wv1_dealt = shared_tile("woven1_2", [P, H * PACK], BF16)
+        src = wv_raw[1][:].rearrange("p j (m t) -> p m t j", t=PACK)
+        dst = wv1_dealt[:].rearrange("p (t m j) -> p m t j", t=PACK, j=PACK)
+        for lo in range(0, P, GPSIMD_STEP):
+            nc.gpsimd.tensor_scalar(dst[:, lo : lo + GPSIMD_STEP], src[:, lo : lo + GPSIMD_STEP], 1.0, 0.0, MULT, ADD)
+        for c in range(3, CHUNKS - 2):
+            score(c)
+        wv_mx = [quantize(shared_tile("keys4", [P, H], U32)[:], "wv0_sc", wv0_dealt[:])]
         score(CHUNKS - 2)
-        wv_mx.append(quantize(shared_tile("keys5", [P, H], U32)[:], "wv1_sc", late_dealt[:, 1, :]))
+        wv_mx.append(quantize(shared_tile("keys5", [P, H], U32)[:], "wv1_sc", wv1_dealt[:]))
         score(CHUNKS - 1)
-        first_scores = shared_tile("big6", [P, PACK, PACK, CHUNK], F32)
+        first_scores = shared_tile("big5", [P, PACK, PACK, CHUNK], F32)
         scores = [first_scores[:, c] if c < PACK else products[:, c] for c in range(CHUNKS)]
         for g in range(S // PAIR):
             target = first_scores if g < 2 else products
@@ -318,7 +324,7 @@ def tile_list_picked_exp_scores_kernel(
                         stop=True,
                     )
                 result = results[half]
-                on_vector = group == len(OUT_GROUPS) - 1 and half == 1
+                on_vector = count == 1 and half == 1
                 for s in range(2):
                     column = bias[:, 2 * half + s : 2 * half + s + 1]
                     if on_vector:

@@ -28,9 +28,18 @@ CHUNK = 128
 PAIR = 2 * CHUNK
 HALF = S // 2
 CHUNKS = S // CHUNK
+PAIRS = S // PAIR
 GPSIMD_STEP = 32
-EARLY_VAL = 4
+EARLY_VAL = 5
+SCALAR_ROWS = 64
 MOVED_ROWS = 112
+KIB = 1024
+PLANE_AT = (0, 8, 16, 24, 32, 40, 48, 64)
+TAB_AT = (56, 64)
+WQ0_AT = 72
+STAGE_AT = 80
+PICKED_AT = (96, 112)
+WOVEN_AT = 132
 OUT_GROUPS = ((0, 2, 0), (2, 2, 2), (4, 2, 4), (6, 1, 0), (7, 1, 2))
 
 
@@ -44,8 +53,8 @@ def tile_list_picked_exp_scores_kernel(
         ring = ctx.enter_context(tc.tile_pool(name="ring", bufs=3))
         psum = ctx.enter_context(tc.psum_pool(name="psum", bufs=1))
 
-        def shared_tile(name, shape, dtype):
-            return shared.tile(shape, dtype, name=name, align_bytes=64)
+        def shared_tile(name, place, shape, dtype):
+            return shared.tile(shape, dtype, name=name, offset=place * KIB, align_bytes=64)
 
         def psum_bank(index, shape):
             return psum.tile(shape, F32, name="bank%d" % index)
@@ -56,36 +65,28 @@ def tile_list_picked_exp_scores_kernel(
                 in_=rows[:, 4 * quad : 4 * quad + 4, :].rearrange("a r n -> r a n").bitcast(I32),
             )
 
-        def load_plane(a, i, name):
-            plane = shared_tile(name, [P, T], F32)
+        def load_plane(a, i):
+            plane = shared_tile("plane%d" % (PACK * a + i), PLANE_AT[PACK * a + i], [P, T], F32)
             nc.sync.dma_start(out=plane[:], in_=xT.rearrange("(a p i) t -> a i p t", a=PASSES, i=PACK)[a, i])
             return plane
 
-        def load_weight(w, a, name, lo=0, hi=H):
-            raw = shared_tile(name, [P, PACK, hi - lo], F32)
+        def load_weight(w, a, name, place, lo=0, hi=H):
+            raw = shared_tile(name, place, [P, PACK, hi - lo], F32)
             nc.sync.dma_start(out=raw[:], in_=w.rearrange("(a p j) r -> a p j r", a=PASSES, j=PACK)[a, :, :, lo:hi])
             return raw
 
-        def project(bank, c, nth, w_codes, w_scales, w_dtype, a_codes, a_scales):
-            entries = slice(c * CHUNK, (c + 1) * CHUNK)
-            for t in range(PACK):
+        def project(bank, slots, entries, nth, weight, a_codes, a_scales):
+            w_codes, w_scales = weight
+            for s, t in enumerate(slots):
                 nc.tensor.matmul_mx(
-                    out=bank[:, t, :],
-                    lhsT=w_codes(t).bitcast(w_dtype),
-                    lhsT_scale=w_scales(t),
+                    out=bank[:, s, :],
+                    lhsT=w_codes[:, t * P : (t + 1) * P].bitcast(FP8X4),
+                    lhsT_scale=w_scales[:, t * P : (t + 1) * P],
                     rhs=a_codes[:, entries].bitcast(FP8X4),
                     rhs_scale=a_scales[:, entries],
-                    start=(nth == 0 and t == 0),
-                    stop=(nth == PASSES - 1 and t == PACK - 1),
+                    start=(nth == 0 and s == 0),
+                    stop=(nth == PASSES - 1 and s == len(slots) - 1),
                 )
-
-        def project_e4m3(bank, c, nth, weight, a_codes, a_scales):
-            codes, scales = weight
-            project(
-                bank, c, nth,
-                lambda t: codes[:, t * P : (t + 1) * P], lambda t: scales[:, t * P : (t + 1) * P], FP8X4,
-                a_codes, a_scales,
-            )
 
         def by_two_entries(values):
             return values.rearrange("p t (c n) -> p c t n", n=2)
@@ -111,34 +112,33 @@ def tile_list_picked_exp_scores_kernel(
                 out=tab_sc[r : P : QUADRANT // PASSES, :].bitcast(I32),
                 in_=tab_scales[:, r:16:4, :].rearrange("a q t -> q a t").bitcast(I32),
             )
-        tab = [shared_tile("big0", [P, T], I32), shared_tile("big1", [P, T], I32)]
+        tab = [shared_tile("tab%d" % a, TAB_AT[a], [P, T], I32) for a in range(PASSES)]
         for a in range(PASSES):
             nc.sync.dma_start(out=tab[a][:], in_=tab_words[a].rearrange("p t i -> p (t i)").bitcast(I32))
         head_lists = keep.tile([P, S // LIST_ROWS], U16, name="head_lists")
         nc.sync.dma_start(head_lists[:], offs2)
-        planes = {(0, 0): load_plane(0, 0, "big2")}
+        planes = {(0, 0): load_plane(0, 0)}
         v_sc0 = keep.tile([P, S], U8, name="v_sc0", align_bytes=64)
         nc.vector.tensor_copy(v_sc0[:], tab_sc[:].indirect(tab_list[:]))
-        nc.sync.dma_start(out=v_sc1[0:MOVED_ROWS, :].bitcast(I32), in_=v_sc0[P - MOVED_ROWS : P, :].bitcast(I32))
         v_sc = [v_sc0, v_sc1]
         for quad in range(P // QUADRANT):
             load_scale_quadrant(wk_sc, wk_scales, quad)
         wk_codes = keep.tile([P, PASSES, 2 * H], U8, name="wk_codes", align_bytes=64)
         nc.sync.dma_start(out=wk_codes[:].bitcast(I32), in_=wk_words.rearrange("a p n -> p a n").bitcast(I32))
-        planes[0, 1] = load_plane(0, 1, "big3")
-        for i in (2, 3):
-            planes[0, i] = load_plane(0, i, "big%d" % (2 + i))
-        planes[1, 0] = load_plane(1, 0, "big6")
-        planes[1, 1] = load_plane(1, 1, "big7")
+        nc.sync.dma_start(out=v_sc1[0:MOVED_ROWS, :].bitcast(I32), in_=v_sc0[P - MOVED_ROWS : P, :].bitcast(I32))
+        for i in (1, 2, 3):
+            planes[0, i] = load_plane(0, i)
+        for i in (0, 1, 2):
+            planes[1, i] = load_plane(1, i)
 
         turned = psum_bank(0, [P, P])
         nc.tensor.transpose(turned[:], wgt_parts[:], identity[:])
-        spread = shared_tile("woven0", [P, CHUNKS, P], F32)
+        spread = shared_tile("spread", STAGE_AT, [P, CHUNKS, P], F32)
         nc.scalar.copy(
             out=spread[:].rearrange("x u (b c) -> x u b c", c=CHUNKS),
             in_=turned[:].rearrange("x (b u) -> x u b", u=CHUNKS).unsqueeze(3).to_broadcast([P, CHUNKS, 16, CHUNKS]),
         )
-        weights = shared_tile("weights", [P, S], F32)
+        weights = keep.tile([P, S], F32, name="weights")
         for half in range(2):
             back = psum_bank(1 + half, [P, PACK, CHUNK])
             for u in range(PACK):
@@ -148,43 +148,48 @@ def tile_list_picked_exp_scores_kernel(
         v_codes = [keep.tile([P, S], U32, name="v_codes%d" % a, align_bytes=64) for a in range(PASSES)]
         for a in range(PASSES):
             nc.vector.tensor_copy(v_codes[a][:], tab[a][:].bitcast(U32).indirect(tab_list[:]))
-        planes[1, 2] = load_plane(1, 2, "big0")
+        wk_dealt = keep.tile([P, PASSES, PACK, 2 * P], U8, name="wk_dealt", align_bytes=64)
+        nc.scalar.copy(
+            out=wk_dealt[:].bitcast(U16), in_=wk_codes[:].bitcast(U16).rearrange("p a (m t) -> p a t m", t=PACK)
+        )
+        wk_sc_dealt = keep.tile([P, PASSES, PACK, P], U8, name="wk_sc_dealt", align_bytes=64)
+        nc.vector.tensor_copy(wk_sc_dealt[:], wk_sc[:].rearrange("p a (m t) -> p a t m", t=PACK))
 
         def gather(dst, plane, lo, hi):
             lists = head_lists[:, lo // LIST_ROWS : hi // LIST_ROWS]
             nc.vector.tensor_tensor(dst[:, lo:hi], plane[:].indirect(lists), weights[:, lo:hi], MULT)
 
-        picked = [shared_tile("picked%d" % a, [P, PACK, S], F32) for a in range(PASSES)]
-        gather(picked[0][:, 0, :], planes[0, 0], 0, S)
-        wq0_raw = load_weight(wq, 0, "big2")
-        gather(picked[0][:, 1, :], planes[0, 1], 0, S)
-        wq1_raw = [load_weight(wq, 1, "big3", 0, H // 2)]
-        planes[1, 3] = load_plane(1, 3, "big1")
-        gather(picked[0][:, 2, :], planes[0, 2], 0, S)
-        wq1_raw.append(load_weight(wq, 1, "big4", H // 2, H))
-        gather(picked[0][:, 3, :], planes[0, 3], 0, S)
-        wv_raw = [load_weight(wv, 0, "big5")]
+        picked = [shared_tile("picked%d" % a, PICKED_AT[a], [P, PACK, S], F32) for a in range(PASSES)]
+        for i in range(PACK):
+            gather(picked[0][:, i, :], planes[0, i], 0, S)
+        wq_raw = [load_weight(wq, 0, "wq0_raw", WQ0_AT), load_weight(wq, 1, "wq1_early", TAB_AT[0], 0, H // 2)]
+        planes[1, 3] = load_plane(1, 3)
+        wq1_late = load_weight(wq, 1, "wq1_late", TAB_AT[0] + 4, H // 2, H)
+        wv_raw = [load_weight(wv, a, "wv%d_raw" % a, PLANE_AT[a]) for a in range(PASSES)]
 
-        keys = [shared_tile("keys%d" % c, [P, PACK, CHUNK], F32) for c in range(CHUNKS)]
-        for c in range(CHUNKS):
-            entries = slice(c * CHUNK, (c + 1) * CHUNK)
-            by_entry = psum_bank(c % PACK, [P, H])
+        def deal(raw, dealt, first=0, engine=nc.scalar, count=P):
+            src = raw[:].rearrange("p j (m t) -> p m j t", t=PACK)[:, 0 : min(count, raw.shape[2] // PACK)]
+            dst = dealt.rearrange("p (t m j) -> p m j t", t=PACK, j=PACK)[:, first : first + src.shape[1]]
+            if engine is nc.scalar:
+                nc.scalar.copy(out=dst, in_=src)
+            else:
+                nc.vector.tensor_copy(dst, src)
+
+        keys = keep.tile([P, PACK, S], F32, name="keys")
+        for b in range(CHUNKS):
+            t, entries = b % PACK, slice(b // PACK * HALF, (b // PACK + 1) * HALF)
+            bank = psum_bank(b, [P, HALF])
             for nth, a in enumerate((1, 0)):
                 nc.tensor.matmul_mx(
-                    out=by_entry[:],
-                    lhsT=v_codes[a][:, entries].bitcast(FP8X4),
-                    lhsT_scale=v_sc[a][:, entries],
-                    rhs=wk_codes[:, a, :].bitcast(FP4X4),
-                    rhs_scale=wk_sc[:, a, :],
+                    out=bank[:],
+                    lhsT=wk_dealt[:, a, t, :].bitcast(FP4X4),
+                    lhsT_scale=wk_sc_dealt[:, a, t, :],
+                    rhs=v_codes[a][:, entries].bitcast(FP8X4),
+                    rhs_scale=v_sc[a][:, entries],
                     start=(nth == 0),
                     stop=(nth == PASSES - 1),
                 )
-            dealt = ring.tile([P, PACK, P], F32, name="keys_by_entry")
-            nc.scalar.copy(out=dealt[:], in_=by_entry[:].rearrange("j (m t) -> j t m", t=PACK))
-            by_channel = psum_bank(PACK + c % PACK, [P, PACK, CHUNK])
-            for t in range(PACK):
-                nc.tensor.transpose(by_channel[:, t, :], dealt[:, t, :], identity[:])
-            nc.scalar.copy(out=keys[c][:], in_=by_channel[:])
+            nc.scalar.copy(out=keys[:, t, entries], in_=bank[:])
 
         def interleave(picked_pass, woven, lo, hi):
             nc.scalar.copy(
@@ -192,114 +197,105 @@ def tile_list_picked_exp_scores_kernel(
                 in_=picked_pass[:, :, lo:hi].rearrange("p i (c n) -> p c i n", n=4),
             )
 
-        def deal(engine, raw, dealt, lo, hi, first=0):
-            src = raw[:].rearrange("p j (m t) -> p m j t", t=PACK)[:, lo - first : hi - first]
-            dst = dealt.rearrange("p (t m j) -> p m j t", t=PACK, j=PACK)[:, lo:hi]
-            if engine is nc.scalar:
-                nc.scalar.copy(out=dst, in_=src)
+        def quantize(name, values, place=None):
+            width = values.shape[1] // PACK
+            if place is None:
+                codes = keep.tile([P, width], U32, name=name + "_codes", align_bytes=64)
             else:
-                nc.vector.tensor_copy(dst, src)
-
-        def quantize(codes, name, values):
-            scales = keep.tile([P, codes.shape[1]], U8, name=name, align_bytes=64)
-            nc.vector.quantize_mx(out=codes.bitcast(FP8X4), scales=scales[:], in_=values)
+                codes = shared_tile(name + "_codes", place, [P, width], U32)
+            scales = keep.tile([P, width], U8, name=name + "_sc", align_bytes=64)
+            nc.vector.quantize_mx(out=codes[:].bitcast(FP8X4), scales=scales[:], in_=values)
             return codes, scales
 
-        woven0 = shared_tile("woven0", [P, S, PACK], BF16)
+        woven0 = shared_tile("woven0", STAGE_AT, [P, S, PACK], BF16)
         for lo in range(0, S, HALF):
             interleave(picked[0], woven0[:, lo : lo + HALF, :], lo, lo + HALF)
-        gather(picked[1][:, 0, :], planes[1, 0], 0, S)
-        wv_raw.append(load_weight(wv, 1, "big6"))
-        gather(picked[1][:, 1, :], planes[1, 1], 0, S)
-        wo_codes = shared_tile("big7", [P, N], I32)
-        nc.sync.dma_start(out=wo_codes[:], in_=wo_words[0].rearrange("p c i -> p (c i)").bitcast(I32))
-        gather(picked[1][:, 2, :], planes[1, 2], 0, S)
-        wq_dealt = shared_tile("picked0", [P, PASSES, H * PACK], BF16)
-        deal(nc.scalar, wq0_raw, wq_dealt[:, 0, :], 0, P)
-        deal(nc.scalar, wq1_raw[0], wq_dealt[:, 1, :], 0, P // 2)
-        first_codes = shared_tile("big0", [P, S + H], U32)
-        xg0_codes = first_codes[:, 0:S]
+        for i in range(PACK - 1):
+            gather(picked[1][:, i, :], planes[1, i], 0, S)
+        dealt = [shared_tile("dealt%d" % a, PICKED_AT[0] + 4 * a, [P, H * PACK], BF16) for a in range(PASSES)]
+        for a in range(PASSES):
+            deal(wq_raw[a], dealt[a][:])
         xg0 = [
-            quantize(
-                xg0_codes[:, lo : lo + HALF], "xg0_sc%d" % lo, woven0[:, lo : lo + HALF, :].rearrange("p n i -> p (n i)")
-            )
-            for lo in range(0, S, HALF)
+            quantize("xg0_%d" % lo, woven0[:, lo : lo + HALF, :].rearrange("p n i -> p (n i)")) for lo in range(0, S, HALF)
         ]
-        wq_mx = [quantize(first_codes[:, S : S + H], "wq0_sc", wq_dealt[:, 0, :])]
-        for lo in range(0, S, PAIR):
-            gather(picked[1][:, 3, :], planes[1, 3], lo, lo + PAIR)
-        bias = shared_tile("big1", [P, N // P], F32)
-        with nc.allow_non_contiguous_dma(reason="one bias value a partition and tile of 128 outputs"):
-            nc.sync.dma_start(out=bias[:], in_=bo.rearrange("(u p) -> p u", p=P))
-        wo_sc = shared_tile("weights", [P, 1, N], U8)
+        wo_codes = shared_tile("wo_codes", STAGE_AT, [P, N], I32)
+        nc.sync.dma_start(out=wo_codes[:], in_=wo_words[0].rearrange("p c i -> p (c i)").bitcast(I32))
+        wo_sc = shared_tile("wo_sc", STAGE_AT + 2, [P, 1, N], U8)
         nc.gpsimd.memset(wo_sc[:].bitcast(I32), 0)
         for quad in range(P // QUADRANT):
             load_scale_quadrant(wo_sc, wo_scales, quad)
+        bias = shared_tile("bias", STAGE_AT + 3, [P, N // P], F32)
+        with nc.allow_non_contiguous_dma(reason="one bias value a partition and tile of 128 outputs"):
+            nc.sync.dma_start(out=bias[:], in_=bo.rearrange("(u p) -> p u", p=P))
+        wq_mx = [quantize("wq0", dealt[0][:])]
+        for lo in range(0, S, PAIR):
+            gather(picked[1][:, PACK - 1, :], planes[1, PACK - 1], lo, lo + PAIR)
 
-        woven1 = [shared_tile("woven1_%d" % g, [P, PAIR, PACK], BF16) for g in range(S // PAIR)]
-        for g in range(S // PAIR):
+        woven1 = [shared_tile("woven1_%d" % g, WOVEN_AT + 2 * g, [P, PAIR, PACK], BF16) for g in range(PAIRS)]
+        interleave(picked[1], woven1[0][:], 0, PAIR)
+        deal(wq1_late, dealt[1][:], P // 2, nc.scalar)
+        for g in range(1, PAIRS):
             interleave(picked[1], woven1[g][:], g * PAIR, (g + 1) * PAIR)
-        deal(nc.vector, wq1_raw[1], wq_dealt[:, 1, :], P // 2, P, P // 2)
-        xg1_codes = keep.tile([P, S], U32, name="xg1_codes", align_bytes=64)
+
+        q_banks = [psum_bank(b, [P, 2, PAIR]) for b in range(CHUNKS)]
+        for b in range(CHUNKS):
+            g = b // 2
+            first = (g % 2) * PAIR
+            project(q_banks[b], (2 * (b % 2), 2 * (b % 2) + 1), slice(first, first + PAIR), 0, wq_mx[0], *xg0[g // 2])
+
+        products = [shared_tile("products%d" % n, PLANE_AT[2 + n], [P, 2, PACK, PAIR], F32) for n in range(2)]
+        scores = [shared_tile("scores%d" % n, PLANE_AT[4 * n], [P, 2, PACK, PAIR], F32) for n in range(2)]
+        val_banks = []
 
         def quantize_pair(g):
-            values = woven1[g][:].rearrange("p n i -> p (n i)")
-            return quantize(xg1_codes[:, g * PAIR : (g + 1) * PAIR], "xg1_sc%d" % g, values)
+            return quantize("xg1_%d" % g, woven1[g][:].rearrange("p n i -> p (n i)"))
+
+        def score(b):
+            g = b // 2
+            slots = slice(2 * (b % 2), 2 * (b % 2) + 2)
+            project(q_banks[b], (slots.start, slots.start + 1), slice(0, PAIR), 1, wq_mx[1], *xg1[g])
+            nc.vector.tensor_tensor(
+                products[g // 2][:, g % 2, slots, :], q_banks[b][:], keys[:, slots, g * PAIR : (g + 1) * PAIR], MULT
+            )
 
         xg1 = [quantize_pair(0)]
-        wq1_codes = keep.tile([P, H], U32, name="wq1_codes", align_bytes=64)
-        wq_mx.append(quantize(wq1_codes[:], "wq1_sc", wq_dealt[:, 1, :]))
+        wq_mx.append(quantize("wq1", dealt[1][:]))
         xg1.append(quantize_pair(1))
-        q_banks = [psum_bank(c, [P, PACK, CHUNK]) for c in range(CHUNKS)]
+        wv_dealt = shared_tile("wv_dealt", WOVEN_AT - 4, [P, PASSES, H * PACK], BF16)
+        deal(wv_raw[0], wv_dealt[:, 0, :], 0, nc.scalar, SCALAR_ROWS)
+        for a, first in ((0, SCALAR_ROWS), (1, 0)):
+            src = wv_raw[a][:].rearrange("p j (m t) -> p m t j", t=PACK)
+            dst = wv_dealt[:, a, :].rearrange("p (t m j) -> p m t j", t=PACK, j=PACK)
+            for lo in range(first, P, GPSIMD_STEP):
+                rows = slice(lo, lo + GPSIMD_STEP)
+                nc.gpsimd.tensor_scalar(dst[:, rows], src[:, rows], 1.0, 0.0, MULT, ADD)
+        wv_mx = []
+        for b in range(CHUNKS):
+            if b in (2, 4):
+                xg1.append(quantize_pair(b // 2 + 1))
+            if b in (5, 7):
+                wv_mx.append(quantize("wv%d" % len(wv_mx), wv_dealt[:, len(wv_mx), :]))
+            score(b)
+        for g in range(PAIRS):
+            nc.scalar.activation(scores[g // 2][:, g % 2], products[g // 2][:, g % 2], EXP)
         for c in range(CHUNKS):
-            project_e4m3(q_banks[c], c % PACK, 0, wq_mx[0], *xg0[c // PACK])
-        wv0_dealt = shared_tile("picked1", [P, H * PACK], BF16)
-        deal(nc.scalar, wv_raw[0], wv0_dealt[:], 0, P)
-
-        products = shared_tile("picked0", [P, CHUNKS, PACK, CHUNK], F32)
-
-        def score(c):
-            if c in (2, 4):
-                xg1.append(quantize_pair(c // 2 + 1))
-            project_e4m3(q_banks[c], c % 2, 1, wq_mx[1], *xg1[c // 2])
-            nc.vector.tensor_tensor(products[:, c], q_banks[c][:], keys[c][:], MULT)
-
-        for c in range(3):
-            score(c)
-        wv1_dealt = shared_tile("woven1_2", [P, H * PACK], BF16)
-        src = wv_raw[1][:].rearrange("p j (m t) -> p m t j", t=PACK)
-        dst = wv1_dealt[:].rearrange("p (t m j) -> p m t j", t=PACK, j=PACK)
-        for lo in range(0, P, GPSIMD_STEP):
-            nc.gpsimd.tensor_scalar(dst[:, lo : lo + GPSIMD_STEP], src[:, lo : lo + GPSIMD_STEP], 1.0, 0.0, MULT, ADD)
-        for c in range(3, CHUNKS - 2):
-            score(c)
-        wv_mx = [quantize(shared_tile("keys4", [P, H], U32)[:], "wv0_sc", wv0_dealt[:])]
-        score(CHUNKS - 2)
-        wv_mx.append(quantize(shared_tile("keys5", [P, H], U32)[:], "wv1_sc", wv1_dealt[:]))
-        score(CHUNKS - 1)
-        first_scores = shared_tile("big5", [P, PACK, PACK, CHUNK], F32)
-        scores = [first_scores[:, c] if c < PACK else products[:, c] for c in range(CHUNKS)]
-        for g in range(S // PAIR):
-            target = first_scores if g < 2 else products
-            nc.scalar.activation(target[:, 2 * g : 2 * g + 2], products[:, 2 * g : 2 * g + 2], EXP)
-
-        val_banks = [psum_bank(c, [P, PACK, CHUNK]) for c in range(CHUNKS)]
+            val_banks.append(psum_bank(c, [P, PACK, CHUNK]))
         for c in range(EARLY_VAL):
-            project_e4m3(val_banks[c], c, 0, wv_mx[0], v_codes[0], v_sc[0])
-        h_tiles = [
-            keep.tile([P, count * CHUNK, PACK], BF16, name="h%d" % first, align_bytes=64)
-            for first, count, first_bank in OUT_GROUPS
-        ]
-        out_rows = out.rearrange("(u p) j -> p u j", p=P)
-        results = [shared_tile("big2", [P, 2, S], F32), shared_tile("big3", [P, 2, S], F32)]
+            project(val_banks[c], range(PACK), slice(c * CHUNK, (c + 1) * CHUNK), 0, wv_mx[0], v_codes[0], v_sc[0])
 
-        def weigh_values(group, u):
-            c = OUT_GROUPS[group][0] + u
+        h_all = shared_tile("h_all", WQ0_AT, [P, S, PACK], BF16)
+        out_rows = out.rearrange("(u p) j -> p u j", p=P)
+        results = shared_tile("results", PICKED_AT[0], [P, PACK, S], F32)
+
+        def weigh_values(c):
+            entries = slice(c * CHUNK, (c + 1) * CHUNK)
             order = (1,) if c < EARLY_VAL else (1, 0)
             for nth, a in enumerate(order):
-                project_e4m3(val_banks[c], c, PASSES - len(order) + nth, wv_mx[a], v_codes[a], v_sc[a])
-            woven = h_tiles[group][:, u * CHUNK : (u + 1) * CHUNK, :].rearrange("p (c n) t -> p c t n", n=2)
-            nc.vector.tensor_tensor(woven, by_two_entries(val_banks[c][:]), by_two_entries(scores[c]), MULT)
+                project(val_banks[c], range(PACK), entries, PASSES - len(order) + nth, wv_mx[a], v_codes[a], v_sc[a])
+            woven = h_all[:, entries, :].rearrange("p (c n) t -> p c t n", n=2)
+            within = slice((c % 2) * CHUNK, (c % 2 + 1) * CHUNK)
+            score_c = scores[c // PACK][:, c // 2 % 2, :, within]
+            nc.vector.tensor_tensor(woven, by_two_entries(val_banks[c][:]), by_two_entries(score_c), MULT)
 
         def finish(group):
             first, count, first_bank = OUT_GROUPS[group]
@@ -308,7 +304,7 @@ def tile_list_picked_exp_scores_kernel(
             h_codes = ring.tile([P, width], U32, name="h_codes", align_bytes=64)
             h_sc = ring.tile([P, width], U8, name="h_sc", align_bytes=64)
             nc.vector.quantize_mx(
-                out=h_codes[:].bitcast(FP8X4), scales=h_sc[:], in_=h_tiles[group][:].rearrange("p n t -> p (n t)")
+                out=h_codes[:].bitcast(FP8X4), scales=h_sc[:], in_=h_all[:, entries, :].rearrange("p n t -> p (n t)")
             )
             for half in range(2):
                 bank = psum_bank(first_bank + half, [P, 2, width])
@@ -323,20 +319,19 @@ def tile_list_picked_exp_scores_kernel(
                         start=True,
                         stop=True,
                     )
-                result = results[half]
                 on_vector = count == 1 and half == 1
                 for s in range(2):
-                    column = bias[:, 2 * half + s : 2 * half + s + 1]
+                    u = 2 * half + s
                     if on_vector:
-                        nc.vector.tensor_scalar_add(result[:, s, entries], bank[:, s, :], column)
+                        nc.vector.tensor_scalar_add(results[:, u, entries], bank[:, s, :], bias[:, u : u + 1])
                     else:
-                        nc.scalar.activation(result[:, s, entries], bank[:, s, :], IDENTITY, bias=column)
-                nc.sync.dma_start(out=out_rows[:, 2 * half : 2 * half + 2, entries], in_=result[:, :, entries])
+                        nc.scalar.activation(results[:, u, entries], bank[:, s, :], IDENTITY, bias=bias[:, u : u + 1])
+                nc.sync.dma_start(out=out_rows[:, 2 * half : 2 * half + 2, entries], in_=results[:, 2 * half : 2 * half + 2, entries])
 
         for group, (first, count, first_bank) in enumerate(OUT_GROUPS):
-            weigh_values(group, 0)
+            weigh_values(first)
             if group > 0:
                 finish(group - 1)
             for u in range(1, count):
-                weigh_values(group, u)
+                weigh_values(first + u)
         finish(len(OUT_GROUPS) - 1)

@@ -31,7 +31,6 @@ CHUNKS = S // CHUNK
 PAIRS = S // PAIR
 GPSIMD_STEP = 32
 EARLY_VAL = 5
-SCALAR_ROWS = 64
 MOVED_ROWS = 112
 KIB = 1024
 PLANE_AT = (0, 8, 16, 24, 32, 40, 48, 64)
@@ -113,16 +112,16 @@ def tile_list_picked_exp_scores_kernel(
                 in_=tab_scales[:, r:16:4, :].rearrange("a q t -> q a t").bitcast(I32),
             )
         tab = [shared_tile("tab%d" % a, TAB_AT[a], [P, T], I32) for a in range(PASSES)]
-        for a in range(PASSES):
-            nc.sync.dma_start(out=tab[a][:], in_=tab_words[a].rearrange("p t i -> p (t i)").bitcast(I32))
+        nc.sync.dma_start(out=tab[0][:], in_=tab_words[0].rearrange("p t i -> p (t i)").bitcast(I32))
+        for quad in range(P // QUADRANT):
+            load_scale_quadrant(wk_sc, wk_scales, quad)
+        nc.sync.dma_start(out=tab[1][:], in_=tab_words[1].rearrange("p t i -> p (t i)").bitcast(I32))
         head_lists = keep.tile([P, S // LIST_ROWS], U16, name="head_lists")
         nc.sync.dma_start(head_lists[:], offs2)
         planes = {(0, 0): load_plane(0, 0)}
         v_sc0 = keep.tile([P, S], U8, name="v_sc0", align_bytes=64)
         nc.vector.tensor_copy(v_sc0[:], tab_sc[:].indirect(tab_list[:]))
         v_sc = [v_sc0, v_sc1]
-        for quad in range(P // QUADRANT):
-            load_scale_quadrant(wk_sc, wk_scales, quad)
         wk_codes = keep.tile([P, PASSES, 2 * H], U8, name="wk_codes", align_bytes=64)
         nc.sync.dma_start(out=wk_codes[:].bitcast(I32), in_=wk_words.rearrange("a p n -> p a n").bitcast(I32))
         nc.sync.dma_start(out=v_sc1[0:MOVED_ROWS, :].bitcast(I32), in_=v_sc0[P - MOVED_ROWS : P, :].bitcast(I32))
@@ -153,7 +152,8 @@ def tile_list_picked_exp_scores_kernel(
             out=wk_dealt[:].bitcast(U16), in_=wk_codes[:].bitcast(U16).rearrange("p a (m t) -> p a t m", t=PACK)
         )
         wk_sc_dealt = keep.tile([P, PASSES, PACK, P], U8, name="wk_sc_dealt", align_bytes=64)
-        nc.vector.tensor_copy(wk_sc_dealt[:], wk_sc[:].rearrange("p a (m t) -> p a t m", t=PACK))
+        for a in range(PASSES):
+            nc.gpsimd.tensor_copy(wk_sc_dealt[:, a], wk_sc[:, a, :].rearrange("p (m t) -> p t m", t=PACK))
 
         def gather(dst, plane, lo, hi):
             lists = head_lists[:, lo // LIST_ROWS : hi // LIST_ROWS]
@@ -162,13 +162,15 @@ def tile_list_picked_exp_scores_kernel(
         picked = [shared_tile("picked%d" % a, PICKED_AT[a], [P, PACK, S], F32) for a in range(PASSES)]
         for i in range(PACK):
             gather(picked[0][:, i, :], planes[0, i], 0, S)
-        wq_raw = [load_weight(wq, 0, "wq0_raw", WQ0_AT), load_weight(wq, 1, "wq1_early", TAB_AT[0], 0, H // 2)]
+        halves = ((0, H // 2), (H // 2, H))
+        wq0_raw = [load_weight(wq, 0, "wq0_raw%d" % n, WQ0_AT + 4 * n, *halves[n]) for n in range(2)]
         planes[1, 3] = load_plane(1, 3)
-        wq1_late = load_weight(wq, 1, "wq1_late", TAB_AT[0] + 4, H // 2, H)
-        wv_raw = [load_weight(wv, a, "wv%d_raw" % a, PLANE_AT[a]) for a in range(PASSES)]
+        wq1_raw = [load_weight(wq, 1, "wq1_raw%d" % n, TAB_AT[0] + 4 * n, *halves[n]) for n in range(2)]
+        wv0_raw = load_weight(wv, 0, "wv0_raw", PLANE_AT[0])
+        wv1_raw = [load_weight(wv, 1, "wv1_raw%d" % n, PLANE_AT[1] + 4 * n, *halves[n]) for n in range(2)]
 
-        def deal(raw, dealt, first=0, engine=nc.scalar, count=P):
-            src = raw[:].rearrange("p j (m t) -> p m j t", t=PACK)[:, 0 : min(count, raw.shape[2] // PACK)]
+        def deal(raw, dealt, first=0, engine=nc.scalar):
+            src = raw[:].rearrange("p j (m t) -> p m j t", t=PACK)
             dst = dealt.rearrange("p (t m j) -> p m j t", t=PACK, j=PACK)[:, first : first + src.shape[1]]
             if engine is nc.scalar:
                 nc.scalar.copy(out=dst, in_=src)
@@ -213,8 +215,8 @@ def tile_list_picked_exp_scores_kernel(
         for i in range(PACK - 1):
             gather(picked[1][:, i, :], planes[1, i], 0, S)
         dealt = [shared_tile("dealt%d" % a, PICKED_AT[0] + 4 * a, [P, H * PACK], BF16) for a in range(PASSES)]
-        for a in range(PASSES):
-            deal(wq_raw[a], dealt[a][:])
+        for n in range(2):
+            deal(wq0_raw[n], dealt[0][:], n * P // 2)
         xg0 = [
             quantize("xg0_%d" % lo, woven0[:, lo : lo + HALF, :].rearrange("p n i -> p (n i)")) for lo in range(0, S, HALF)
         ]
@@ -228,12 +230,12 @@ def tile_list_picked_exp_scores_kernel(
         with nc.allow_non_contiguous_dma(reason="one bias value a partition and tile of 128 outputs"):
             nc.sync.dma_start(out=bias[:], in_=bo.rearrange("(u p) -> p u", p=P))
         wq_mx = [quantize("wq0", dealt[0][:])]
-        for lo in range(0, S, PAIR):
-            gather(picked[1][:, PACK - 1, :], planes[1, PACK - 1], lo, lo + PAIR)
+        for lo, hi in ((0, PAIR), (PAIR, S)):
+            gather(picked[1][:, PACK - 1, :], planes[1, PACK - 1], lo, hi)
 
         woven1 = [shared_tile("woven1_%d" % g, WOVEN_AT + 2 * g, [P, PAIR, PACK], BF16) for g in range(PAIRS)]
         interleave(picked[1], woven1[0][:], 0, PAIR)
-        deal(wq1_late, dealt[1][:], P // 2, nc.scalar)
+        deal(wq1_raw[0], dealt[1][:])
         for g in range(1, PAIRS):
             interleave(picked[1], woven1[g][:], g * PAIR, (g + 1) * PAIR)
 
@@ -244,7 +246,7 @@ def tile_list_picked_exp_scores_kernel(
             project(q_banks[b], (2 * (b % 2), 2 * (b % 2) + 1), slice(first, first + PAIR), 0, wq_mx[0], *xg0[g // 2])
 
         products = [shared_tile("products%d" % n, PLANE_AT[2 + n], [P, 2, PACK, PAIR], F32) for n in range(2)]
-        scores = [shared_tile("scores%d" % n, PLANE_AT[4 * n], [P, 2, PACK, PAIR], F32) for n in range(2)]
+        scores = [shared_tile("scores%d" % n, PLANE_AT[1 + 3 * n], [P, 2, PACK, PAIR], F32) for n in range(2)]
         val_banks = []
 
         def quantize_pair(g):
@@ -258,15 +260,16 @@ def tile_list_picked_exp_scores_kernel(
                 products[g // 2][:, g % 2, slots, :], q_banks[b][:], keys[:, slots, g * PAIR : (g + 1) * PAIR], MULT
             )
 
+        deal(wq1_raw[1], dealt[1][:], P // 2, nc.vector)
         xg1 = [quantize_pair(0)]
         wq_mx.append(quantize("wq1", dealt[1][:]))
         xg1.append(quantize_pair(1))
         wv_dealt = shared_tile("wv_dealt", WOVEN_AT - 4, [P, PASSES, H * PACK], BF16)
-        deal(wv_raw[0], wv_dealt[:, 0, :], 0, nc.scalar, SCALAR_ROWS)
-        for a, first in ((0, SCALAR_ROWS), (1, 0)):
-            src = wv_raw[a][:].rearrange("p j (m t) -> p m t j", t=PACK)
+        deal(wv1_raw[1], wv_dealt[:, 1, :], P // 2)
+        for a, raw in enumerate((wv0_raw, wv1_raw[0])):
+            src = raw[:].rearrange("p j (m t) -> p m t j", t=PACK)
             dst = wv_dealt[:, a, :].rearrange("p (t m j) -> p m t j", t=PACK, j=PACK)
-            for lo in range(first, P, GPSIMD_STEP):
+            for lo in range(0, src.shape[1], GPSIMD_STEP):
                 rows = slice(lo, lo + GPSIMD_STEP)
                 nc.gpsimd.tensor_scalar(dst[:, rows], src[:, rows], 1.0, 0.0, MULT, ADD)
         wv_mx = []

@@ -31,7 +31,7 @@ CHUNKS = S // CHUNK
 PAIRS = S // PAIR
 GPSIMD_STEP = 32
 EARLY_VAL = 5
-MOVED_ROWS = 112
+FIRST_MOVES = 5
 KIB = 1024
 PLANE_AT = (0, 8, 16, 24, 32, 40, 48, 64)
 TAB_AT = (56, 64)
@@ -92,40 +92,45 @@ def tile_list_picked_exp_scores_kernel(
 
         tab_sc = keep.tile([P, T], U8, name="tab_sc", align_bytes=64)
         wk_sc = keep.tile([P, PASSES, H], U8, name="wk_sc", align_bytes=64)
-        v_sc1 = keep.tile([P, S], U8, name="v_sc1", align_bytes=64)
-        nc.gpsimd.memset(tab_sc[:].bitcast(I32), 0)
-        nc.vector.memset(wk_sc[:].bitcast(I32), 0)
-        nc.vector.memset(v_sc1[:].bitcast(I32), 0)
+        v_sc = [keep.tile([P, S], U8, name="v_sc%d" % a, align_bytes=64) for a in range(PASSES)]
+        nc.gpsimd.memset(wk_sc[:].bitcast(I32), 0)
+        nc.vector.memset(tab_sc[QUADRANT : 2 * QUADRANT, :].bitcast(I32), 0)
+        nc.vector.memset(tab_sc[2 * QUADRANT : P, :].bitcast(I32), 0)
+        for a in range(PASSES):
+            nc.gpsimd.memset(v_sc[a][:].bitcast(I32), 0)
         identity = keep.tile([P, P], F32, name="identity")
         make_identity(nc, identity[:])
 
         tab_list = keep.tile([P, S // LIST_ROWS], U16, name="tab_list")
         nc.sync.dma_start(tab_list[:], offs)
+        nc.sync.dma_start(
+            out=tab_sc[0:QUADRANT, :].bitcast(I32), in_=tab_scales.rearrange("a q t -> (a q) t").bitcast(I32)
+        )
+        tab = [shared_tile("tab%d" % a, TAB_AT[a], [P, T], I32) for a in range(PASSES)]
+        nc.sync.dma_start(out=tab[0][:], in_=tab_words[0].rearrange("p t i -> p (t i)").bitcast(I32))
         wgt_parts = keep.tile([P, CHUNK], F32, name="wgt_parts")
         nc.sync.dma_start(
             out=wgt_parts[:],
             in_=wgt.rearrange("(b u) (v x) -> b (u v) x", u=CHUNKS, v=CHUNKS)[:, 0 : CHUNKS * CHUNKS : CHUNKS + 1, :],
         )
-        for r in range(4):
-            nc.sync.dma_start(
-                out=tab_sc[r : P : QUADRANT // PASSES, :].bitcast(I32),
-                in_=tab_scales[:, r:16:4, :].rearrange("a q t -> q a t").bitcast(I32),
-            )
-        tab = [shared_tile("tab%d" % a, TAB_AT[a], [P, T], I32) for a in range(PASSES)]
-        nc.sync.dma_start(out=tab[0][:], in_=tab_words[0].rearrange("p t i -> p (t i)").bitcast(I32))
         for quad in range(P // QUADRANT):
             load_scale_quadrant(wk_sc, wk_scales, quad)
         nc.sync.dma_start(out=tab[1][:], in_=tab_words[1].rearrange("p t i -> p (t i)").bitcast(I32))
         head_lists = keep.tile([P, S // LIST_ROWS], U16, name="head_lists")
         nc.sync.dma_start(head_lists[:], offs2)
         planes = {(0, 0): load_plane(0, 0)}
-        v_sc0 = keep.tile([P, S], U8, name="v_sc0", align_bytes=64)
-        nc.vector.tensor_copy(v_sc0[:], tab_sc[:].indirect(tab_list[:]))
-        v_sc = [v_sc0, v_sc1]
+        picked_sc = keep.tile([P, S], U8, name="picked_sc", align_bytes=64)
+        nc.vector.tensor_copy(picked_sc[:], tab_sc[:].indirect(tab_list[:]))
         wk_codes = keep.tile([P, PASSES, 2 * H], U8, name="wk_codes", align_bytes=64)
         nc.sync.dma_start(out=wk_codes[:].bitcast(I32), in_=wk_words.rearrange("a p n -> p a n").bitcast(I32))
-        nc.sync.dma_start(out=v_sc1[0:MOVED_ROWS, :].bitcast(I32), in_=v_sc0[P - MOVED_ROWS : P, :].bitcast(I32))
-        for i in (1, 2, 3):
+        moves = [(quad, a) for quad in range(P // QUADRANT) for a in range(PASSES)]
+        for i, run in ((1, moves[:FIRST_MOVES]), (2, moves[FIRST_MOVES:]), (3, [])):
+            for quad, a in run:
+                first = 16 * a + 4 * quad
+                nc.sync.dma_start(
+                    out=v_sc[a][QUADRANT * quad : QUADRANT * quad + 4, :].bitcast(I32),
+                    in_=picked_sc[first : first + 4, :].bitcast(I32),
+                )
             planes[0, i] = load_plane(0, i)
         for i in (0, 1, 2):
             planes[1, i] = load_plane(1, i)
@@ -265,11 +270,15 @@ def tile_list_picked_exp_scores_kernel(
         wq_mx.append(quantize("wq1", dealt[1][:]))
         xg1.append(quantize_pair(1))
         wv_dealt = shared_tile("wv_dealt", WOVEN_AT - 4, [P, PASSES, H * PACK], BF16)
+        nc.scalar.copy(
+            out=wv_dealt[:, 0, :].rearrange("p (t m j) -> p m j t", t=PACK, j=PACK)[:, P // 2 : P],
+            in_=wv0_raw[:].rearrange("p j (m t) -> p m j t", t=PACK)[:, P // 2 : P],
+        )
         deal(wv1_raw[1], wv_dealt[:, 1, :], P // 2)
         for a, raw in enumerate((wv0_raw, wv1_raw[0])):
             src = raw[:].rearrange("p j (m t) -> p m t j", t=PACK)
             dst = wv_dealt[:, a, :].rearrange("p (t m j) -> p m t j", t=PACK, j=PACK)
-            for lo in range(0, src.shape[1], GPSIMD_STEP):
+            for lo in range(0, P // 2, GPSIMD_STEP):
                 rows = slice(lo, lo + GPSIMD_STEP)
                 nc.gpsimd.tensor_scalar(dst[:, rows], src[:, rows], 1.0, 0.0, MULT, ADD)
         wv_mx = []

@@ -39,7 +39,7 @@ WQ0_AT = 72
 STAGE_AT = 80
 PICKED_AT = (96, 112)
 WOVEN_AT = 132
-OUT_GROUPS = ((0, 2, 0), (2, 2, 2), (4, 2, 4), (6, 1, 0), (7, 1, 2))
+OUT_GROUPS = ((0, 1, 0), (1, 2, 2), (3, 2, 0), (5, 1, 2), (6, 1, 4), (7, 1, 0))
 
 
 def tile_list_picked_exp_scores_kernel(
@@ -222,9 +222,7 @@ def tile_list_picked_exp_scores_kernel(
         dealt = [shared_tile("dealt%d" % a, PICKED_AT[0] + 4 * a, [P, H * PACK], BF16) for a in range(PASSES)]
         for n in range(2):
             deal(wq0_raw[n], dealt[0][:], n * P // 2)
-        xg0 = [
-            quantize("xg0_%d" % lo, woven0[:, lo : lo + HALF, :].rearrange("p n i -> p (n i)")) for lo in range(0, S, HALF)
-        ]
+        xg0 = quantize("xg0", woven0[:].rearrange("p n i -> p (n i)"))
         wo_codes = shared_tile("wo_codes", STAGE_AT, [P, N], I32)
         nc.sync.dma_start(out=wo_codes[:], in_=wo_words[0].rearrange("p c i -> p (c i)").bitcast(I32))
         wo_sc = shared_tile("wo_sc", STAGE_AT + 2, [P, 1, N], U8)
@@ -238,17 +236,19 @@ def tile_list_picked_exp_scores_kernel(
         for lo, hi in ((0, PAIR), (PAIR, S)):
             gather(picked[1][:, PACK - 1, :], planes[1, PACK - 1], lo, hi)
 
-        woven1 = [shared_tile("woven1_%d" % g, WOVEN_AT + 2 * g, [P, PAIR, PACK], BF16) for g in range(PAIRS)]
-        interleave(picked[1], woven1[0][:], 0, PAIR)
+        pieces = ((0, PAIR), (PAIR, HALF), (HALF, S))
+        woven1 = [
+            shared_tile("woven1_%d" % n, WOVEN_AT + 2 * n, [P, hi - lo, PACK], BF16) for n, (lo, hi) in enumerate(pieces)
+        ]
+        interleave(picked[1], woven1[0][:], *pieces[0])
         deal(wq1_raw[0], dealt[1][:])
-        for g in range(1, PAIRS):
-            interleave(picked[1], woven1[g][:], g * PAIR, (g + 1) * PAIR)
+        for n in (1, 2):
+            interleave(picked[1], woven1[n][:], *pieces[n])
 
         q_banks = [psum_bank(b, [P, 2, PAIR]) for b in range(CHUNKS)]
         for b in range(CHUNKS):
-            g = b // 2
-            first = (g % 2) * PAIR
-            project(q_banks[b], (2 * (b % 2), 2 * (b % 2) + 1), slice(first, first + PAIR), 0, wq_mx[0], *xg0[g // 2])
+            first = b // 2 * PAIR
+            project(q_banks[b], (2 * (b % 2), 2 * (b % 2) + 1), slice(first, first + PAIR), 0, wq_mx[0], *xg0)
 
         products = [shared_tile("products%d" % n, PLANE_AT[2 + n], [P, 2, PACK, PAIR], F32) for n in range(2)]
         scores = [shared_tile("scores%d" % n, PLANE_AT[1 + 3 * n], [P, 2, PACK, PAIR], F32) for n in range(2)]
@@ -260,7 +260,9 @@ def tile_list_picked_exp_scores_kernel(
         def score(b):
             g = b // 2
             slots = slice(2 * (b % 2), 2 * (b % 2) + 2)
-            project(q_banks[b], (slots.start, slots.start + 1), slice(0, PAIR), 1, wq_mx[1], *xg1[g])
+            n = min(g, 2)
+            within = slice(g * PAIR - pieces[n][0], (g + 1) * PAIR - pieces[n][0])
+            project(q_banks[b], (slots.start, slots.start + 1), within, 1, wq_mx[1], *xg1[n])
             nc.vector.tensor_tensor(
                 products[g // 2][:, g % 2, slots, :], q_banks[b][:], keys[:, slots, g * PAIR : (g + 1) * PAIR], MULT
             )
@@ -283,8 +285,8 @@ def tile_list_picked_exp_scores_kernel(
                 nc.gpsimd.tensor_scalar(dst[:, rows], src[:, rows], 1.0, 0.0, MULT, ADD)
         wv_mx = []
         for b in range(CHUNKS):
-            if b in (2, 4):
-                xg1.append(quantize_pair(b // 2 + 1))
+            if b == 3:
+                xg1.append(quantize_pair(2))
             if b in (5, 7):
                 wv_mx.append(quantize("wv%d" % len(wv_mx), wv_dealt[:, len(wv_mx), :]))
             score(b)
@@ -331,14 +333,16 @@ def tile_list_picked_exp_scores_kernel(
                         start=True,
                         stop=True,
                     )
-                on_vector = count == 1 and half == 1
-                for s in range(2):
-                    u = 2 * half + s
-                    if on_vector:
-                        nc.vector.tensor_scalar_add(results[:, u, entries], bank[:, s, :], bias[:, u : u + 1])
-                    else:
+                tiles = slice(2 * half, 2 * half + 2)
+                if group >= len(OUT_GROUPS) - 2 and half == 1:
+                    spread_bias = bias[:, tiles].unsqueeze(2).to_broadcast([P, 2, width])
+                    nc.vector.tensor_tensor(results[:, tiles, entries], bank[:], spread_bias, ADD)
+                else:
+                    for s in range(2):
+                        u = 2 * half + s
                         nc.scalar.activation(results[:, u, entries], bank[:, s, :], IDENTITY, bias=bias[:, u : u + 1])
-                nc.sync.dma_start(out=out_rows[:, 2 * half : 2 * half + 2, entries], in_=results[:, 2 * half : 2 * half + 2, entries])
+                queue = nc.scalar if group == len(OUT_GROUPS) - 1 and half == 0 else nc.sync
+                queue.dma_start(out=out_rows[:, tiles, entries], in_=results[:, tiles, entries])
 
         for group, (first, count, first_bank) in enumerate(OUT_GROUPS):
             weigh_values(first)

@@ -60,8 +60,8 @@ def tile_list_picked_exp_scores_kernel(
 
         def load_scale_quadrant(tile, rows, quad):
             nc.sync.dma_start(
-                out=tile[QUADRANT * quad : QUADRANT * quad + 4, :, :].bitcast(I32),
-                in_=rows[:, 4 * quad : 4 * quad + 4, :].rearrange("a r n -> r a n").bitcast(I32),
+                out=tile[quad:P:QUADRANT, :, :].bitcast(I32),
+                in_=rows[:, quad:16:4, :].rearrange("a q n -> q a n").bitcast(I32),
             )
 
         def load_plane(a, i):
@@ -126,10 +126,9 @@ def tile_list_picked_exp_scores_kernel(
         moves = [(quad, a) for quad in range(P // QUADRANT) for a in range(PASSES)]
         for i, run in ((1, moves[:FIRST_MOVES]), (2, moves[FIRST_MOVES:]), (3, [])):
             for quad, a in run:
-                first = 16 * a + 4 * quad
                 nc.sync.dma_start(
-                    out=v_sc[a][QUADRANT * quad : QUADRANT * quad + 4, :].bitcast(I32),
-                    in_=picked_sc[first : first + 4, :].bitcast(I32),
+                    out=v_sc[a][quad:P:QUADRANT, :].bitcast(I32),
+                    in_=picked_sc[16 * a + quad : 16 * a + 16 : 4, :].bitcast(I32),
                 )
             planes[0, i] = load_plane(0, i)
         for i in (0, 1, 2):

@@ -31,6 +31,7 @@ CHUNKS = S // CHUNK
 PAIRS = S // PAIR
 GPSIMD_STEP = 32
 EARLY_VAL = 5
+EARLY_Q = 6
 FIRST_MOVES = 5
 KIB = 1024
 PLANE_AT = (0, 8, 16, 24, 32, 40, 48, 64)
@@ -167,7 +168,7 @@ def tile_list_picked_exp_scores_kernel(
         for i in range(PACK):
             gather(picked[0][:, i, :], planes[0, i], 0, S)
         halves = ((0, H // 2), (H // 2, H))
-        wq0_raw = [load_weight(wq, 0, "wq0_raw%d" % n, WQ0_AT + 4 * n, *halves[n]) for n in range(2)]
+        wq0_raw = load_weight(wq, 0, "wq0_raw", WQ0_AT)
         planes[1, 3] = load_plane(1, 3)
         wq1_raw = [load_weight(wq, 1, "wq1_raw%d" % n, TAB_AT[0] + 4 * n, *halves[n]) for n in range(2)]
         wv0_raw = load_weight(wv, 0, "wv0_raw", PLANE_AT[0])
@@ -219,8 +220,7 @@ def tile_list_picked_exp_scores_kernel(
         for i in range(PACK - 1):
             gather(picked[1][:, i, :], planes[1, i], 0, S)
         dealt = [shared_tile("dealt%d" % a, PICKED_AT[0] + 4 * a, [P, H * PACK], BF16) for a in range(PASSES)]
-        for n in range(2):
-            deal(wq0_raw[n], dealt[0][:], n * P // 2)
+        deal(wq0_raw, dealt[0][:])
         xg0 = quantize("xg0", woven0[:].rearrange("p n i -> p (n i)"))
         wo_codes = shared_tile("wo_codes", STAGE_AT, [P, N], I32)
         nc.sync.dma_start(out=wo_codes[:], in_=wo_words[0].rearrange("p c i -> p (c i)").bitcast(I32))
@@ -235,17 +235,17 @@ def tile_list_picked_exp_scores_kernel(
         for lo, hi in ((0, PAIR), (PAIR, S)):
             gather(picked[1][:, PACK - 1, :], planes[1, PACK - 1], lo, hi)
 
-        pieces = ((0, PAIR), (PAIR, HALF), (HALF, S))
+        pieces = [(lo, lo + PAIR) for lo in range(0, S, PAIR)]
         woven1 = [
             shared_tile("woven1_%d" % n, WOVEN_AT + 2 * n, [P, hi - lo, PACK], BF16) for n, (lo, hi) in enumerate(pieces)
         ]
         interleave(picked[1], woven1[0][:], *pieces[0])
         deal(wq1_raw[0], dealt[1][:])
-        for n in (1, 2):
+        for n in range(1, PAIRS):
             interleave(picked[1], woven1[n][:], *pieces[n])
 
         q_banks = [psum_bank(b, [P, 2, PAIR]) for b in range(CHUNKS)]
-        for b in range(CHUNKS):
+        for b in range(EARLY_Q):
             first = b // 2 * PAIR
             project(q_banks[b], (2 * (b % 2), 2 * (b % 2) + 1), slice(first, first + PAIR), 0, wq_mx[0], *xg0)
 
@@ -259,9 +259,12 @@ def tile_list_picked_exp_scores_kernel(
         def score(b):
             g = b // 2
             slots = slice(2 * (b % 2), 2 * (b % 2) + 2)
-            n = min(g, 2)
+            n = g
             within = slice(g * PAIR - pieces[n][0], (g + 1) * PAIR - pieces[n][0])
-            project(q_banks[b], (slots.start, slots.start + 1), within, 1, wq_mx[1], *xg1[n])
+            early = b < EARLY_Q
+            project(q_banks[b], (slots.start, slots.start + 1), within, int(early), wq_mx[1], *xg1[n])
+            if not early:
+                project(q_banks[b], (slots.start, slots.start + 1), slice(g * PAIR, (g + 1) * PAIR), 1, wq_mx[0], *xg0)
             nc.vector.tensor_tensor(
                 products[g // 2][:, g % 2, slots, :], q_banks[b][:], keys[:, slots, g * PAIR : (g + 1) * PAIR], MULT
             )
@@ -284,8 +287,8 @@ def tile_list_picked_exp_scores_kernel(
                 nc.gpsimd.tensor_scalar(dst[:, rows], src[:, rows], 1.0, 0.0, MULT, ADD)
         wv_mx = []
         for b in range(CHUNKS):
-            if b == 3:
-                xg1.append(quantize_pair(2))
+            if b in (2, 4):
+                xg1.append(quantize_pair(len(xg1)))
             if b in (5, 7):
                 wv_mx.append(quantize("wv%d" % len(wv_mx), wv_dealt[:, len(wv_mx), :]))
             score(b)

@@ -30,8 +30,8 @@ HALF = S // 2
 CHUNKS = S // CHUNK
 PAIRS = S // PAIR
 GPSIMD_STEP = 32
-EARLY_VAL = 5
-EARLY_Q = 6
+EARLY_VAL = 6
+EARLY_Q = 8
 FIRST_MOVES = 5
 KIB = 1024
 PLANE_AT = (0, 8, 16, 24, 32, 40, 48, 64)
@@ -168,7 +168,7 @@ def tile_list_picked_exp_scores_kernel(
         for i in range(PACK):
             gather(picked[0][:, i, :], planes[0, i], 0, S)
         halves = ((0, H // 2), (H // 2, H))
-        wq0_raw = load_weight(wq, 0, "wq0_raw", WQ0_AT)
+        wq0_raw = [load_weight(wq, 0, "wq0_raw%d" % n, WQ0_AT + 4 * n, *halves[n]) for n in range(2)]
         planes[1, 3] = load_plane(1, 3)
         wq1_raw = [load_weight(wq, 1, "wq1_raw%d" % n, TAB_AT[0] + 4 * n, *halves[n]) for n in range(2)]
         wv0_raw = load_weight(wv, 0, "wv0_raw", PLANE_AT[0])
@@ -220,7 +220,8 @@ def tile_list_picked_exp_scores_kernel(
         for i in range(PACK - 1):
             gather(picked[1][:, i, :], planes[1, i], 0, S)
         dealt = [shared_tile("dealt%d" % a, PICKED_AT[0] + 4 * a, [P, H * PACK], BF16) for a in range(PASSES)]
-        deal(wq0_raw, dealt[0][:])
+        for n in range(2):
+            deal(wq0_raw[n], dealt[0][:], n * P // 2)
         xg0 = quantize("xg0", woven0[:].rearrange("p n i -> p (n i)"))
         wo_codes = shared_tile("wo_codes", STAGE_AT, [P, N], I32)
         nc.sync.dma_start(out=wo_codes[:], in_=wo_words[0].rearrange("p c i -> p (c i)").bitcast(I32))

@@ -40,7 +40,6 @@ WQ0_AT = 72
 STAGE_AT = 80
 PICKED_AT = (96, 112)
 WOVEN_AT = 132
-OUT_GROUPS = ((0, 1, 0), (1, 2, 2), (3, 2, 0), (5, 1, 2), (6, 1, 4), (7, 1, 0))
 
 
 def tile_list_picked_exp_scores_kernel(
@@ -314,43 +313,45 @@ def tile_list_picked_exp_scores_kernel(
             score_c = scores[c // PACK][:, c // 2 % 2, :, within]
             nc.vector.tensor_tensor(woven, by_two_entries(val_banks[c][:]), by_two_entries(score_c), MULT)
 
-        def finish(group):
-            first, count, first_bank = OUT_GROUPS[group]
-            width = count * CHUNK
-            entries = slice(first * CHUNK, first * CHUNK + width)
-            h_codes = ring.tile([P, width], U32, name="h_codes", align_bytes=64)
-            h_sc = ring.tile([P, width], U8, name="h_sc", align_bytes=64)
+        def finish(c):
+            entries = slice(c * CHUNK, (c + 1) * CHUNK)
+            h_codes = ring.tile([P, CHUNK], U32, name="h_codes", align_bytes=64)
+            h_sc = ring.tile([P, CHUNK], U8, name="h_sc", align_bytes=64)
             nc.vector.quantize_mx(
                 out=h_codes[:].bitcast(FP8X4), scales=h_sc[:], in_=h_all[:, entries, :].rearrange("p n t -> p (n t)")
             )
+            last = c == CHUNKS - 1
+            own = psum_bank(c, [P, PACK, CHUNK])
+            banks = (own, psum_bank(0, [P, PACK, CHUNK]) if last else own)
+            for u in range(PACK):
+                outputs = slice(u * P, (u + 1) * P)
+                nc.tensor.matmul_mx(
+                    out=banks[u // 2][:, u, :],
+                    lhsT=wo_codes[:, outputs].bitcast(FP8X4),
+                    lhsT_scale=wo_sc[:, 0, outputs],
+                    rhs=h_codes[:].bitcast(FP8X4),
+                    rhs_scale=h_sc[:],
+                    start=True,
+                    stop=True,
+                )
             for half in range(2):
-                bank = psum_bank(first_bank + half, [P, 2, width])
-                for s in range(2):
-                    outputs = slice((2 * half + s) * P, (2 * half + s + 1) * P)
-                    nc.tensor.matmul_mx(
-                        out=bank[:, s, :],
-                        lhsT=wo_codes[:, outputs].bitcast(FP8X4),
-                        lhsT_scale=wo_sc[:, 0, outputs],
-                        rhs=h_codes[:].bitcast(FP8X4),
-                        rhs_scale=h_sc[:],
-                        start=True,
-                        stop=True,
-                    )
                 tiles = slice(2 * half, 2 * half + 2)
-                if group >= len(OUT_GROUPS) - 2 and half == 1:
-                    spread_bias = bias[:, tiles].unsqueeze(2).to_broadcast([P, 2, width])
-                    nc.vector.tensor_tensor(results[:, tiles, entries], bank[:], spread_bias, ADD)
+                if last and half == 1:
+                    spread_bias = bias[:, tiles].unsqueeze(2).to_broadcast([P, 2, CHUNK])
+                    nc.vector.tensor_tensor(results[:, tiles, entries], banks[half][:, tiles, :], spread_bias, ADD)
                 else:
-                    for s in range(2):
-                        u = 2 * half + s
-                        nc.scalar.activation(results[:, u, entries], bank[:, s, :], IDENTITY, bias=bias[:, u : u + 1])
-                queue = nc.scalar if group == len(OUT_GROUPS) - 1 and half == 0 else nc.sync
-                queue.dma_start(out=out_rows[:, tiles, entries], in_=results[:, tiles, entries])
+                    for u in range(2 * half, 2 * half + 2):
+                        nc.scalar.activation(
+                            results[:, u, entries], banks[half][:, u, :], IDENTITY, bias=bias[:, u : u + 1]
+                        )
+                if c >= CHUNKS - 2:
+                    queue = nc.scalar if last and half == 0 else nc.sync
+                    queue.dma_start(out=out_rows[:, tiles, entries], in_=results[:, tiles, entries])
+            if c < CHUNKS - 2:
+                nc.sync.dma_start(out=out_rows[:, :, entries], in_=results[:, :, entries])
 
-        for group, (first, count, first_bank) in enumerate(OUT_GROUPS):
-            weigh_values(first)
-            if group > 0:
-                finish(group - 1)
-            for u in range(1, count):
-                weigh_values(first + u)
-        finish(len(OUT_GROUPS) - 1)
+        for c in range(CHUNKS):
+            weigh_values(c)
+            if c > 0:
+                finish(c - 1)
+        finish(CHUNKS - 1)

@@ -167,7 +167,7 @@ def tile_list_picked_exp_scores_kernel(
         for i in range(PACK):
             gather(picked[0][:, i, :], planes[0, i], 0, S)
         halves = ((0, H // 2), (H // 2, H))
-        wq0_raw = [load_weight(wq, 0, "wq0_raw%d" % n, WQ0_AT + 4 * n, *halves[n]) for n in range(2)]
+        wq0_raw = load_weight(wq, 0, "wq0_raw", WQ0_AT)
         planes[1, 3] = load_plane(1, 3)
         wq1_raw = [load_weight(wq, 1, "wq1_raw%d" % n, TAB_AT[0] + 4 * n, *halves[n]) for n in range(2)]
         wv0_raw = load_weight(wv, 0, "wv0_raw", PLANE_AT[0])
@@ -219,8 +219,7 @@ def tile_list_picked_exp_scores_kernel(
         for i in range(PACK - 1):
             gather(picked[1][:, i, :], planes[1, i], 0, S)
         dealt = [shared_tile("dealt%d" % a, PICKED_AT[0] + 4 * a, [P, H * PACK], BF16) for a in range(PASSES)]
-        for n in range(2):
-            deal(wq0_raw[n], dealt[0][:], n * P // 2)
+        deal(wq0_raw, dealt[0][:])
         xg0 = quantize("xg0", woven0[:].rearrange("p n i -> p (n i)"))
         wo_codes = shared_tile("wo_codes", STAGE_AT, [P, N], I32)
         nc.sync.dma_start(out=wo_codes[:], in_=wo_words[0].rearrange("p c i -> p (c i)").bitcast(I32))

from contextlib import ExitStack

import concourse.mybir as mybir
from concourse.masks import make_identity

K, M, T, S, H, N = 1024, 1024, 2048, 1024, 512, 512
FLOPS = 2 * S * (K * H + 2 * M * H + H * N)

F32 = mybir.dt.float32
BF16 = mybir.dt.bfloat16
I32 = mybir.dt.int32
U32 = mybir.dt.uint32
U16 = mybir.dt.uint16
U8 = mybir.dt.uint8
FP8X4 = mybir.dt.float8_e4m3fn_x4
FP4X4 = mybir.dt.float4_e2m1fn_x4
MULT = mybir.AluOpType.mult
ADD = mybir.AluOpType.add
EXP = mybir.ActivationFunctionType.Exp
IDENTITY = mybir.ActivationFunctionType.Identity

P = 128
PACK = 4
PASSES = 2
LIST_ROWS = 16
QUADRANT = 32
CHUNK = 128
PAIR = 2 * CHUNK
HALF = S // 2
CHUNKS = S // CHUNK
PAIRS = S // PAIR
GPSIMD_STEP = 32
EARLY_VAL = 6
EARLY_Q = 8
FIRST_MOVES = 5
KIB = 1024
PLANE_AT = (0, 8, 16, 24, 32, 40, 48, 64)
TAB_AT = (56, 64)
WQ0_AT = 72
STAGE_AT = 80
PICKED_AT = (96, 112)
WOVEN_AT = 132


def tile_list_picked_exp_scores_kernel(
    tc, xT, wgt, offs2, tab_words, tab_scales, offs, wq, wk_words, wk_scales, wv, wo_words, wo_scales, bo, out
):
    nc = tc.nc
    with ExitStack() as ctx:
        keep = ctx.enter_context(tc.tile_pool(name="keep", bufs=1))
        shared = ctx.enter_context(tc.tile_pool(name="shared", bufs=1))
        ring = ctx.enter_context(tc.tile_pool(name="ring", bufs=3))
        psum = ctx.enter_context(tc.psum_pool(name="psum", bufs=1))

        def shared_tile(name, place, shape, dtype):
            return shared.tile(shape, dtype, name=name, offset=place * KIB, align_bytes=64)

        def psum_bank(index, shape):
            return psum.tile(shape, F32, name="bank%d" % index)

        def load_scale_quadrant(tile, rows, quad):
            nc.sync.dma_start(
                out=tile[quad:P:QUADRANT, :, :].bitcast(I32),
                in_=rows[:, quad:16:4, :].rearrange("a q n -> q a n").bitcast(I32),
            )

        def load_plane(a, i):
            plane = shared_tile("plane%d" % (PACK * a + i), PLANE_AT[PACK * a + i], [P, T], F32)
            nc.sync.dma_start(out=plane[:], in_=xT.rearrange("(a p i) t -> a i p t", a=PASSES, i=PACK)[a, i])
            return plane

        def load_weight(w, a, name, place, lo=0, hi=H):
            raw = shared_tile(name, place, [P, PACK, hi - lo], F32)
            nc.sync.dma_start(out=raw[:], in_=w.rearrange("(a p j) r -> a p j r", a=PASSES, j=PACK)[a, :, :, lo:hi])
            return raw

        def project(bank, slots, entries, nth, weight, a_codes, a_scales):
            w_codes, w_scales = weight
            for s, t in enumerate(slots):
                nc.tensor.matmul_mx(
                    out=bank[:, s, :],
                    lhsT=w_codes[:, t * P : (t + 1) * P].bitcast(FP8X4),
                    lhsT_scale=w_scales[:, t * P : (t + 1) * P],
                    rhs=a_codes[:, entries].bitcast(FP8X4),
                    rhs_scale=a_scales[:, entries],
                    start=(nth == 0 and s == 0),
                    stop=(nth == PASSES - 1 and s == len(slots) - 1),
                )

        def by_two_entries(values):
            return values.rearrange("p t (c n) -> p c t n", n=2)

        tab_sc = keep.tile([P, T], U8, name="tab_sc", align_bytes=64)
        wk_sc = keep.tile([P, PASSES, H], U8, name="wk_sc", align_bytes=64)
        v_sc = [keep.tile([P, S], U8, name="v_sc%d" % a, align_bytes=64) for a in range(PASSES)]
        nc.gpsimd.memset(wk_sc[:].bitcast(I32), 0)
        nc.vector.memset(tab_sc[QUADRANT : 2 * QUADRANT, :].bitcast(I32), 0)
        nc.vector.memset(tab_sc[2 * QUADRANT : P, :].bitcast(I32), 0)
        for a in range(PASSES):
            nc.gpsimd.memset(v_sc[a][:].bitcast(I32), 0)
        identity = keep.tile([P, P], F32, name="identity")
        make_identity(nc, identity[:])

        tab_list = keep.tile([P, S // LIST_ROWS], U16, name="tab_list")
        nc.sync.dma_start(tab_list[:], offs)
        nc.sync.dma_start(
            out=tab_sc[0:QUADRANT, :].bitcast(I32), in_=tab_scales.rearrange("a q t -> (a q) t").bitcast(I32)
        )
        tab = [shared_tile("tab%d" % a, TAB_AT[a], [P, T], I32) for a in range(PASSES)]
        nc.sync.dma_start(out=tab[0][:], in_=tab_words[0].rearrange("p t i -> p (t i)").bitcast(I32))
        wgt_parts = keep.tile([P, CHUNK], F32, name="wgt_parts")
        nc.sync.dma_start(
            out=wgt_parts[:],
            in_=wgt.rearrange("(b u) (v x) -> b (u v) x", u=CHUNKS, v=CHUNKS)[:, 0 : CHUNKS * CHUNKS : CHUNKS + 1, :],
        )
        for quad in range(P // QUADRANT):
            load_scale_quadrant(wk_sc, wk_scales, quad)
        nc.sync.dma_start(out=tab[1][:], in_=tab_words[1].rearrange("p t i -> p (t i)").bitcast(I32))
        head_lists = keep.tile([P, S // LIST_ROWS], U16, name="head_lists")
        nc.sync.dma_start(head_lists[:], offs2)
        planes = {(0, 0): load_plane(0, 0)}
        picked_sc = keep.tile([P, S], U8, name="picked_sc", align_bytes=64)
        nc.vector.tensor_copy(picked_sc[:], tab_sc[:].indirect(tab_list[:]))
        wk_codes = keep.tile([P, PASSES, 2 * H], U8, name="wk_codes", align_bytes=64)
        nc.sync.dma_start(out=wk_codes[:].bitcast(I32), in_=wk_words.rearrange("a p n -> p a n").bitcast(I32))
        moves = [(quad, a) for quad in range(P // QUADRANT) for a in range(PASSES)]
        for i, run in ((1, moves[:FIRST_MOVES]), (2, moves[FIRST_MOVES:]), (3, [])):
            for quad, a in run:
                nc.sync.dma_start(
                    out=v_sc[a][quad:P:QUADRANT, :].bitcast(I32),
                    in_=picked_sc[16 * a + quad : 16 * a + 16 : 4, :].bitcast(I32),
                )
            planes[0, i] = load_plane(0, i)
        for i in (0, 1, 2):
            planes[1, i] = load_plane(1, i)

        turned = psum_bank(0, [P, P])
        nc.tensor.transpose(turned[:], wgt_parts[:], identity[:])
        spread = shared_tile("spread", STAGE_AT, [P, CHUNKS, P], F32)
        nc.scalar.copy(
            out=spread[:].rearrange("x u (b c) -> x u b c", c=CHUNKS),
            in_=turned[:].rearrange("x (b u) -> x u b", u=CHUNKS).unsqueeze(3).to_broadcast([P, CHUNKS, 16, CHUNKS]),
        )
        weights = keep.tile([P, S], F32, name="weights")
        for half in range(2):
            back = psum_bank(1 + half, [P, PACK, CHUNK])
            for u in range(PACK):
                nc.tensor.transpose(back[:, u, :], spread[:, PACK * half + u, :], identity[:])
            nc.scalar.copy(out=weights[:, half * HALF : (half + 1) * HALF], in_=back[:].rearrange("p u x -> p (u x)"))

        v_codes = [keep.tile([P, S], U32, name="v_codes%d" % a, align_bytes=64) for a in range(PASSES)]
        for a in range(PASSES):
            nc.vector.tensor_copy(v_codes[a][:], tab[a][:].bitcast(U32).indirect(tab_list[:]))
        wk_dealt = keep.tile([P, PASSES, PACK, 2 * P], U8, name="wk_dealt", align_bytes=64)
        nc.scalar.copy(
            out=wk_dealt[:].bitcast(U16), in_=wk_codes[:].bitcast(U16).rearrange("p a (m t) -> p a t m", t=PACK)
        )
        wk_sc_dealt = keep.tile([P, PASSES, PACK, P], U8, name="wk_sc_dealt", align_bytes=64)
        for a in range(PASSES):
            nc.gpsimd.tensor_copy(wk_sc_dealt[:, a], wk_sc[:, a, :].rearrange("p (m t) -> p t m", t=PACK))

        def gather(dst, plane, lo, hi):
            lists = head_lists[:, lo // LIST_ROWS : hi // LIST_ROWS]
            nc.vector.tensor_tensor(dst[:, lo:hi], plane[:].indirect(lists), weights[:, lo:hi], MULT)

        picked = [shared_tile("picked%d" % a, PICKED_AT[a], [P, PACK, S], F32) for a in range(PASSES)]
        for i in range(PACK):
            gather(picked[0][:, i, :], planes[0, i], 0, S)
        halves = ((0, H // 2), (H // 2, H))
        wq0_raw = load_weight(wq, 0, "wq0_raw", WQ0_AT)
        planes[1, 3] = load_plane(1, 3)
        wq1_raw = [load_weight(wq, 1, "wq1_raw%d" % n, TAB_AT[0] + 4 * n, *halves[n]) for n in range(2)]
        wv0_raw = load_weight(wv, 0, "wv0_raw", PLANE_AT[0])
        wv1_raw = [load_weight(wv, 1, "wv1_raw%d" % n, PLANE_AT[1] + 4 * n, *halves[n]) for n in range(2)]

        def deal(raw, dealt, first=0, engine=nc.scalar):
            src = raw[:].rearrange("p j (m t) -> p m j t", t=PACK)
            dst = dealt.rearrange("p (t m j) -> p m j t", t=PACK, j=PACK)[:, first : first + src.shape[1]]
            if engine is nc.scalar:
                nc.scalar.copy(out=dst, in_=src)
            else:
                nc.vector.tensor_copy(dst, src)

        keys = keep.tile([P, PACK, S], F32, name="keys")
        for b in range(CHUNKS):
            t, entries = b % PACK, slice(b // PACK * HALF, (b // PACK + 1) * HALF)
            bank = psum_bank(b, [P, HALF])
            for nth, a in enumerate((1, 0)):
                nc.tensor.matmul_mx(
                    out=bank[:],
                    lhsT=wk_dealt[:, a, t, :].bitcast(FP4X4),
                    lhsT_scale=wk_sc_dealt[:, a, t, :],
                    rhs=v_codes[a][:, entries].bitcast(FP8X4),
                    rhs_scale=v_sc[a][:, entries],
                    start=(nth == 0),
                    stop=(nth == PASSES - 1),
                )
            nc.scalar.copy(out=keys[:, t, entries], in_=bank[:])

        def interleave(picked_pass, woven, lo, hi):
            nc.scalar.copy(
                out=woven.rearrange("p (c n) i -> p c i n", n=4),
                in_=picked_pass[:, :, lo:hi].rearrange("p i (c n) -> p c i n", n=4),
            )

        def quantize(name, values, place=None):
            width = values.shape[1] // PACK
            if place is None:
                codes = keep.tile([P, width], U32, name=name + "_codes", align_bytes=64)
            else:
                codes = shared_tile(name + "_codes", place, [P, width], U32)
            scales = keep.tile([P, width], U8, name=name + "_sc", align_bytes=64)
            nc.vector.quantize_mx(out=codes[:].bitcast(FP8X4), scales=scales[:], in_=values)
            return codes, scales

        woven0 = shared_tile("woven0", STAGE_AT, [P, S, PACK], BF16)
        for lo in range(0, S, HALF):
            interleave(picked[0], woven0[:, lo : lo + HALF, :], lo, lo + HALF)
        for i in range(PACK - 1):
            gather(picked[1][:, i, :], planes[1, i], 0, S)
        dealt = [shared_tile("dealt%d" % a, PICKED_AT[0] + 4 * a, [P, H * PACK], BF16) for a in range(PASSES)]
        deal(wq0_raw, dealt[0][:])
        xg0 = quantize("xg0", woven0[:].rearrange("p n i -> p (n i)"))
        wo_codes = shared_tile("wo_codes", STAGE_AT, [P, N], I32)
        nc.sync.dma_start(out=wo_codes[:], in_=wo_words[0].rearrange("p c i -> p (c i)").bitcast(I32))
        wo_sc = shared_tile("wo_sc", STAGE_AT + 2, [P, 1, N], U8)
        nc.gpsimd.memset(wo_sc[:].bitcast(I32), 0)
        for quad in range(P // QUADRANT):
            load_scale_quadrant(wo_sc, wo_scales, quad)
        bias = shared_tile("bias", STAGE_AT + 3, [P, N // P], F32)
        with nc.allow_non_contiguous_dma(reason="one bias value a partition and tile of 128 outputs"):
            nc.sync.dma_start(out=bias[:], in_=bo.rearrange("(u p) -> p u", p=P))
        wq_mx = [quantize("wq0", dealt[0][:])]
        for lo, hi in ((0, PAIR), (PAIR, S)):
            gather(picked[1][:, PACK - 1, :], planes[1, PACK - 1], lo, hi)

        pieces = [(lo, lo + PAIR) for lo in range(0, S, PAIR)]
        woven1 = [
            shared_tile("woven1_%d" % n, WOVEN_AT + 2 * n, [P, hi - lo, PACK], BF16) for n, (lo, hi) in enumerate(pieces)
        ]
        interleave(picked[1], woven1[0][:], *pieces[0])
        deal(wq1_raw[0], dealt[1][:])
        for n in range(1, PAIRS):
            interleave(picked[1], woven1[n][:], *pieces[n])

        q_banks = [psum_bank(b, [P, 2, PAIR]) for b in range(CHUNKS)]
        for b in range(EARLY_Q):
            first = b // 2 * PAIR
            project(q_banks[b], (2 * (b % 2), 2 * (b % 2) + 1), slice(first, first + PAIR), 0, wq_mx[0], *xg0)

        products = [shared_tile("products%d" % n, PLANE_AT[2 + n], [P, 2, PACK, PAIR], F32) for n in range(2)]
        scores = [shared_tile("scores%d" % n, PLANE_AT[1 + 3 * n], [P, 2, PACK, PAIR], F32) for n in range(2)]
        val_banks = []

        def quantize_pair(g):
            return quantize("xg1_%d" % g, woven1[g][:].rearrange("p n i -> p (n i)"))

        def score(b):
            g = b // 2
            slots = slice(2 * (b % 2), 2 * (b % 2) + 2)
            n = g
            within = slice(g * PAIR - pieces[n][0], (g + 1) * PAIR - pieces[n][0])
            early = b < EARLY_Q
            project(q_banks[b], (slots.start, slots.start + 1), within, int(early), wq_mx[1], *xg1[n])
            if not early:
                project(q_banks[b], (slots.start, slots.start + 1), slice(g * PAIR, (g + 1) * PAIR), 1, wq_mx[0], *xg0)
            nc.vector.tensor_tensor(
                products[g // 2][:, g % 2, slots, :], q_banks[b][:], keys[:, slots, g * PAIR : (g + 1) * PAIR], MULT
            )

        deal(wq1_raw[1], dealt[1][:], P // 2, nc.vector)
        xg1 = [quantize_pair(0)]
        wq_mx.append(quantize("wq1", dealt[1][:]))
        xg1.append(quantize_pair(1))
        wv_dealt = shared_tile("wv_dealt", WOVEN_AT - 4, [P, PASSES, H * PACK], BF16)
        nc.scalar.copy(
            out=wv_dealt[:, 0, :].rearrange("p (t m j) -> p m j t", t=PACK, j=PACK)[:, P // 2 : P],
            in_=wv0_raw[:].rearrange("p j (m t) -> p m j t", t=PACK)[:, P // 2 : P],
        )
        deal(wv1_raw[1], wv_dealt[:, 1, :], P // 2)
        for a, raw in enumerate((wv0_raw, wv1_raw[0])):
            src = raw[:].rearrange("p j (m t) -> p m t j", t=PACK)
            dst = wv_dealt[:, a, :].rearrange("p (t m j) -> p m t j", t=PACK, j=PACK)
            for lo in range(0, P // 2, GPSIMD_STEP):
                rows = slice(lo, lo + GPSIMD_STEP)
                nc.gpsimd.tensor_scalar(dst[:, rows], src[:, rows], 1.0, 0.0, MULT, ADD)
        wv_mx = []
        for b in range(CHUNKS):
            if b in (2, 4):
                xg1.append(quantize_pair(len(xg1)))
            if b in (5, 7):
                wv_mx.append(quantize("wv%d" % len(wv_mx), wv_dealt[:, len(wv_mx), :]))
            score(b)
        for g in range(PAIRS):
            nc.scalar.activation(scores[g // 2][:, g % 2], products[g // 2][:, g % 2], EXP)
        for c in range(CHUNKS):
            val_banks.append(psum_bank(c, [P, PACK, CHUNK]))
        for c in range(EARLY_VAL):
            project(val_banks[c], range(PACK), slice(c * CHUNK, (c + 1) * CHUNK), 0, wv_mx[0], v_codes[0], v_sc[0])

        h_all = shared_tile("h_all", WQ0_AT, [P, S, PACK], BF16)
        out_rows = out.rearrange("(u p) j -> p u j", p=P)
        results = shared_tile("results", PICKED_AT[0], [P, PACK, S], F32)

        def weigh_values(c):
            entries = slice(c * CHUNK, (c + 1) * CHUNK)
            order = (1,) if c < EARLY_VAL else (1, 0)
            for nth, a in enumerate(order):
                project(val_banks[c], range(PACK), entries, PASSES - len(order) + nth, wv_mx[a], v_codes[a], v_sc[a])
            woven = h_all[:, entries, :].rearrange("p (c n) t -> p c t n", n=2)
            within = slice((c % 2) * CHUNK, (c % 2 + 1) * CHUNK)
            score_c = scores[c // PACK][:, c // 2 % 2, :, within]
            nc.vector.tensor_tensor(woven, by_two_entries(val_banks[c][:]), by_two_entries(score_c), MULT)

        def finish(c):
            entries = slice(c * CHUNK, (c + 1) * CHUNK)
            h_codes = ring.tile([P, CHUNK], U32, name="h_codes", align_bytes=64)
            h_sc = ring.tile([P, CHUNK], U8, name="h_sc", align_bytes=64)
            nc.vector.quantize_mx(
                out=h_codes[:].bitcast(FP8X4), scales=h_sc[:], in_=h_all[:, entries, :].rearrange("p n t -> p (n t)")
            )
            last = c == CHUNKS - 1
            own = psum_bank(c, [P, PACK, CHUNK])
            banks = (own, psum_bank(0, [P, PACK, CHUNK]) if last else own)
            for u in range(PACK):
                outputs = slice(u * P, (u + 1) * P)
                nc.tensor.matmul_mx(
                    out=banks[u // 2][:, u, :],
                    lhsT=wo_codes[:, outputs].bitcast(FP8X4),
                    lhsT_scale=wo_sc[:, 0, outputs],
                    rhs=h_codes[:].bitcast(FP8X4),
                    rhs_scale=h_sc[:],
                    start=True,
                    stop=True,
                )
            for half in range(2):
                tiles = slice(2 * half, 2 * half + 2)
                if last and half == 1:
                    spread_bias = bias[:, tiles].unsqueeze(2).to_broadcast([P, 2, CHUNK])
                    nc.vector.tensor_tensor(results[:, tiles, entries], banks[half][:, tiles, :], spread_bias, ADD)
                else:
                    for u in range(2 * half, 2 * half + 2):
                        nc.scalar.activation(
                            results[:, u, entries], banks[half][:, u, :], IDENTITY, bias=bias[:, u : u + 1]
                        )
                if c >= CHUNKS - 2:
                    queue = nc.scalar if last and half == 0 else nc.sync
                    queue.dma_start(out=out_rows[:, tiles, entries], in_=results[:, tiles, entries])
            if c < CHUNKS - 2:
                nc.sync.dma_start(out=out_rows[:, :, entries], in_=results[:, :, entries])

        for c in range(CHUNKS):
            weigh_values(c)
            if c > 0:
                finish(c - 1)
        finish(CHUNKS - 1)
